import numpy as np, ml_dtypes
CORES = [16,18,20,22]
N = 4
import mx_ref
BF = ml_dtypes.bfloat16
def gentries(a):
    return np.ascontiguousarray(a.reshape(8, 16, -1).transpose(0, 2, 1)).reshape(8, -1)
def gtable(e):
    e = np.asarray(e); return np.ascontiguousarray(e.reshape(8, -1, 16).transpose(0, 2, 1)).reshape(128, -1).astype(np.int32)
def gcols(t, e):
    v = np.concatenate([t.reshape(8, 16, -1, 4), np.zeros((8, 16, 1, 4), BF)], axis=2)
    return np.ascontiguousarray(np.stack([v[g][:, e[g]] for g in range(8)])).reshape(128, -1)
def tile(rs):
    return np.stack(rs, axis=2).reshape(128, -1).astype(BF)
def cut(t, i, w=512):
    return t[:, w * i:w * i + w]
def pick(q, e):
    c = np.concatenate([q[0].reshape(128, -1, 4), np.zeros((128, 1, 4), np.uint8)], axis=1); s = np.concatenate([q[1], np.ones((16, 1), np.uint8)], axis=1)
    return (np.ascontiguousarray(c[:, e].reshape(128, -1)), np.ascontiguousarray(s[:, e]))
def join(*qs):
    return (np.concatenate([q[0] for q in qs], axis=1), np.concatenate([q[1] for q in qs], axis=1))
def put(q, e, v):
    c, s = q[0].reshape(128, -1, 4).copy(), q[1].copy(); c[:, e] = v[0].reshape(128, -1, 4); s[:, e] = v[1]
    return (c.reshape(128, -1), s)
def pk(c, s):
    return (np.ascontiguousarray(c), mx_ref.live(s))
def emit(q):
    return q[0], q[1]
def packed(v, rng):
    q = [mx_ref.quantize(np.ascontiguousarray(v[r])) for r in range(N)]
    return np.stack([a for a, b in q]), np.stack([mx_ref.plane(b, rng) for a, b in q])
def values_of_codes():
    e, c = np.zeros((128, 128, 4), np.float32), np.zeros((128, 2, 4), np.uint8)
    e[np.arange(128), np.arange(128), 0] = 1
    c[:127, :, 0] = np.arange(256).reshape(2, 128).T[:127]
    return mx_ref.matmul(mx_ref.quantize(e.reshape(128, 512).astype(BF)), (c.reshape(128, 8), np.full((16, 2), 127, np.uint8))).T.reshape(-1).astype(np.float64)
CODE_VALUE, SCALE_VALUE = values_of_codes(), 2.0 ** (np.arange(256) - 127.0)
def decode(q):
    return (CODE_VALUE[q[0]].reshape(16, 8, -1, 4) * SCALE_VALUE[q[1]][:, None, :, None] + 0.0).reshape(128, -1).astype(np.float32)
def f(rng, *shape):
    return mx_ref.flush((rng.standard_normal(shape, dtype=np.float32) * np.exp2(rng.integers(-2, 3, shape[:-1] + (1,)))).astype(BF))
def wide(rng, *shape, cols=0):
    v = rng.standard_normal(shape, dtype=np.float32) * np.exp2(rng.integers(-12, 13, shape)).astype(np.float32)
    if cols: v *= np.repeat(np.exp2(rng.integers(-cols, cols + 1, shape[:-2] + (1, shape[-1] // 4))) * (rng.random(shape[:-2] + (1, shape[-1] // 4)) > 0.0625), 4, axis=-1).astype(np.float32)
    return mx_ref.flush(v.astype(BF))
C, A, R, T = 256, 64, 3, 8
STEP = [1, 2, 3]
def turn(p, s):
    at = np.argmax((s + np.float32(0.0)).reshape(8, T, 32), axis=2) + 32 * np.arange(T)
    back, on, new, way = at, np.ones((8, T), bool), p.copy(), np.full((8, T, 32), -1)
    for i in range(32):
        way[:, :, i] = np.where(on, at, -1)
        np.put_along_axis(new, at, back, axis=1)
        up = np.take_along_axis(p, at, axis=1)
        back = np.where(up == at, back, at)
        on = on & (up != at)
        at = up
    slot, home = np.full((8, A), -1), np.full((8, C), -1)
    for g in range(8):
        n = 0
        for k in range(T):
            w = way[g, k][way[g, k] >= 0][:A - n]
            slot[g, n:n + len(w)] = w
            home[g, w] = n + len(w) - 1 - np.arange(len(w))
            n += len(w)
    return new, slot, home
def numbers_of(rng):
    return {"x": np.array(f(rng, N, 128, 4 * C)), "u": np.array(f(rng, N, 128, 512)), "v": np.array(f(rng, N, 128, 512))}
def packing(rng, w):
    c, p = packed(w, rng)
    return {"wc": c, "ws": p}
def weights(rng, off=None, deaf=False):
    w = np.array(f(rng, N, 128, 2048)).reshape(N, 128, 4, 128, 4)
    if off is not None:
        w[:, :, :, off] = 0
        if deaf: w[:, off] = 0
    return packing(rng, w.reshape(N, 128, 2048))
def forest(rng):
    o = np.argsort(rng.random((N, 8, T, 32)), axis=3)
    i = np.arange(32)
    n = rng.choice([1, 2, 3, 32], (N, 8, T, 1))
    b = np.minimum(1 + rng.integers(0, n, o.shape), i)
    p = np.zeros_like(o)
    np.put_along_axis(p, o, np.take_along_axis(o, i - b, axis=3), axis=3)
    return p
def stored(p):
    return np.stack([gtable((p[r] + 32 * np.arange(T)[:, None]).reshape(8, C)) for r in range(N)])
def signs(rng):
    return np.stack([rng.permutation(8) % 2 * 2.0 - 1.0 for r in range(N)])
def setup_inputs(rng):
    return {**numbers_of(rng), "par": stored(forest(rng)), **weights(rng)}
def setup_inputs_ties(rng):
    d = numbers_of(rng)
    e = rng.permutation(N)
    x = d["x"].reshape(N, 8, 16, C, 4)
    for r in range(N):
        k = rng.permutation(C) % 3
        if e[r] == 0: k[:] = 0
        a = x[r][:, :8, :3].copy()
        a[:, :, 2] = 0
        if e[r] == 1: a[:] = 0
        x[r][:, :8] = a[:, :, k]
    u = d["u"].reshape(N, 8, 16, 128, 4)
    for t in range(R): u[:, :, 8:, t::16] = 0
    return {"x": x.reshape(N, 128, 4 * C), "u": u.reshape(N, 128, 512), "v": d["v"], "par": stored(forest(rng)), **weights(rng, np.arange(128) % 16 < 8)}
def setup_inputs_near(rng):
    d = numbers_of(rng)
    x = d["x"].astype(np.float32).reshape(N, 8, 16, C, 4)
    s = np.argsort(rng.random((N, 8, R, T, 32)), axis=4) // 2
    up = (np.arange(N)[:, None, None] + np.arange(8)[:, None] + np.arange(R)) % 2 == int(rng.integers(2))
    s = np.where(up[..., None, None], np.arange(32) // 2, s).reshape(N, 8, R, C)
    x[:, :, 0] = 0
    x[:, :, 0, :, 0] = signs(rng)[:, :, None]
    x[:, :, 8:8 + R] = ((s[..., None] >> np.arange(4)) & 1) * np.exp2(np.arange(4) - 23.0)
    x[:, :, 8 + R:] = rng.integers(4, 8, (N, 8, 8 - R, C, 4)) * rng.choice([-1.0, 1.0], (N, 8, 8 - R, C, 4)) * 2.0 ** -20
    for g in rng.permutation(8)[:4]:
        x[:, int(g), 0, 32 * np.arange(T) + rng.integers(0, 32, T), 0] = -2.0 ** 30
    k = np.where(rng.permutation(N) < N // 2, 2.0 ** -30, 1.0).astype(np.float32).astype(BF)
    u = d["u"].reshape(N, 128, 128, 4)
    for t in range(R):
        u[:, :, t::16] = 0
        for h in range(0, 128, 16):
            u[:, h, h + t, 0] = k
            u[:, h + 8 + t, h + t] = k[:, None]
    i = np.arange(128) % 16
    return {"x": x.reshape(N, 128, 4 * C).astype(BF), "u": u.reshape(N, 128, 512), "v": d["v"], "par": stored(forest(rng)), **weights(rng, (i == 0) | (i >= 8), True)}
def setup_inputs_shapes(rng):
    d, p = numbers_of(rng), forest(rng)
    e, q = rng.permutation(N), int(rng.integers(8))
    x = d["x"].reshape(N, 8, 16, C, 4)
    u = d["u"].reshape(N, 128, 128, 4)
    for t in range(R): u[:, :, t::16] = 0
    for r in range(N):
        kinds = rng.permutation(8)
        if e[r] == 0: kinds[:] = 4
        if e[r] == 1: kinds[:] = 3
        chain = np.argsort(rng.random((8, T, 32)), axis=2)
        for g in range(8):
            h, at = int(kinds[g]), np.zeros(T, int)
            if h < 7: np.put_along_axis(p[r, g], chain[g], chain[g][:, np.maximum(np.arange(32) - 1, 0)], axis=1)
            if h == 7: chain[g, :, 0] = np.argmax(p[r, g] == np.arange(32), axis=1)
            for t in range(R):
                if h < 3:
                    cutoff = rng.permutation(np.repeat(np.arange(T), 16))[:17 * T - (A, A + 1, A - 1)[h]]
                    n = 16 - np.bincount(cutoff, minlength=T)
                    at = np.where((at + n <= 31) & ((at < n) | (rng.random(T) < 0.5)), at + n, at - n)
                elif h in (4, 5):
                    at = 31 - at
                    if h == 5: at[0] = int(rng.integers(32))
                elif h > 5: at = rng.integers(0, 32, T)
                low = int(rng.integers(2))
                mark = -rng.integers(2, 4, C).astype(np.float32) if low else rng.integers(-1, 2, C).astype(np.float32)
                mark[32 * np.arange(T) + chain[g, np.arange(T), at]] = (2.0, -1.0)[low]
                k = R * g + t
                x[r, q, k // 4, :, k % 4] = mark.astype(BF)
                u[r, 16 * q + k // 4, 16 * g + t, k % 4] = 1.0
    return {"x": x.reshape(N, 128, 4 * C), "u": u.reshape(N, 128, 512), "v": d["v"], "par": stored(p), **weights(rng, np.arange(128) // 8 == 2 * q)}
def setup_inputs_huge(rng):
    d = numbers_of(rng)
    x = 2.0 ** 30 * (0.6 + 0.35 * rng.random((N, 128, C, 4)))
    mixed = rng.permutation(N) < N // 2
    side = (np.argsort(rng.random((N, T, 32)), axis=2) % 2).reshape(N, C)
    first = np.arange(128) % 16 < 8
    x *= (~mixed[:, None, None] | (first[None, :, None] == (side[:, None, :] == 1)))[..., None]
    u = d["u"].reshape(N, 128, 128, 4)
    for t in range(R):
        c = signs(rng)[:, None, :] * np.where(mixed[:, None, None] & ~first[None, :, None], -1.0, 1.0)
        u[:, :, t::16] = (2.0 ** 30 * (0.75 + 0.25 * rng.random((N, 128, 8, 4))) * c[..., None]).astype(np.float32).astype(BF)
    w = np.zeros((N, 128, 4, 128, 4), np.float32)
    i = np.arange(128)
    for b in range(4): w[:, i, b, i, b] = 0.125
    return {"x": x.astype(np.float32).reshape(N, 128, 4 * C).astype(BF), "u": u.reshape(N, 128, 512), "v": d["v"], "par": stored(forest(rng)), **packing(rng, w.reshape(N, 128, 2048).astype(BF))}
def setup_inputs_spread(rng):
    d = setup_inputs(rng)
    d["x"] = wide(rng, N, 128, 4 * C, cols=6)
    return d
def check_inputs(d):
    b = []
    for k in ("x", "u", "v"):
        a = np.abs(d[k].astype(np.float32))
        if not (np.isfinite(a).all() and ((a == 0) | (a >= 2.0 ** -30) & (a <= 2.0 ** 30)).all()): b.append("a value of " + k)
    if np.isin(d["wc"], [127, 255]).any(): b.append("wc: a code that is no number")
    for r in range(N):
        a = np.abs(decode(pk(d["wc"][r], d["ws"][r])))
        if not ((a == 0) | (a >= 2.0 ** -30) & (a <= 2.0 ** 30)).all(): b.append("wc and ws: a number out of range")
        p = gentries(d["par"][r]).astype(np.int64)
        if (p // 32 != np.arange(C) // 32).any():
            b.append("par: a parent outside the tree")
            continue
        a = p
        for i in range(5): a = np.take_along_axis(a, a, axis=1)
        z = a.reshape(8, T, 32)
        if (z != z[:, :, :1]).any() or (np.take_along_axis(p, a, axis=1) != a).any(): b.append("par: a tree without one root that all its nodes come to")
    return b
def reference(x, u, v, par, wc, ws):
    qu = [mx_ref.quantize(u[r]) for r in range(N)]
    lay = [pk(wc[r], ws[r]) for r in range(N)]
    now = [x[r] for r in range(N)]
    parent = [gentries(par[r]).astype(np.int64) for r in range(N)]
    for t in range(R):
        sent, homes, made = [], [], []
        for r in range(N):
            q = mx_ref.quantize(now[r])
            parent[r], slot, home = turn(parent[r], mx_ref.matmul(qu[r], q)[t::16])
            homes.append(home)
            sent.append(mx_ref.quantize(gcols(decode(q).astype(BF), slot)))
        for r in range(N):
            p = sent[r ^ STEP[t]]
            h = tile([np.maximum(mx_ref.matmul(pick(lay[r], np.arange(128 * b, 128 * b + 128)), p), np.float32(0.0)) * np.float32(0.03125) for b in range(4)])
            made.append(mx_ref.quantize(h))
        came = decode(join(*made)).astype(BF)
        for r in range(N):
            got = gcols(cut(came, r ^ STEP[t], 4 * A), homes[r])
            now[r] = (now[r].astype(np.float32) + got.astype(np.float32)).astype(BF)
    y, op = np.zeros((N, 128, C), np.float32), np.zeros((N, 8, C), np.float32)
    oc, osc = np.zeros((N, 128, 4 * C), np.uint8), np.zeros((N, 16, C), np.uint8)
    for r in range(N):
        q = mx_ref.quantize(now[r])
        y[r] = mx_ref.matmul(mx_ref.quantize(v[r]), q)
        op[r] = parent[r]
        oc[r], osc[r] = emit(q)
    return {"y": y, "op": op, "oc": oc, "osc": osc}

@@ -1,0 +1,563 @@
+from concourse.bass import DstId, RemoteDMATransfer
+from concourse.mybir import dt, AluOpType, ActivationFunctionType
+
+A = AluOpType
+F = ActivationFunctionType
+R = 3
+STEP = [1, 2, 3]
+BF, F32, I32, U16, U8, X4 = "bfloat16", "float32", "int32", "uint16", "uint8", "float8_e4m3fn_x4"
+SENT = 272
+BIG = 2.0 ** 90
+A0, A1, DP, ZZ, VV = 0, 256, 512, 768, 800
+
+SCRATCH = {}
+
+
+def _sb(name, cols, dtype):
+    SCRATCH[name] = ("sbuf", [128, cols], dtype)
+
+
+for _t in range(R + 1):
+    _sb("xb%d" % _t, 1280, BF)
+    _sb("xq%d" % _t, 256, X4)
+    _sb("xs%d" % _t, 256, U8)
+for _t in range(R):
+    _sb("lq%d" % _t, 320, X4)
+    _sb("ls%d" % _t, 512, U8)
+    _sb("ll%d" % _t, 4, U16)
+    _sb("sl%d" % _t, 16, U16)
+    _sb("hq%d" % _t, 256, X4)
+    _sb("hs%d" % _t, 256, U8)
+for _n, _c, _d in [
+    ("ut", 512, BF), ("vt", 512, BF), ("uq", 128, X4), ("us", 128, U8), ("vq", 128, X4), ("vs", 128, U8),
+    ("up", 384, X4), ("ups", 384, U8), ("wq", 512, X4), ("wss", 512, U8), ("eq", 512, X4), ("es", 512, U8),
+    ("ez", 520, BF), ("pari", 16, I32), ("iota", 288, BF), ("io4", 256, BF), ("ki", 64, I32), ("kf", 64, F32),
+    ("ku", 40, U16), ("jl", 16, F32), ("dmp", 16, F32), ("j4", 64, F32), ("c64", 64, F32), ("base", 8, F32),
+    ("cm", 256, BF), ("cm1", 256, BF), ("dm", 256, BF), ("dm1", 256, BF), ("kc", 64, F32),
+    ("mx", 264, F32), ("em", 256, BF), ("ct", 256, BF),
+    ("ja", 288, BF), ("jb", 288, BF), ("jo", 192, U16), ("tt", 512, BF),
+    ("va", 288, BF), ("vb", 288, BF), ("vc", 272, BF), ("v32", 32, BF), ("wa", 1088, BF), ("un", 512, BF),
+    ("offs", 8, U16), ("gi", 48, I32), ("mi", 48, I32), ("s", 640, F32), ("en", 24, F32), ("so", 16, U16),
+    ("win", 1040, BF), ("wim", 528, BF), ("ts", 128, BF), ("tm", 128, BF), ("mo", 16, U16), ("xo", 16, U16),
+    ("ho", 64, U16), ("po", 16, U16), ("lo", 16, U16), ("cin", 64, F32), ("lt", 128, F32),
+    ("dp", 1088, BF), ("pt", 512, BF), ("ht", 512, BF), ("xg", 256, BF), ("opf", 256, F32), ("yf", 256, F32),
+]:
+    _sb(_n, _c, _d)
+SCRATCH["pa"] = ("psum", [128, 2048], F32)
+SCRATCH["pc"] = ("psum", [128, 2048], F32)
+
+SEMAPHORES = ["sV", "sA", "sP", "sG", "dpar", "dx", "du", "dv", "dw", "dws", "dout", "loc"] + \
+             ["%s%d" % (_k, _t) for _k in ("qx", "li", "hh") for _t in range(R)]
+
+
+def _overlap(a, b):
+    if a[0] != b[0] or a[2] <= b[1] or b[2] <= a[1]:
+        return False
+    if a[3] == b[3] and a[3] > 1:
+        return (a[1] - b[1]) % a[3] == 0
+    return True
+
+
+def rank_program(g, core, T, topo):
+    rank = T.rank_of(core)
+    if rank is None:
+        return
+    eng = {"V": g.vector, "A": g.scalar, "P": g.tensor, "G": g, "S": g.sync}
+    known = {e: {} for e in eng}
+    hist = []
+    total = {}
+
+    def v(name, lo=0, hi=None, step=1):
+        if hi is None:
+            hi = SCRATCH[name][1][1]
+        ap = T[name][:, lo:hi] if step == 1 else T[name][:, lo:hi:step]
+        if SCRATCH[name][0] == "psum":
+            return (ap, [(name, lo // 512 * 512, (hi + 511) // 512 * 512, 1)])
+        return (ap, [(name, lo, hi, step)])
+
+    def col(name, c):
+        return v(name, c, c + 1)
+
+    def ind(w, o):
+        return (w[0].indirect(o[0]), w[1] + o[1])
+
+    def wait(e, tok):
+        sem, val, clock = tok
+        if known[e].get(sem, 0) >= val:
+            return
+        eng[e].wait_ge(T.sem[sem], val)
+        for k, x in list(clock.items()) + [(sem, val)]:
+            if known[e].get(k, 0) < x:
+                known[e][k] = x
+
+    def issue(e, fn, reads, writes, after=(), sem=None, inc=1):
+        rr = [r for x in reads for r in x[1]]
+        ww = [r for x in writes for r in x[1]]
+        need = {}
+        for reg, isw, tok, q in hist:
+            ps = SCRATCH[reg[0]][0] == "psum" and q != e
+            if any(_overlap(reg, r) for r in ww) or ((isw or ps) and any(_overlap(reg, r) for r in rr)):
+                if tok[0] not in need or need[tok[0]][1] < tok[1]:
+                    need[tok[0]] = tok
+        for tok in sorted(list(need.values()) + list(after), key=lambda x: -len(x[2])):
+            wait(e, tok)
+        if sem is None:
+            sem = "s" + e
+        total[sem] = total.get(sem, 0) + inc
+        tok = (sem, total[sem], dict(known[e]))
+        ins = fn()
+        if ins is not None:
+            ins.then_inc(T.sem[sem], inc)
+        keep = [h for h in hist if not any(h[0][0] == w[0] and w[3] == 1 and w[1] <= h[0][1] and h[0][2] <= w[2] for w in ww)]
+        hist[:] = keep + [(r, False, tok, e) for r in rr] + [(r, True, tok, e) for r in ww]
+        return tok
+
+    def arrived(sem, val, *views):
+        tok = (sem, val, {})
+        total[sem] = val
+        for x in views:
+            for r in x[1]:
+                hist.append((r, True, tok, "R"))
+        return tok
+
+    def sc(x):
+        return x[0] if isinstance(x, tuple) else x
+
+    def tup(*xs):
+        return [x for x in xs if isinstance(x, tuple)]
+
+    def ts(out, a, s1, op0, s2=None, op1=None):
+        if op1 is None:
+            return issue("V", lambda: g.vector.tensor_scalar(out[0], a[0], sc(s1), None, op0), tup(a, s1), [out])
+        return issue("V", lambda: g.vector.tensor_scalar(out[0], a[0], sc(s1), sc(s2), op0, op1), tup(a, s1, s2), [out])
+
+    def tt(out, a, b, op):
+        return issue("V", lambda: g.vector.tensor_tensor(out[0], a[0], b[0], op), [a, b], [out])
+
+    def cp(out, a):
+        return issue("V", lambda: g.vector.tensor_copy(out[0], a[0]), [a], [out])
+
+    def scat(w, o, a):
+        return issue("V", lambda: g.vector.tensor_copy(w[0].indirect(o[0]), a[0]), [a, o], [w])
+
+    def ms(out, c):
+        return issue("V", lambda: g.vector.memset(out[0], c), [], [out])
+
+    def scan(out, a, b, init, op0, op1):
+        return issue("V", lambda: g.vector.tensor_tensor_scan(out[0], a[0], b[0], sc(init), op0, op1), tup(a, b, init), [out])
+
+    def tr(out, a):
+        return issue("V", lambda: g.vector.transpose(out[0], a[0]), [a], [out])
+
+    def qz(q, s, a):
+        return issue("V", lambda: g.vector.quantize_mx(q[0], s[0], a[0]), [a], [q, s])
+
+    def act(out, a, f, bias=None, scale=None):
+        kw = {}
+        if bias is not None:
+            kw["bias"] = sc(bias)
+        if scale is not None:
+            kw["scale"] = sc(scale)
+        return issue("A", lambda: g.scalar.activation(out[0], a[0], f, **kw), tup(a, bias, scale), [out])
+
+    def lin(out, a, scale, bias):
+        return act(out, a, F.Identity, bias, scale)
+
+    def fill(out, c):
+        r = out[1][0]
+        return lin(out, v("iota", 0, (r[2] - r[1] + r[3] - 1) // r[3]), 0.0, c)
+
+    def mm(out, lq, ls, rq, rs):
+        return issue("P", lambda: g.tensor.matmul_mx(out[0], lq[0], ls[0], rq[0], rs[0], True, True), [lq, ls, rq, rs], [out])
+
+    def iota(out, pat, base, cm, small=False):
+        if small:
+            return issue("G", lambda: g.iota(out[0], pat, base, cm, allow_small_or_imprecise_dtypes=True), [], [out])
+        return issue("G", lambda: g.iota(out[0], pat, base, cm), [], [out])
+
+    def dma(e, out, in_, sem, reads=(), writes=(), after=()):
+        return issue(e, lambda: eng[e].dma_start(out, in_), list(reads), list(writes), after, sem, 16)
+
+    def u8(x):
+        return x[0].bitcast(dt.uint8)
+
+    def send(to, dst, src, raw, sem):
+        rid, pid = topo.addr(to)[:2]
+        m = topo.mask(core, to)
+
+        def fn():
+            g.remote_dma(u8(dst) if raw else dst[0], u8(src) if raw else src[0], T.sem[sem], T.sem.loc, pid, rid, m)
+        issue("G", fn, [src], [], (), "loc", len(topo.engines(core, to)))
+
+    def send2(to, dq, sq, ds, ss, sem):
+        rid, pid = topo.addr(to)[:2]
+        en = topo.engines(core, to)
+        h = len(en) // 2
+        masks = [sum(1 << e for e in en[:h]), sum(1 << e for e in en[h:])]
+
+        def fn():
+            g.remote_dma_fused([
+                RemoteDMATransfer(dst_ids=[DstId(rid=rid, pnc=pid)], dma_engine_mask=masks[0], remote_sem=T.sem[sem], src=u8(sq), dst=u8(dq)),
+                RemoteDMATransfer(dst_ids=[DstId(rid=rid, pnc=pid)], dma_engine_mask=masks[1], remote_sem=T.sem[sem], src=ss[0], dst=ds[0]),
+            ], local_sem=T.sem.loc)
+        issue("G", fn, [sq, ss], [], (), "loc", len(en))
+
+    partner = [T.cores[rank ^ STEP[t]] for t in range(R)]
+    ne = [len(topo.engines(partner[t], core)) for t in range(R)]
+
+    dma("S", T.pari[:], T.par[:], "dpar", writes=[v("pari")])
+    tx = dma("S", T.xb0[:, 0:1024], T.x[:], "dx", writes=[v("xb0", 0, 1024)])
+    dma("S", T.ut[:], T.u[:], "du", writes=[v("ut")])
+    dma("S", T.wq[:].bitcast(dt.uint8), T.wc[:], "dw", writes=[v("wq")], after=[tx])
+    dma("S", T.wss[:], T.ws[:], "dws", writes=[v("wss")])
+    dma("S", T.vt[:], T.v[:], "dv", writes=[v("vt")])
+
+    P_, I_, E_, H_, K_, B1, Q_, S1, C1 = range(9)
+    iota(col("ki", P_), [[0, 1]], 0, 1)
+    iota(v("iota"), [[1, 288]], 0, 0, True)
+    iota(v("ki", 32, 56), [[1, 3], [16, 8]], 0, 0)
+    iota(v("ki", 56, 58), [[16, 2]], 15, 0)
+    iota(v("c64"), [[64, 4], [0, 16]], 0, 0, True)
+    iota(v("kc", 0, 16), [[1, 4], [0, 4]], 0, 0, True)
+    iota(v("io4"), [[4, 256]], 0, 0, True)
+    ms(v("ez"), 0.0)
+    for c, m in ((I_, 15), (E_, 16), (H_, 1), (K_, 14), (B1, 2)):
+        ts(col("ki", c), col("ki", P_), m, A.bitwise_and)
+    cp(v("kf", 0, 6), v("ki", 0, 6))
+    kf = lambda c: col("kf", c)
+    ts(col("ki", Q_), kf(I_), 16.0, A.mult, kf(E_), A.subtract)
+    ts(col("ku", 1), kf(E_), 31.0, A.mult)
+    ts(col("ki", S1), col("ki", Q_), 16, A.bitwise_and)
+    ts(col("ki", C1), col("ki", Q_), 224, A.bitwise_and)
+    ts(v("ez", 3, 515, 4), v("iota", 0, 128), kf(P_), A.is_equal)
+    ts(v("v32", 0, 16), v("iota", 0, 16), kf(I_), A.is_equal, 64.0, A.mult)
+    ts(v("v32", 16, 32), v("iota", 0, 16), kf(I_), A.is_equal, 128.0, A.mult)
+    cp(v("kf", S1, C1 + 1), v("ki", S1, C1 + 1))
+    lin(v("jl"), v("iota", 0, 256, 16), 1.0, kf(I_))
+    fill(v("win", 272, 288), float(SENT))
+    lin(kf(21), kf(K_), -16.0 / 30.5, 192.0 - 15.5 / 30.5)
+    fill(v("jb", 272, 288), float(SENT))
+    fill(col("mx", 0), 0.0)
+    lin(v("va", 0, 32), v("v32"), 1.0, 1.0)
+    fill(v("va", 272, 288), 0.0)
+    act(v("va", 32, 64), v("va", 0, 32), F.Copy)
+    fill(v("vb", 272, 288), 0.0)
+    act(v("va", 64, 128), v("va", 0, 64), F.Copy)
+    fill(v("ja", 272, 288), float(SENT))
+    act(v("va", 128, 256), v("va", 0, 128), F.Copy)
+    act(v("va", 256, 272), v("va", 0, 16), F.Copy)
+    lin(kf(22), kf(K_), -16.0, -15.5)
+    act(v("vc"), v("va", 0, 272), F.Copy)
+    lin(v("cm1"), v("iota", 0, 256), 1.0 / 30.5, kf(21))
+    ts(kf(12), kf(S1), 16.0, A.mult, kf(C1), A.add)
+    for b in range(4):
+        qz(v("eq", 128 * b, 128 * b + 128), v("es", 128 * b, 128 * b + 128), v("ez", 3 - b, 515 - b))
+    ts(col("ku", 0), kf(12), kf(E_), A.add)
+    cp(v("ku", 8, 34), v("ki", 32, 58))
+    ts(v("ku", 4, 8), v("iota", 0, 4), 0.0, A.mult, kf(I_), A.add)
+
+    def s(k, n=1):
+        return v("s", 16 * k, 16 * (k + n))
+
+    def sh(k, h):
+        return v("s", 16 * k + h, 16 * k + 16, 2)
+    jo = lambda m: v("jo", 32 * m, 32 * m + 17)
+
+    def tolist(src, lo, out):
+        tr(v("tt", 0, 256), v(src, lo, lo + 256))
+        tr(v("tt", 256, 512), v(src, lo + 16, lo + 272))
+        n = out[1][0][2] - out[1][0][1]
+        return cp(out, ind(v("tt"), v("ku", 0, n // 16)))
+
+    def quant_x(t):
+        for h in range(2):
+            qz(v("xq%d" % t, 128 * h, 128 * h + 128), v("xs%d" % t, 128 * h, 128 * h + 128), v("xb%d" % t, 512 * h, 512 * h + 512))
+
+    def send_x(t):
+        send(partner[t], v("ls%d" % t, 0, 256), v("xs%d" % t), False, "qx%d" % t)
+        send(partner[t], v("lq%d" % t, 0, 256), v("xq%d" % t), True, "qx%d" % t)
+
+    def scores(t):
+        for h in range(2):
+            mm(v("pc", 512 * h, 512 * h + 128), v("up", 128 * t, 128 * t + 128), v("ups", 128 * t, 128 * t + 128),
+               v("xq%d" % t, 128 * h, 128 * h + 128), v("xs%d" % t, 128 * h, 128 * h + 128))
+
+    def pick_u(t):
+        o = v("ku", 8 + 8 * t, 16 + 8 * t)
+        out, w = v("up", 128 * t, 128 * t + 128), v("uq")
+        issue("V", lambda: g.vector.tensor_copy(out[0].bitcast(dt.uint32), w[0].bitcast(dt.uint32).indirect(o[0])), [w, o], [out])
+        act(v("ups", 128 * t, 128 * t + 128), ind(v("us"), o), F.Copy)
+
+    def best(stage):
+        for h in range(2):
+            a, b = 128 * h, 128 * h + 128
+            if stage == 0:
+                scan(v("mx", a + 1, b + 1), v("cm", a, b), v("pc", 512 * h, 512 * h + 128), 0.0, A.add, A.max)
+            if stage == 1:
+                tt(v("em", a, b), v("pc", 512 * h, 512 * h + 128), v("mx", a, b), A.is_le)
+            if stage == 2:
+                scan(v("ct", a, b), v("em", a, b), v("dm", a, b), col("ct", 127) if h else 0.0, A.mult, A.add)
+
+    def unpack_x(t):
+        arrived("qx%d" % t, 2 * ne[t], v("lq%d" % t, 0, 256), v("ls%d" % t, 0, 256))
+        for b in range(4):
+            mm(v("pa", 512 * b, 512 * b + 256), v("eq", 128 * b, 128 * b + 128), v("es", 128 * b, 128 * b + 128),
+               v("lq%d" % t, 0, 256), v("ls%d" % t, 0, 256))
+        for b in range(4):
+            act(v("dp", 272 * b, 272 * b + 256), v("pa", 512 * b, 512 * b + 256), F.Copy)
+
+    DJ, OFF, Y, BD, K0, MN, DZ, ZE = 10, 11, 12, 13, 14, 15, 24, 25
+    en_s, en_e = v("en", 0, 16), v("en", 2, 18)
+
+    tt(s(0), v("pari"), v("jl"), A.not_equal)
+    ts(s(1), v("pari"), -1.0, A.mult, float(SENT), A.add)
+    tt(s(2), s(0), s(1), A.mult)
+    ts(v("jo", 0, 16), s(2), -1.0, A.mult, float(SENT), A.add)
+    ts(col("jo", 16), col("s", 32), -1.0, A.mult, float(SENT), A.add)
+    act(v("win", 0, 272), ind(v("iota"), jo(0)), F.Copy)
+    act(v("jb", 0, 272), ind(v("win", 0, 288), jo(0)), F.Copy)
+    tt(v("vb", 0, 272), ind(v("va"), jo(0)), v("vc"), A.add)
+    act(v("vc"), v("vb", 0, 272), F.Copy)
+    lin(v("cm"), v("cm1"), BIG, -192.0 * BIG)
+    quant_x(0)
+    send_x(0)
+    js, vs = ["jb", "ja"], ["va", "vb"]
+    for m in range(1, 5):
+        tolist(js[(m - 1) % 2], 0, v("jo", 32 * m, 32 * m + 32))
+        if m < 4:
+            act(v(js[m % 2], 0, 272), ind(v(js[(m - 1) % 2]), jo(m)), F.Copy)
+            tt(v(vs[(m + 1) % 2], 0, 272), ind(v(vs[m % 2]), jo(m)), v("vc"), A.add)
+            act(v("vc"), v(vs[(m + 1) % 2], 0, 272), F.Copy)
+        else:
+            tt(v("wa", VV, VV + 272), ind(v(vs[m % 2]), jo(m)), v("vc"), A.add)
+        if m == 1:
+            qz(v("uq"), v("us"), v("ut"))
+            pick_u(0)
+            scores(0)
+        if m == 2:
+            act(v("dm1"), v("iota", 0, 256), F.Abs, bias=kf(22))
+            lin(kf(14), kf(K_), 16.0, 32.0)
+            lin(kf(15), kf(H_), -1.0, 1.0)
+            lin(kf(13), kf(B1), 16.0, kf(E_))
+            lin(col("base", 6), kf(14), 1.0, float(VV - ZZ))
+            lin(col("base", 7), kf(14), kf(15), float(VV - ZZ))
+            lin(kf(16), kf(H_), 64.0, kf(13))
+            best(0)
+            best(1)
+        if m == 3:
+            fill(v("wa", ZZ, VV), 0.0)
+            lin(v("dmp"), v("jl"), 1.0, float(SENT))
+            fill(s(ZE), 0.0)
+            fill(v("en", 0, 2), kf(E_))
+            fill(v("win", 256, 352), 256.0)
+            fill(v("win", 352, 568), 0.0)
+            fill(v("win", 568, 784), 0.0)
+            for b in range(4):
+                fill(v("dp", 272 * b + 256, 272 * b + 272), 0.0)
+            ts(v("dm"), v("dm1"), 16.0, A.is_lt)
+            cp(col("ku", 2), kf(16))
+            best(2)
+            ts(v("offs", 6, 8), v("base", 6, 8), col("ct", 255), A.subtract)
+            lin(kf(17), kf(E_), 1.0, 64.0)
+            lin(kf(18), kf(E_), -1.0, 1024.0)
+            fill(v("wim", 0, 96), 0.0)
+            fill(v("pt", 256, 512), 0.0)
+            fill(v("ht", 256, 512), 0.0)
+    unpack_x(0)
+
+    def places(t):
+        if t == 0:
+            cp(v("gi", 0, 32), ind(v("wa", ZZ, VV + 272), v("offs", 6, 8)))
+            tolist("wa", VV, v("gi", 32, 48))
+            ts(v("mi", 0, 16, 2), v("gi", 0, 16, 2), 64, A.bitwise_and)
+            ts(v("mi", 16, 48), v("gi", 16, 48), 63, A.bitwise_and)
+            ts(v("mi", 1, 16, 2), v("gi", 1, 16, 2), 128, A.bitwise_and)
+            cp(s(DJ - 1, 2), v("mi", 16, 48))
+            ts(s(OFF), v("mi", 0, 16), 0.0, A.is_equal)
+            scan(en_e, s(DJ - 1), s(ZE), kf(E_), A.add, A.add)
+            tt(s(1), s(OFF), v("dmp"), A.mult)
+            tt(s(2), en_e, s(DJ), A.subtract)
+        else:
+            ts(v("offs", 0, 6), v("base", 0, 6), col("ct", 255), A.subtract)
+            tt(s(0, 4), ind(v("wa", 0, VV), v("offs", 0, 4)), v("cin"), A.mult)
+            tr(v("lt", 0, 32), s(0, 2))
+            tt(s(4), s(3), s(DZ), A.add)
+            scan(v("lt", 32, 64), v("kc", 16, 48), v("lt", 0, 32), 0.0, A.add, A.min)
+            tt(s(5), s(2), s(BD), A.subtract)
+            cp(v("lt", 64, 96), ind(v("lt", 32, 64), v("ku", 32, 34)))
+            tr(v("lt", 96, 128), v("lt", 64, 96))
+            tt(s(6), v("lt", 96, 112), v("lt", 112, 128), A.min)
+            scan(en_e, s(6), s(4), kf(E_), A.add, A.add)
+            tt(s(7), s(6), s(MN), A.mult)
+            tt(s(OFF), s(5), s(6), A.is_gt)
+            tt(s(8), s(7), s(K0), A.subtract)
+            tt(s(1), s(OFF), v("dmp"), A.mult)
+            tt(s(2), s(8), en_e, A.add)
+        tt(s(Y), s(2), s(1), A.max)
+        cp(v("so"), s(Y))
+        scat(v("win", 256, 784), v("so"), v("iota", 0, 256))
+        tr(v("ts", 0, 64), v("win", 256, 320))
+        tr(v("ts", 64, 128), v("win", 272, 336))
+        cp(v("sl%d" % t), ind(v("ts"), col("ku", 2)))
+        send(partner[t], v("ll%d" % t), v("sl%d" % t, 0, 4), False, "li%d" % t)
+
+    def tables_a():
+        cp(v("lo"), s(DJ))
+        act(v("un", 0, 256), v("wa", VV, VV + 256), F.Abs, bias=-128.5)
+        act(v("wa", A1, A1 + 256), v("wa", VV, VV + 256), F.Sign, bias=-128.5)
+        act(v("un", 256, 512), v("un", 0, 256), F.Abs, bias=-64.0)
+        act(v("wa", DP, DP + 256), ind(v("iota"), v("lo")), F.Copy)
+        act(v("wa", A0, A0 + 256), v("un", 256, 512), F.Sign, bias=32.0, scale=-1.0)
+
+    def tables_b():
+        for b in range(4):
+            lin(v("j4", 16 * b, 16 * b + 16), v("jl"), 4.0, float(b))
+        lin(col("base", 4), kf(H_), 256.0, kf(14))
+        lin(col("base", 5), kf(14), 1.0, float(DP))
+
+    def tables_c():
+        lin(kf(19), kf(14), 1.0, float(DP - VV))
+        lin(col("base", 0), kf(H_), 256.0, kf(14))
+        lin(col("base", 1), kf(15), 256.0, kf(14))
+        lin(col("base", 2), kf(H_), 256.0, kf(14))
+        lin(col("base", 3), kf(19), kf(15), float(VV))
+        fill(v("kc", 16, 48), 0.0)
+        fill(v("cin", 48, 64), 1.0)
+        fill(sh(DZ, 1), 0.0)
+        fill(v("kc", 16, 48, 16), 1024.0)
+
+    def mirror_a(t):
+        if t:
+            cp(v("en", 2, 18, 2), v("en", 3, 18, 2))
+        ts(s(2), s(Y), kf(17), A.is_ge)
+        ts(s(0), en_e, kf(17), A.min, -1.0, A.add)
+        tt(s(1), en_s, s(Y), A.subtract)
+        tt(s(4), s(2), v("dmp"), A.mult)
+        tt(s(3), s(0), s(1), A.add)
+        ts(s(6), s(2), -4096.0, A.mult, kf(18), A.add)
+        tt(s(5), s(3), s(4), A.max)
+        tt(s(26), s(3), s(6), A.add)
+        cp(v("mo"), s(5))
+        scat(v("wim"), v("mo"), v("io4"))
+
+    def mirror_b(t):
+        tr(v("tm", 0, 64), v("wim", 0, 64))
+        tr(v("tm", 64, 128), v("wim", 16, 80))
+        tt(s(16, 4), ind(s(26), v("ku", 4, 8)), v("c64"), A.add)
+        tt(s(0), ind(v("tm"), col("ku", 2)), v("kc", 0, 16), A.add)
+        tt(s(20, 4), s(16, 4), v("j4"), A.max)
+        cp(v("xo"), s(0))
+        for b in range(4):
+            act(v("xg", 64 * b, 64 * b + 64), ind(v("xb%d" % t, 0, 1024), v("xo", 4 * b, 4 * b + 4)), F.Copy)
+        cp(v("ho"), s(20, 4))
+
+    def parents_a(t):
+        ts(s(0), s(Y), -1.0, A.add)
+        ts(s(1), s(OFF), (-527.0, 257.0)[t % 2], A.mult, (256.0, 0.0)[t % 2], A.add)
+        tt(s(2), s(0), en_s, A.max)
+        tt(s(3), s(2), s(1), A.add)
+        cp(v("po"), s(3))
+
+    def parents_b(t):
+        if t % 2 == 0:
+            act(v("win", 784, 1040) if t == 0 else v("opf"), ind(v("win", 0, 784), v("po")), F.Copy)
+        else:
+            act(v("win", 0, 256), ind(v("win", 256, 1040), v("po")), F.Copy)
+
+    def prep_a(t):
+        if t == 0:
+            ts(v("offs", 4, 6), v("base", 4, 6), col("ct", 255), A.subtract)
+        cp(s(28, 2), ind(v("wa", 0, VV), v("offs", 4, 6)))
+        ts(s(30), s(28), 0.0, A.is_gt)
+        tt(s(31), s(29), s(DJ), A.add)
+        tt(s(BD), s(30), s(DJ), A.mult)
+        ts(s(32), s(BD), -2.0, A.mult, 1.0, A.add)
+        tt(s(K0), s(31), s(32), A.add)
+
+    def prep_b():
+        lin(v("cin", 32, 48), s(30), 64.0, -64.0)
+        lin(v("cin", 0, 16), s(BD), -1.0, 0.0)
+        lin(v("cin", 16, 32, 2), sh(BD, 1), -1.0, 0.0)
+        lin(v("cin", 17, 32, 2), sh(BD, 0), -1.0, 0.0)
+        lin(sh(DZ, 0), sh(29, 0), 1.0, 1.0)
+        lin(sh(MN, 0), sh(30, 0), 2.0, -1.0)
+        lin(sh(MN, 1), sh(30, 1), 2.0, -2.0)
+
+    def layer(t):
+        arrived("li%d" % t, ne[t], v("ll%d" % t))
+        o = v("ll%d" % t)
+        for b in range(4):
+            w = ind(v("dp", 272 * b, 272 * b + 272), o)
+            if b % 2:
+                act(v("pt", b, 256, 4), w, F.Copy)
+            else:
+                cp(v("pt", b, 256, 4), w)
+        pq, ps = v("hq%d" % t, 128, 256), v("hs%d" % t, 128, 256)
+        qz(pq, ps, v("pt"))
+        for b in range(4):
+            mm(v("pc", 512 * b, 512 * b + 128), v("wq", 128 * b, 128 * b + 128), v("wss", 128 * b, 128 * b + 128), pq, ps)
+        for b in range(4):
+            if b % 2:
+                ts(v("ht", b, 256, 4), v("pc", 512 * b, 512 * b + 64), 0.0, A.max, 0.03125, A.mult)
+            else:
+                act(v("ht", b, 256, 4), v("pc", 512 * b, 512 * b + 64), F.Relu, scale=0.03125)
+        qz(v("hq%d" % t, 0, 128), v("hs%d" % t, 0, 128), v("ht"))
+        send2(partner[t], v("lq%d" % t, 256, 320), v("hq%d" % t, 0, 64), v("ls%d" % t, 256, 512), v("hs%d" % t), "hh%d" % t)
+
+    def update(t):
+        arrived("hh%d" % t, ne[t], v("lq%d" % t, 256, 320), v("ls%d" % t, 256, 512))
+        xb, xn = "xb%d" % t, "xb%d" % (t + 1)
+        for b in range(4):
+            mm(v("pa", 512 * b, 512 * b + 128), v("eq", 128 * b, 128 * b + 128), v("es", 128 * b, 128 * b + 128),
+               v("lq%d" % t, 192, 320), v("ls%d" % t, 192, 320))
+        for b in range(4):
+            tt(v(xb, 1024 + 64 * b, 1088 + 64 * b), v("pa", 512 * b + 64, 512 * b + 128), v("xg", 64 * b, 64 * b + 64), A.add)
+        for b in range(4):
+            w = ind(v(xb, 0, 1088 + 64 * b), v("ho", 16 * b, 16 * b + 16))
+            if b < 2:
+                act(v(xn, b, 1024, 4), w, F.Copy)
+            else:
+                cp(v(xn, b, 1024, 4), w)
+        quant_x(t + 1)
+
+    for t in range(R):
+        if t:
+            send_x(t)
+            scores(t)
+            unpack_x(t)
+            for st in range(3):
+                best(st)
+        places(t)
+        if t == 0:
+            tables_a()
+        mirror_a(t)
+        layer(t)
+        if t == 0:
+            tables_b()
+        mirror_b(t)
+        if t < R - 1:
+            pick_u(t + 1)
+            prep_a(t)
+        parents_a(t)
+        if t == R - 1:
+            parents_b(t)
+            qz(v("vq"), v("vs"), v("vt"))
+            dma("S", T.op[:], T.opf[0:128:16, :], "dout", reads=[v("opf")])
+        update(t)
+        if t == 0:
+            tables_c()
+        if t < R - 1:
+            prep_b()
+            parents_b(t)
+            fill(v("win", 256, 352), 256.0)
+
+    for h in range(2):
+        mm(v("pc", 512 * h, 512 * h + 128), v("vq"), v("vs"), v("xq3", 128 * h, 128 * h + 128), v("xs3", 128 * h, 128 * h + 128))
+    dma("S", T.oc[:], T.xq3[:].bitcast(dt.uint8), "dout", reads=[v("xq3")])
+    for k in range(4):
+        dma("A", T.osc[4 * k:4 * k + 4, :], T.xs3[32 * k:32 * k + 4, :], "dout", reads=[v("xs3")])
+    for h in range(2):
+        cp(v("yf", 128 * h, 128 * h + 128), v("pc", 512 * h, 512 * h + 128))
+    dma("S", T.y[:], T.yf[:], "dout", reads=[v("yf")])
+    for sem in sorted(total):
+        wait("S", (sem, total[sem], {}))

@@ -8,7 +8,7 @@ STEP = [1, 2, 3]
 BF, F32, I32, U16, U8, X4 = "bfloat16", "float32", "int32", "uint16", "uint8", "float8_e4m3fn_x4"
 SENT = 272
 BIG = 2.0 ** 90
-A0, A1, DP, ZZ, VV = 0, 256, 512, 768, 800
+A0, A1, DP, NL, ZZ, VV = 0, 256, 512, 768, 1024, 1056
 
 SCRATCH = {}
 
@@ -33,13 +33,14 @@ for _n, _c, _d in [
     ("up", 384, X4), ("ups", 384, U8), ("wq", 512, X4), ("wss", 512, U8), ("eq", 512, X4), ("es", 512, U8),
     ("ez", 520, BF), ("pari", 16, I32), ("iota", 288, BF), ("io4", 256, BF), ("ki", 64, I32), ("kf", 64, F32),
     ("ku", 40, U16), ("jl", 16, F32), ("dmp", 16, F32), ("j4", 64, F32), ("c64", 64, F32), ("base", 8, F32),
-    ("cm", 256, BF), ("cm1", 256, BF), ("dm", 256, BF), ("dm1", 256, BF), ("kc", 64, F32),
+    ("cm", 256, BF), ("cm1", 256, BF), ("dm", 256, BF), ("dm1", 256, BF), ("kc", 16, F32),
     ("mx", 264, F32), ("em", 256, BF), ("ct", 256, BF),
     ("ja", 288, BF), ("jb", 288, BF), ("jo", 192, U16), ("tt", 512, BF),
-    ("va", 288, BF), ("vb", 288, BF), ("vc", 272, BF), ("v32", 32, BF), ("wa", 1088, BF), ("un", 512, BF),
+    ("va", 288, BF), ("vb", 288, BF), ("vc", 272, BF), ("v32", 32, BF), ("wa", 1344, BF), ("un", 512, BF),
+    ("rs", 512, BF), ("kb", 48, U16), ("kbi", 48, I32), ("k0", 24, F32),
     ("offs", 8, U16), ("gi", 48, I32), ("mi", 48, I32), ("s", 640, F32), ("en", 24, F32), ("so", 16, U16),
     ("win", 1040, BF), ("wim", 528, BF), ("ts", 128, BF), ("tm", 128, BF), ("mo", 16, U16), ("xo", 16, U16),
-    ("ho", 64, U16), ("po", 16, U16), ("lo", 16, U16), ("cin", 64, F32), ("lt", 128, F32),
+    ("ho", 64, U16), ("po", 16, U16), ("lo", 16, U16), ("cin", 64, F32),
     ("dp", 1088, BF), ("pt", 512, BF), ("ht", 512, BF), ("xg", 256, BF), ("opf", 256, F32), ("yf", 256, F32),
 ]:
     _sb(_n, _c, _d)
@@ -216,9 +217,10 @@ def rank_program(g, core, T, topo):
     iota(col("ki", P_), [[0, 1]], 0, 1)
     iota(v("iota"), [[1, 288]], 0, 0, True)
     iota(v("ki", 32, 56), [[1, 3], [16, 8]], 0, 0)
-    iota(v("ki", 56, 58), [[16, 2]], 15, 0)
     iota(v("c64"), [[64, 4], [0, 16]], 0, 0, True)
-    iota(v("kc", 0, 16), [[1, 4], [0, 4]], 0, 0, True)
+    iota(v("kc"), [[1, 4], [0, 4]], 0, 0, True)
+    iota(v("kbi", 0, 32), [[1, 2], [2, 8], [0, 2]], 0, 0)
+    iota(v("kbi", 32, 48), [[1, 16]], 0, 0)
     iota(v("io4"), [[4, 256]], 0, 0, True)
     ms(v("ez"), 0.0)
     for c, m in ((I_, 15), (E_, 16), (H_, 1), (K_, 14), (B1, 2)):
@@ -253,7 +255,7 @@ def rank_program(g, core, T, topo):
     for b in range(4):
         qz(v("eq", 128 * b, 128 * b + 128), v("es", 128 * b, 128 * b + 128), v("ez", 3 - b, 515 - b))
     ts(col("ku", 0), kf(12), kf(E_), A.add)
-    cp(v("ku", 8, 34), v("ki", 32, 58))
+    cp(v("ku", 8, 32), v("ki", 32, 56))
     ts(v("ku", 4, 8), v("iota", 0, 4), 0.0, A.mult, kf(I_), A.add)
 
     def s(k, n=1):
@@ -262,12 +264,6 @@ def rank_program(g, core, T, topo):
     def sh(k, h):
         return v("s", 16 * k + h, 16 * k + 16, 2)
     jo = lambda m: v("jo", 32 * m, 32 * m + 17)
-
-    def tolist(src, lo, out):
-        tr(v("tt", 0, 256), v(src, lo, lo + 256))
-        tr(v("tt", 256, 512), v(src, lo + 16, lo + 272))
-        n = out[1][0][2] - out[1][0][1]
-        return cp(out, ind(v("tt"), v("ku", 0, n // 16)))
 
     def quant_x(t):
         for h in range(2):
@@ -282,21 +278,24 @@ def rank_program(g, core, T, topo):
             mm(v("pc", 512 * h, 512 * h + 128), v("up", 128 * t, 128 * t + 128), v("ups", 128 * t, 128 * t + 128),
                v("xq%d" % t, 128 * h, 128 * h + 128), v("xs%d" % t, 128 * h, 128 * h + 128))
 
-    def pick_u(t):
+    def pick_q(t):
         o = v("ku", 8 + 8 * t, 16 + 8 * t)
         out, w = v("up", 128 * t, 128 * t + 128), v("uq")
         issue("V", lambda: g.vector.tensor_copy(out[0].bitcast(dt.uint32), w[0].bitcast(dt.uint32).indirect(o[0])), [w, o], [out])
-        act(v("ups", 128 * t, 128 * t + 128), ind(v("us"), o), F.Copy)
 
-    def best(stage):
-        for h in range(2):
+    def pick_s(t):
+        act(v("ups", 128 * t, 128 * t + 128), ind(v("us"), v("ku", 8 + 8 * t, 16 + 8 * t)), F.Copy)
+
+    def best(stage, hs=(0, 1)):
+        if stage == 2:
+            scan(v("ct"), v("em"), v("dm"), 0.0, A.mult, A.add)
+            return
+        for h in hs:
             a, b = 128 * h, 128 * h + 128
             if stage == 0:
                 scan(v("mx", a + 1, b + 1), v("cm", a, b), v("pc", 512 * h, 512 * h + 128), 0.0, A.add, A.max)
             if stage == 1:
                 tt(v("em", a, b), v("pc", 512 * h, 512 * h + 128), v("mx", a, b), A.is_le)
-            if stage == 2:
-                scan(v("ct", a, b), v("em", a, b), v("dm", a, b), col("ct", 127) if h else 0.0, A.mult, A.add)
 
     def unpack_x(t):
         arrived("qx%d" % t, 2 * ne[t], v("lq%d" % t, 0, 256), v("ls%d" % t, 0, 256))
@@ -306,7 +305,7 @@ def rank_program(g, core, T, topo):
         for b in range(4):
             act(v("dp", 272 * b, 272 * b + 256), v("pa", 512 * b, 512 * b + 256), F.Copy)
 
-    DJ, OFF, Y, BD, K0, MN, DZ, ZE = 10, 11, 12, 13, 14, 15, 24, 25
+    DJ, OFF, Y, BD, ZE = 10, 11, 12, 13, 25
     en_s, en_e = v("en", 0, 16), v("en", 2, 18)
 
     tt(s(0), v("pari"), v("jl"), A.not_equal)
@@ -319,32 +318,51 @@ def rank_program(g, core, T, topo):
     tt(v("vb", 0, 272), ind(v("va"), jo(0)), v("vc"), A.add)
     act(v("vc"), v("vb", 0, 272), F.Copy)
     lin(v("cm"), v("cm1"), BIG, -192.0 * BIG)
+    act(v("dm1"), v("iota", 0, 256), F.Abs, bias=kf(22))
     quant_x(0)
     send_x(0)
     js, vs = ["jb", "ja"], ["va", "vb"]
     for m in range(1, 5):
-        tolist(js[(m - 1) % 2], 0, v("jo", 32 * m, 32 * m + 32))
+        tr(v("tt", 0, 256), v(js[(m - 1) % 2], 0, 256))
+        tr(v("tt", 256, 512), v(js[(m - 1) % 2], 16, 272))
+        if m == 1:
+            qz(v("uq"), v("us"), v("ut"))
+        if m == 2:
+            pick_q(1)
+        if m == 3:
+            best(1, (0,))
+        if m == 4:
+            best(2)
+            cp(v("kb"), v("kbi"))
+        cp(v("jo", 32 * m, 32 * m + 32), ind(v("tt"), v("ku", 0, 2)))
+        if m == 1:
+            pick_q(0)
+        if m == 2:
+            best(0, (0,))
+        if m == 3:
+            best(1, (1,))
+        if m == 4:
+            ts(v("offs", 6, 8), v("base", 6, 8), col("ct", 255), A.subtract)
+            cp(col("ku", 2), kf(16))
         if m < 4:
             act(v(js[m % 2], 0, 272), ind(v(js[(m - 1) % 2]), jo(m)), F.Copy)
             tt(v(vs[(m + 1) % 2], 0, 272), ind(v(vs[m % 2]), jo(m)), v("vc"), A.add)
+            if m == 1:
+                pick_s(0)
             act(v("vc"), v(vs[(m + 1) % 2], 0, 272), F.Copy)
         else:
             tt(v("wa", VV, VV + 272), ind(v(vs[m % 2]), jo(m)), v("vc"), A.add)
         if m == 1:
-            qz(v("uq"), v("us"), v("ut"))
-            pick_u(0)
             scores(0)
         if m == 2:
-            act(v("dm1"), v("iota", 0, 256), F.Abs, bias=kf(22))
             lin(kf(14), kf(K_), 16.0, 32.0)
             lin(kf(15), kf(H_), -1.0, 1.0)
             lin(kf(13), kf(B1), 16.0, kf(E_))
+            best(0, (1,))
+        if m == 3:
             lin(col("base", 6), kf(14), 1.0, float(VV - ZZ))
             lin(col("base", 7), kf(14), kf(15), float(VV - ZZ))
             lin(kf(16), kf(H_), 64.0, kf(13))
-            best(0)
-            best(1)
-        if m == 3:
             fill(v("wa", ZZ, VV), 0.0)
             lin(v("dmp"), v("jl"), 1.0, float(SENT))
             fill(s(ZE), 0.0)
@@ -355,9 +373,6 @@ def rank_program(g, core, T, topo):
             for b in range(4):
                 fill(v("dp", 272 * b + 256, 272 * b + 272), 0.0)
             ts(v("dm"), v("dm1"), 16.0, A.is_lt)
-            cp(col("ku", 2), kf(16))
-            best(2)
-            ts(v("offs", 6, 8), v("base", 6, 8), col("ct", 255), A.subtract)
             lin(kf(17), kf(E_), 1.0, 64.0)
             lin(kf(18), kf(E_), -1.0, 1024.0)
             fill(v("wim", 0, 96), 0.0)
@@ -368,95 +383,93 @@ def rank_program(g, core, T, topo):
     def places(t):
         if t == 0:
             cp(v("gi", 0, 32), ind(v("wa", ZZ, VV + 272), v("offs", 6, 8)))
-            tolist("wa", VV, v("gi", 32, 48))
+            tr(v("tt", 0, 256), v("wa", VV, VV + 256))
+            tr(v("tt", 256, 512), v("wa", VV + 16, VV + 272))
+            ts(v("mi", 16, 32), v("gi", 16, 32), 63, A.bitwise_and)
             ts(v("mi", 0, 16, 2), v("gi", 0, 16, 2), 64, A.bitwise_and)
-            ts(v("mi", 16, 48), v("gi", 16, 48), 63, A.bitwise_and)
             ts(v("mi", 1, 16, 2), v("gi", 1, 16, 2), 128, A.bitwise_and)
-            cp(s(DJ - 1, 2), v("mi", 16, 48))
+            cp(v("gi", 32, 48), ind(v("tt"), col("ku", 0)))
+            cp(s(9), v("mi", 16, 32))
             ts(s(OFF), v("mi", 0, 16), 0.0, A.is_equal)
-            scan(en_e, s(DJ - 1), s(ZE), kf(E_), A.add, A.add)
+            ts(v("mi", 32, 48), v("gi", 32, 48), 63, A.bitwise_and)
+            scan(en_e, s(9), s(ZE), kf(E_), A.add, A.add)
             tt(s(1), s(OFF), v("dmp"), A.mult)
-            tt(s(2), en_e, s(DJ), A.subtract)
+            tt(s(2), en_e, v("mi", 32, 48), A.subtract)
         else:
             ts(v("offs", 0, 6), v("base", 0, 6), col("ct", 255), A.subtract)
-            tt(s(0, 4), ind(v("wa", 0, VV), v("offs", 0, 4)), v("cin"), A.mult)
-            tr(v("lt", 0, 32), s(0, 2))
-            tt(s(4), s(3), s(DZ), A.add)
-            scan(v("lt", 32, 64), v("kc", 16, 48), v("lt", 0, 32), 0.0, A.add, A.min)
-            tt(s(5), s(2), s(BD), A.subtract)
-            cp(v("lt", 64, 96), ind(v("lt", 32, 64), v("ku", 32, 34)))
-            tr(v("lt", 96, 128), v("lt", 64, 96))
-            tt(s(6), v("lt", 96, 112), v("lt", 112, 128), A.min)
-            scan(en_e, s(6), s(4), kf(E_), A.add, A.add)
-            tt(s(7), s(6), s(MN), A.mult)
-            tt(s(OFF), s(5), s(6), A.is_gt)
-            tt(s(8), s(7), s(K0), A.subtract)
+            tt(s(6, 2), ind(v("wa", 0, VV), v("offs", 2, 4)), v("cin", 32, 64), A.add)
+            tt(s(4, 2), ind(v("wa", 0, VV), v("offs", 0, 2)), v("cin", 0, 32), A.mult)
+            scan(s(8), s(6), s(7), kf(E_), A.add, A.add)
+            tt(s(OFF), s(6), s(4), A.is_lt)
+            tt(s(2), s(8), s(5), A.add)
             tt(s(1), s(OFF), v("dmp"), A.mult)
-            tt(s(2), s(8), en_e, A.add)
         tt(s(Y), s(2), s(1), A.max)
         cp(v("so"), s(Y))
         scat(v("win", 256, 784), v("so"), v("iota", 0, 256))
+        if t:
+            for h in range(2):
+                tt(v("en", 2 + h, 18, 2), sh(8, 1), v("k0", 9, 24, 2), A.add)
+        else:
+            cp(s(DJ), v("mi", 32, 48))
+            cp(v("lo"), v("mi", 32, 48))
         tr(v("ts", 0, 64), v("win", 256, 320))
         tr(v("ts", 64, 128), v("win", 272, 336))
+        ts(s(2), s(Y), kf(17), A.is_ge)
+        ts(s(0), en_e, kf(17), A.min, -1.0, A.add)
         cp(v("sl%d" % t), ind(v("ts"), col("ku", 2)))
         send(partner[t], v("ll%d" % t), v("sl%d" % t, 0, 4), False, "li%d" % t)
 
     def tables_a():
-        cp(v("lo"), s(DJ))
         act(v("un", 0, 256), v("wa", VV, VV + 256), F.Abs, bias=-128.5)
         act(v("wa", A1, A1 + 256), v("wa", VV, VV + 256), F.Sign, bias=-128.5)
         act(v("un", 256, 512), v("un", 0, 256), F.Abs, bias=-64.0)
-        act(v("wa", DP, DP + 256), ind(v("iota"), v("lo")), F.Copy)
         act(v("wa", A0, A0 + 256), v("un", 256, 512), F.Sign, bias=32.0, scale=-1.0)
+        fill(v("rs", 0, 256), 1.0)
+        fill(v("rs", 256, 512), 1.0)
+        act(v("wa", DP, DP + 256), ind(v("iota"), v("lo")), F.Copy)
+        fill(v("rs", 0, 512, 16), 0.0)
 
     def tables_b():
         for b in range(4):
             lin(v("j4", 16 * b, 16 * b + 16), v("jl"), 4.0, float(b))
         lin(col("base", 4), kf(H_), 256.0, kf(14))
         lin(col("base", 5), kf(14), 1.0, float(DP))
+        fill(sh(37, 1), 0.0)
+        fill(col("k0", 7), 0.0)
 
     def tables_c():
         lin(kf(19), kf(14), 1.0, float(DP - VV))
         lin(col("base", 0), kf(H_), 256.0, kf(14))
-        lin(col("base", 1), kf(15), 256.0, kf(14))
-        lin(col("base", 2), kf(H_), 256.0, kf(14))
+        lin(col("base", 1), kf(14), 1.0, float(NL))
+        lin(col("base", 2), kf(14), 1.0, float(NL))
         lin(col("base", 3), kf(19), kf(15), float(VV))
-        fill(v("kc", 16, 48), 0.0)
-        fill(v("cin", 48, 64), 1.0)
-        fill(sh(DZ, 1), 0.0)
-        fill(v("kc", 16, 48, 16), 1024.0)
 
     def mirror_a(t):
-        if t:
-            cp(v("en", 2, 18, 2), v("en", 3, 18, 2))
-        ts(s(2), s(Y), kf(17), A.is_ge)
-        ts(s(0), en_e, kf(17), A.min, -1.0, A.add)
         tt(s(1), en_s, s(Y), A.subtract)
         tt(s(4), s(2), v("dmp"), A.mult)
-        tt(s(3), s(0), s(1), A.add)
         ts(s(6), s(2), -4096.0, A.mult, kf(18), A.add)
+        ts(s(33), s(Y), -1.0, A.add)
+        tt(s(3), s(0), s(1), A.add)
+        ts(s(34), s(OFF), (-527.0, 257.0)[t % 2], A.mult, (256.0, 0.0)[t % 2], A.add)
+        tt(s(35), s(33), en_s, A.max)
         tt(s(5), s(3), s(4), A.max)
         tt(s(26), s(3), s(6), A.add)
+        tt(s(36), s(35), s(34), A.add)
         cp(v("mo"), s(5))
+        cp(v("po"), s(36))
         scat(v("wim"), v("mo"), v("io4"))
 
     def mirror_b(t):
         tr(v("tm", 0, 64), v("wim", 0, 64))
         tr(v("tm", 64, 128), v("wim", 16, 80))
         tt(s(16, 4), ind(s(26), v("ku", 4, 8)), v("c64"), A.add)
-        tt(s(0), ind(v("tm"), col("ku", 2)), v("kc", 0, 16), A.add)
-        tt(s(20, 4), s(16, 4), v("j4"), A.max)
+        tt(s(0), ind(v("tm"), col("ku", 2)), v("kc"), A.add)
+
+    def mirror_c(t):
         cp(v("xo"), s(0))
+        tt(s(20, 4), s(16, 4), v("j4"), A.max)
         for b in range(4):
             act(v("xg", 64 * b, 64 * b + 64), ind(v("xb%d" % t, 0, 1024), v("xo", 4 * b, 4 * b + 4)), F.Copy)
-        cp(v("ho"), s(20, 4))
-
-    def parents_a(t):
-        ts(s(0), s(Y), -1.0, A.add)
-        ts(s(1), s(OFF), (-527.0, 257.0)[t % 2], A.mult, (256.0, 0.0)[t % 2], A.add)
-        tt(s(2), s(0), en_s, A.max)
-        tt(s(3), s(2), s(1), A.add)
-        cp(v("po"), s(3))
 
     def parents_b(t):
         if t % 2 == 0:
@@ -467,21 +480,29 @@ def rank_program(g, core, T, topo):
     def prep_a(t):
         if t == 0:
             ts(v("offs", 4, 6), v("base", 4, 6), col("ct", 255), A.subtract)
-        cp(s(28, 2), ind(v("wa", 0, VV), v("offs", 4, 6)))
+        cp(s(28, 2), ind(v("wa", 0, NL), v("offs", 4, 6)))
+        cp(v("ho"), s(20, 4))
         ts(s(30), s(28), 0.0, A.is_gt)
         tt(s(31), s(29), s(DJ), A.add)
-        tt(s(BD), s(30), s(DJ), A.mult)
-        ts(s(32), s(BD), -2.0, A.mult, 1.0, A.add)
-        tt(s(K0), s(31), s(32), A.add)
+        ts(sh(37, 0), sh(29, 0), 1.0, A.add)
+        bd = v("cin", 32, 48)
+        tt(bd, s(30), s(DJ), A.mult)
+        for h in range(2):
+            tt(v("un", 256 * h, 256 * h + 256), ind(bd, v("kb", 16 * h, 16 * h + 16)), v("wa", 256 * h, 256 * h + 256), A.mult)
+        ts(s(32), bd, -2.0, A.mult, 1.0, A.add)
+        tt(s(BD), s(37), bd, A.subtract)
+        tr(v("tt"), v("un"))
+        tt(v("k0", 8, 24), s(31), s(32), A.add)
+        scan(v("un"), v("rs"), v("tt"), 0.0, A.mult, A.max)
+        tt(s(38), v("k0", 7, 23), v("k0", 8, 24), A.subtract)
+        tt(s(39), v("un", 15, 256, 16), v("un", 271, 512, 16), A.max)
+        tt(v("cin", 48, 64), s(38), s(BD), A.add)
 
     def prep_b():
-        lin(v("cin", 32, 48), s(30), 64.0, -64.0)
-        lin(v("cin", 0, 16), s(BD), -1.0, 0.0)
-        lin(v("cin", 16, 32, 2), sh(BD, 1), -1.0, 0.0)
-        lin(v("cin", 17, 32, 2), sh(BD, 0), -1.0, 0.0)
-        lin(sh(DZ, 0), sh(29, 0), 1.0, 1.0)
-        lin(sh(MN, 0), sh(30, 0), 2.0, -1.0)
-        lin(sh(MN, 1), sh(30, 1), 2.0, -2.0)
+        act(v("tt", 0, 256), ind(s(39), v("kb", 32, 48)), F.Identity, scale=-1.0)
+        lin(v("cin", 0, 16), s(30), 64.0, -64.0)
+        lin(v("cin", 16, 32, 2), sh(30, 0), 2.0, -1.0)
+        lin(v("cin", 17, 32, 2), sh(30, 1), 2.0, -2.0)
 
     def layer(t):
         arrived("li%d" % t, ne[t], v("ll%d" % t))
@@ -496,6 +517,7 @@ def rank_program(g, core, T, topo):
         qz(pq, ps, v("pt"))
         for b in range(4):
             mm(v("pc", 512 * b, 512 * b + 128), v("wq", 128 * b, 128 * b + 128), v("wss", 128 * b, 128 * b + 128), pq, ps)
+        mirror_b(t)
         for b in range(4):
             if b % 2:
                 ts(v("ht", b, 256, 4), v("pc", 512 * b, 512 * b + 64), 0.0, A.max, 0.03125, A.mult)
@@ -525,8 +547,12 @@ def rank_program(g, core, T, topo):
             send_x(t)
             scores(t)
             unpack_x(t)
-            for st in range(3):
-                best(st)
+            if t == 1:
+                pick_q(2)
+            best(0)
+            tr(v("wa", NL, NL + 256), v("tt", 0, 256))
+            best(1)
+            best(2)
         places(t)
         if t == 0:
             tables_a()
@@ -534,20 +560,20 @@ def rank_program(g, core, T, topo):
         layer(t)
         if t == 0:
             tables_b()
-        mirror_b(t)
+        mirror_c(t)
         if t < R - 1:
-            pick_u(t + 1)
+            pick_s(t + 1)
             prep_a(t)
-        parents_a(t)
-        if t == R - 1:
+        else:
+            cp(v("ho"), s(20, 4))
             parents_b(t)
             qz(v("vq"), v("vs"), v("vt"))
             dma("S", T.op[:], T.opf[0:128:16, :], "dout", reads=[v("opf")])
         update(t)
-        if t == 0:
-            tables_c()
         if t < R - 1:
             prep_b()
+            if t == 0:
+                tables_c()
             parents_b(t)
             fill(v("win", 256, 352), 256.0)
 
@@ -559,5 +585,5 @@ def rank_program(g, core, T, topo):
     for h in range(2):
         cp(v("yf", 128 * h, 128 * h + 128), v("pc", 512 * h, 512 * h + 128))
     dma("S", T.y[:], T.yf[:], "dout", reads=[v("yf")])
-    for sem in sorted(total):
+    for sem in sorted(total, key=lambda x: x == "dout"):
         wait("S", (sem, total[sem], {}))

@@ -37,8 +37,8 @@ for _n, _c, _d in [
     ("mx", 264, F32), ("em", 256, BF), ("ct", 256, BF),
     ("ja", 288, BF), ("jb", 288, BF), ("jo", 192, U16), ("tt", 512, BF),
     ("va", 288, BF), ("vb", 288, BF), ("vc", 272, BF), ("v32", 32, BF), ("wa", 1344, BF), ("un", 512, BF),
-    ("rs", 512, BF), ("kb", 48, U16), ("kbi", 48, I32), ("k0", 24, F32),
-    ("offs", 8, U16), ("gi", 48, I32), ("mi", 48, I32), ("s", 640, F32), ("en", 24, F32), ("so", 16, U16),
+    ("rs", 512, BF), ("kb", 48, U16), ("kbi", 48, I32), ("k0", 24, F32), ("vo", 18, U16),
+    ("offs", 8, U16), ("gi", 48, I32), ("mi", 64, I32), ("s", 768, F32), ("en", 24, F32), ("so", 16, U16),
     ("win", 1040, BF), ("wim", 528, BF), ("ts", 128, BF), ("tm", 128, BF), ("mo", 16, U16), ("xo", 16, U16),
     ("ho", 64, U16), ("po", 16, U16), ("lo", 16, U16), ("cin", 64, F32),
     ("dp", 1088, BF), ("pt", 512, BF), ("ht", 512, BF), ("xg", 256, BF), ("opf", 256, F32), ("yf", 256, F32),
@@ -216,47 +216,44 @@ def rank_program(g, core, T, topo):
     P_, I_, E_, H_, K_, B1, Q_, S1, C1 = range(9)
     iota(col("ki", P_), [[0, 1]], 0, 1)
     iota(v("iota"), [[1, 288]], 0, 0, True)
+    iota(v("ki", 10, 28), [[0, 9], [16, 2]], 0, 0)
     iota(v("ki", 32, 56), [[1, 3], [16, 8]], 0, 0)
     iota(v("c64"), [[64, 4], [0, 16]], 0, 0, True)
     iota(v("kc"), [[1, 4], [0, 4]], 0, 0, True)
     iota(v("kbi", 0, 32), [[1, 2], [2, 8], [0, 2]], 0, 0)
     iota(v("kbi", 32, 48), [[1, 16]], 0, 0)
     iota(v("io4"), [[4, 256]], 0, 0, True)
-    ms(v("ez"), 0.0)
     for c, m in ((I_, 15), (E_, 16), (H_, 1), (K_, 14), (B1, 2)):
         ts(col("ki", c), col("ki", P_), m, A.bitwise_and)
+    ms(v("ez", 0, 256), 0.0)
     cp(v("kf", 0, 6), v("ki", 0, 6))
+    ms(v("ez", 256, 520), 0.0)
     kf = lambda c: col("kf", c)
     ts(col("ki", Q_), kf(I_), 16.0, A.mult, kf(E_), A.subtract)
     ts(col("ku", 1), kf(E_), 31.0, A.mult)
+    ts(v("vo"), v("ki", 10, 28), kf(I_), A.add)
+    ts(v("v32", 0, 16), v("iota", 0, 16), kf(I_), A.is_equal, 64.0, A.mult)
+    ts(v("v32", 16, 32), v("iota", 0, 16), kf(I_), A.is_equal, 128.0, A.mult)
     ts(col("ki", S1), col("ki", Q_), 16, A.bitwise_and)
     ts(col("ki", C1), col("ki", Q_), 224, A.bitwise_and)
     ts(v("ez", 3, 515, 4), v("iota", 0, 128), kf(P_), A.is_equal)
-    ts(v("v32", 0, 16), v("iota", 0, 16), kf(I_), A.is_equal, 64.0, A.mult)
-    ts(v("v32", 16, 32), v("iota", 0, 16), kf(I_), A.is_equal, 128.0, A.mult)
+    cp(v("ku", 8, 32), v("ki", 32, 56))
     cp(v("kf", S1, C1 + 1), v("ki", S1, C1 + 1))
     lin(v("jl"), v("iota", 0, 256, 16), 1.0, kf(I_))
     fill(v("win", 272, 288), float(SENT))
     lin(kf(21), kf(K_), -16.0 / 30.5, 192.0 - 15.5 / 30.5)
     fill(v("jb", 272, 288), float(SENT))
     fill(col("mx", 0), 0.0)
-    lin(v("va", 0, 32), v("v32"), 1.0, 1.0)
     fill(v("va", 272, 288), 0.0)
-    act(v("va", 32, 64), v("va", 0, 32), F.Copy)
     fill(v("vb", 272, 288), 0.0)
-    act(v("va", 64, 128), v("va", 0, 64), F.Copy)
     fill(v("ja", 272, 288), float(SENT))
-    act(v("va", 128, 256), v("va", 0, 128), F.Copy)
-    act(v("va", 256, 272), v("va", 0, 16), F.Copy)
     lin(kf(22), kf(K_), -16.0, -15.5)
-    act(v("vc"), v("va", 0, 272), F.Copy)
+    lin(v("va", 0, 272), ind(v("v32"), v("vo", 0, 17)), 1.0, 1.0)
     lin(v("cm1"), v("iota", 0, 256), 1.0 / 30.5, kf(21))
-    ts(kf(12), kf(S1), 16.0, A.mult, kf(C1), A.add)
-    for b in range(4):
-        qz(v("eq", 128 * b, 128 * b + 128), v("es", 128 * b, 128 * b + 128), v("ez", 3 - b, 515 - b))
-    ts(col("ku", 0), kf(12), kf(E_), A.add)
-    cp(v("ku", 8, 32), v("ki", 32, 56))
     ts(v("ku", 4, 8), v("iota", 0, 4), 0.0, A.mult, kf(I_), A.add)
+
+    def quant_e(b):
+        qz(v("eq", 128 * b, 128 * b + 128), v("es", 128 * b, 128 * b + 128), v("ez", 3 - b, 515 - b))
 
     def s(k, n=1):
         return v("s", 16 * k, 16 * (k + n))
@@ -310,15 +307,22 @@ def rank_program(g, core, T, topo):
 
     tt(s(0), v("pari"), v("jl"), A.not_equal)
     ts(s(1), v("pari"), -1.0, A.mult, float(SENT), A.add)
+    ts(kf(12), kf(S1), 16.0, A.mult, kf(C1), A.add)
+    quant_e(0)
     tt(s(2), s(0), s(1), A.mult)
+    quant_e(1)
     ts(v("jo", 0, 16), s(2), -1.0, A.mult, float(SENT), A.add)
     ts(col("jo", 16), col("s", 32), -1.0, A.mult, float(SENT), A.add)
+    cp(v("vc"), v("va", 0, 272))
+    ts(col("ku", 0), kf(12), kf(E_), A.add)
+    quant_e(2)
     act(v("win", 0, 272), ind(v("iota"), jo(0)), F.Copy)
     act(v("jb", 0, 272), ind(v("win", 0, 288), jo(0)), F.Copy)
     tt(v("vb", 0, 272), ind(v("va"), jo(0)), v("vc"), A.add)
     act(v("vc"), v("vb", 0, 272), F.Copy)
     lin(v("cm"), v("cm1"), BIG, -192.0 * BIG)
     act(v("dm1"), v("iota", 0, 256), F.Abs, bias=kf(22))
+    quant_e(3)
     quant_x(0)
     send_x(0)
     js, vs = ["jb", "ja"], ["va", "vb"]
@@ -376,6 +380,7 @@ def rank_program(g, core, T, topo):
             lin(kf(17), kf(E_), 1.0, 64.0)
             lin(kf(18), kf(E_), -1.0, 1024.0)
             fill(v("wim", 0, 96), 0.0)
+            fill(sh(37, 1), 0.0)
             fill(v("pt", 256, 512), 0.0)
             fill(v("ht", 256, 512), 0.0)
     unpack_x(0)
@@ -391,31 +396,42 @@ def rank_program(g, core, T, topo):
             cp(v("gi", 32, 48), ind(v("tt"), col("ku", 0)))
             cp(s(9), v("mi", 16, 32))
             ts(s(OFF), v("mi", 0, 16), 0.0, A.is_equal)
+            ts(s(30), v("mi", 0, 16), 0.0, A.not_equal)
             ts(v("mi", 32, 48), v("gi", 32, 48), 63, A.bitwise_and)
             scan(en_e, s(9), s(ZE), kf(E_), A.add, A.add)
             tt(s(1), s(OFF), v("dmp"), A.mult)
+            ts(v("mi", 48, 64), v("gi", 0, 16), 63, A.bitwise_and)
             tt(s(2), en_e, v("mi", 32, 48), A.subtract)
+            cp(s(DJ), v("mi", 32, 48))
+            cp(v("lo"), v("mi", 32, 48))
         else:
             ts(v("offs", 0, 6), v("base", 0, 6), col("ct", 255), A.subtract)
             tt(s(6, 2), ind(v("wa", 0, VV), v("offs", 2, 4)), v("cin", 32, 64), A.add)
             tt(s(4, 2), ind(v("wa", 0, VV), v("offs", 0, 2)), v("cin", 0, 32), A.mult)
+            if t < R - 1:
+                cp(s(28, 2), ind(v("wa", 0, NL), v("offs", 4, 6)))
             scan(s(8), s(6), s(7), kf(E_), A.add, A.add)
             tt(s(OFF), s(6), s(4), A.is_lt)
+            if t < R - 1:
+                ts(s(30), s(28), 0.0, A.is_gt)
             tt(s(2), s(8), s(5), A.add)
             tt(s(1), s(OFF), v("dmp"), A.mult)
-        tt(s(Y), s(2), s(1), A.max)
-        cp(v("so"), s(Y))
-        scat(v("win", 256, 784), v("so"), v("iota", 0, 256))
-        if t:
             for h in range(2):
                 tt(v("en", 2 + h, 18, 2), sh(8, 1), v("k0", 9, 24, 2), A.add)
-        else:
-            cp(s(DJ), v("mi", 32, 48))
-            cp(v("lo"), v("mi", 32, 48))
+        tt(s(Y), s(2), s(1), A.max)
+        if t < R - 1:
+            tt(v("cin", 32, 48), s(30), s(DJ), A.mult)
+        ts(s(40), en_e, kf(17), A.min, -1.0, A.add)
+        cp(v("so"), s(Y))
+        ts(s(41), s(Y), kf(17), A.is_ge)
+        tt(s(42), en_s, s(Y), A.subtract)
+        scat(v("win", 256, 784), v("so"), v("iota", 0, 256))
+        tt(s(3), s(40), s(42), A.add)
+        tt(s(43), s(41), v("dmp"), A.mult)
         tr(v("ts", 0, 64), v("win", 256, 320))
         tr(v("ts", 64, 128), v("win", 272, 336))
-        ts(s(2), s(Y), kf(17), A.is_ge)
-        ts(s(0), en_e, kf(17), A.min, -1.0, A.add)
+        tt(s(45), s(3), s(43), A.max)
+        ts(s(33), s(Y), -1.0, A.add)
         cp(v("sl%d" % t), ind(v("ts"), col("ku", 2)))
         send(partner[t], v("ll%d" % t), v("sl%d" % t, 0, 4), False, "li%d" % t)
 
@@ -423,18 +439,13 @@ def rank_program(g, core, T, topo):
         act(v("un", 0, 256), v("wa", VV, VV + 256), F.Abs, bias=-128.5)
         act(v("wa", A1, A1 + 256), v("wa", VV, VV + 256), F.Sign, bias=-128.5)
         act(v("un", 256, 512), v("un", 0, 256), F.Abs, bias=-64.0)
-        act(v("wa", A0, A0 + 256), v("un", 256, 512), F.Sign, bias=32.0, scale=-1.0)
         fill(v("rs", 0, 256), 1.0)
+        act(v("wa", A0, A0 + 256), v("un", 256, 512), F.Sign, bias=32.0, scale=-1.0)
         fill(v("rs", 256, 512), 1.0)
         act(v("wa", DP, DP + 256), ind(v("iota"), v("lo")), F.Copy)
         fill(v("rs", 0, 512, 16), 0.0)
-
-    def tables_b():
         for b in range(4):
             lin(v("j4", 16 * b, 16 * b + 16), v("jl"), 4.0, float(b))
-        lin(col("base", 4), kf(H_), 256.0, kf(14))
-        lin(col("base", 5), kf(14), 1.0, float(DP))
-        fill(sh(37, 1), 0.0)
         fill(col("k0", 7), 0.0)
 
     def tables_c():
@@ -442,22 +453,18 @@ def rank_program(g, core, T, topo):
         lin(col("base", 0), kf(H_), 256.0, kf(14))
         lin(col("base", 1), kf(14), 1.0, float(NL))
         lin(col("base", 2), kf(14), 1.0, float(NL))
+        lin(col("base", 4), kf(H_), 256.0, kf(14))
+        lin(col("base", 5), kf(14), 1.0, float(DP))
         lin(col("base", 3), kf(19), kf(15), float(VV))
 
     def mirror_a(t):
-        tt(s(1), en_s, s(Y), A.subtract)
-        tt(s(4), s(2), v("dmp"), A.mult)
-        ts(s(6), s(2), -4096.0, A.mult, kf(18), A.add)
-        ts(s(33), s(Y), -1.0, A.add)
-        tt(s(3), s(0), s(1), A.add)
-        ts(s(34), s(OFF), (-527.0, 257.0)[t % 2], A.mult, (256.0, 0.0)[t % 2], A.add)
+        cp(v("mo"), s(45))
+        ts(s(44), s(41), -4096.0, A.mult, kf(18), A.add)
         tt(s(35), s(33), en_s, A.max)
-        tt(s(5), s(3), s(4), A.max)
-        tt(s(26), s(3), s(6), A.add)
-        tt(s(36), s(35), s(34), A.add)
-        cp(v("mo"), s(5))
-        cp(v("po"), s(36))
+        ts(s(34), s(OFF), (-527.0, 257.0)[t % 2], A.mult, (256.0, 0.0)[t % 2], A.add)
         scat(v("wim"), v("mo"), v("io4"))
+        tt(s(26), s(3), s(44), A.add)
+        tt(s(36), s(35), s(34), A.add)
 
     def mirror_b(t):
         tr(v("tm", 0, 64), v("wim", 0, 64))
@@ -467,7 +474,7 @@ def rank_program(g, core, T, topo):
 
     def mirror_c(t):
         cp(v("xo"), s(0))
-        tt(s(20, 4), s(16, 4), v("j4"), A.max)
+        cp(v("po"), s(36))
         for b in range(4):
             act(v("xg", 64 * b, 64 * b + 64), ind(v("xb%d" % t, 0, 1024), v("xo", 4 * b, 4 * b + 4)), F.Copy)
 
@@ -478,22 +485,18 @@ def rank_program(g, core, T, topo):
             act(v("win", 0, 256), ind(v("win", 256, 1040), v("po")), F.Copy)
 
     def prep_a(t):
-        if t == 0:
-            ts(v("offs", 4, 6), v("base", 4, 6), col("ct", 255), A.subtract)
-        cp(s(28, 2), ind(v("wa", 0, NL), v("offs", 4, 6)))
-        cp(v("ho"), s(20, 4))
-        ts(s(30), s(28), 0.0, A.is_gt)
-        tt(s(31), s(29), s(DJ), A.add)
-        ts(sh(37, 0), sh(29, 0), 1.0, A.add)
         bd = v("cin", 32, 48)
-        tt(bd, s(30), s(DJ), A.mult)
         for h in range(2):
             tt(v("un", 256 * h, 256 * h + 256), ind(bd, v("kb", 16 * h, 16 * h + 16)), v("wa", 256 * h, 256 * h + 256), A.mult)
+        tt(s(20, 4), s(16, 4), v("j4"), A.max)
         ts(s(32), bd, -2.0, A.mult, 1.0, A.add)
-        tt(s(BD), s(37), bd, A.subtract)
+        tt(s(31), s(29) if t else v("mi", 48, 64), s(DJ), A.add)
         tr(v("tt"), v("un"))
+        ts(sh(37, 0), sh(29, 0) if t else v("mi", 48, 64, 2), 1.0, A.add)
         tt(v("k0", 8, 24), s(31), s(32), A.add)
+        cp(v("ho"), s(20, 4))
         scan(v("un"), v("rs"), v("tt"), 0.0, A.mult, A.max)
+        tt(s(BD), s(37), bd, A.subtract)
         tt(s(38), v("k0", 7, 23), v("k0", 8, 24), A.subtract)
         tt(s(39), v("un", 15, 256, 16), v("un", 271, 512, 16), A.max)
         tt(v("cin", 48, 64), s(38), s(BD), A.add)
@@ -558,16 +561,15 @@ def rank_program(g, core, T, topo):
             tables_a()
         mirror_a(t)
         layer(t)
-        if t == 0:
-            tables_b()
         mirror_c(t)
         if t < R - 1:
             pick_s(t + 1)
             prep_a(t)
         else:
+            tt(s(20, 4), s(16, 4), v("j4"), A.max)
+            qz(v("vq"), v("vs"), v("vt"))
             cp(v("ho"), s(20, 4))
             parents_b(t)
-            qz(v("vq"), v("vs"), v("vt"))
             dma("S", T.op[:], T.opf[0:128:16, :], "dout", reads=[v("opf")])
         update(t)
         if t < R - 1:

@@ -6,9 +6,19 @@ F = ActivationFunctionType
 R = 3
 STEP = [1, 2, 3]
 BF, F32, I32, U16, U8, X4 = "bfloat16", "float32", "int32", "uint16", "uint8", "float8_e4m3fn_x4"
-SENT = 272
+SENT = 256
+DUMP = 544
 BIG = 2.0 ** 90
-A0, A1, DP, NL, ZZ, VV = 0, 256, 512, 768, 1024, 1056
+M64 = 1.5 * 2.0 ** 29
+DP, T0, T1, ZZ, LS, VV = 0, 256, 512, 768, 1024, 1296
+HT, PT, DX = 0, 256, 512
+JA, JB, J1 = 16, 288, 256
+BLOCKS = [("i", 0, [[0, 2], [1, 16]]), ("jo", None, None), ("k32", 0, [[0, 2], [32, 4], [0, 4]]),
+          ("la", None, None), ("lc", None, None), ("lf", 0, [[0, 8], [256, 4]]),
+          ("e16", 0, [[16, 2], [0, 16]]), ("sl", 0, [[4, 8], [32, 2], [64, 2]]), ("r16", 7, [[0, 2], [4, 8], [0, 2]]),
+          ("xm", 0, [[4, 8], [32, 4]]), ("r32", 3, [[0, 4], [4, 8]]), ("mo", 7, [[0, 4], [8, 4], [0, 2]]),
+          ("y16", 0, [[0, 2], [4, 8], [1, 2]]), ("pc", None, None)]
+BL = {_b[0]: _k for _k, _b in enumerate(BLOCKS)}
 
 SCRATCH = {}
 
@@ -31,17 +41,18 @@ for _t in range(R):
 for _n, _c, _d in [
     ("ut", 512, BF), ("vt", 512, BF), ("uq", 128, X4), ("us", 128, U8), ("vq", 128, X4), ("vs", 128, U8),
     ("up", 384, X4), ("ups", 384, U8), ("wq", 512, X4), ("wss", 512, U8), ("eq", 512, X4), ("es", 512, U8),
-    ("ez", 520, BF), ("pari", 16, I32), ("iota", 288, BF), ("io4", 256, BF), ("ki", 64, I32), ("kf", 64, F32),
-    ("ku", 40, U16), ("jl", 16, F32), ("dmp", 16, F32), ("j4", 64, F32), ("c64", 64, F32), ("base", 8, F32),
-    ("cm", 256, BF), ("cm1", 256, BF), ("dm", 256, BF), ("dm1", 256, BF), ("kc", 16, F32),
-    ("mx", 264, F32), ("em", 256, BF), ("ct", 256, BF),
-    ("ja", 288, BF), ("jb", 288, BF), ("jo", 192, U16), ("tt", 512, BF),
-    ("va", 288, BF), ("vb", 288, BF), ("vc", 272, BF), ("v32", 32, BF), ("wa", 1344, BF), ("un", 512, BF),
-    ("rs", 512, BF), ("kb", 48, U16), ("kbi", 48, I32), ("k0", 24, F32), ("vo", 18, U16),
-    ("offs", 8, U16), ("gi", 48, I32), ("mi", 64, I32), ("s", 768, F32), ("en", 24, F32), ("so", 16, U16),
-    ("win", 1040, BF), ("wim", 528, BF), ("ts", 128, BF), ("tm", 128, BF), ("mo", 16, U16), ("xo", 16, U16),
-    ("ho", 64, U16), ("po", 16, U16), ("lo", 16, U16), ("cin", 64, F32),
-    ("dp", 1088, BF), ("pt", 512, BF), ("ht", 512, BF), ("xg", 256, BF), ("opf", 256, F32), ("yf", 256, F32),
+    ("ez", 520, BF), ("pari", 16, I32), ("iota", 272, BF), ("ki", 96, I32), ("kf", 8, F32), ("c16", 16, F32),
+    ("blk", 32 * len(BLOCKS), BF), ("blt", 32 * len(BLOCKS) + 32, BF), ("ku", 40, U16), ("pk", 24, U16), ("kb", 48, U16),
+    ("jl", 16, F32), ("dmp", 16, F32), ("j4", 64, F32), ("c64", 64, F32), ("base", 8, F32), ("kc", 16, F32), ("kk", 8, F32),
+    ("cn", 32, F32), ("cd", 32, F32), ("cm", 128, BF), ("cm1", 128, BF), ("dm", 128, BF),
+    ("mx", 272, F32), ("em", 256, BF), ("ct", 256, BF),
+    ("jj", 560, BF), ("j1", 1056, F32), ("jo", 80, U16), ("tt", 544, BF),
+    ("vv", 544, BF), ("vc", 1024, BF), ("v32", 32, BF), ("vo", 16, U16), ("wa", VV + 272, BF),
+    ("un", 512, BF), ("rs", 256, BF), ("tu", 512, BF), ("ub", 512, BF), ("lw", 256, BF),
+    ("offs", 8, U16), ("gi", 48, I32), ("mi", 32, I32), ("s", 1088, F32), ("en", 40, F32), ("sg", 40, F32), ("ds", 40, F32),
+    ("so", 16, U16), ("win", 512 * 31 + 16, BF), ("ts", 128, BF), ("wm", 128, BF), ("tm", 128, BF), ("mo", 16, U16), ("xo", 16, U16),
+    ("ho", 64, U16), ("po", 16, U16),
+    ("dp", DX + 1088, BF), ("xg", 256, BF), ("yf", 256, F32),
 ]:
     _sb(_n, _c, _d)
 SCRATCH["pa"] = ("psum", [128, 2048], F32)
@@ -49,6 +60,23 @@ SCRATCH["pc"] = ("psum", [128, 2048], F32)
 
 SEMAPHORES = ["sV", "sA", "sP", "sG", "dpar", "dx", "du", "dv", "dw", "dws", "dout", "loc"] + \
              ["%s%d" % (_k, _t) for _k in ("qx", "li", "hh") for _t in range(R)]
+
+CYC, WAKE, HOP, LOAD = 1.0, 150.0, 700.0, 900.0
+GATHER, SCATTER, PE = 1.3, 3.2, 0.8
+SLACK = 150.0
+RADIX = (3, 3, 4)
+FIRST = [
+    "pari:0 xb0:0 ut:0",
+    "blk:i c16:0 ki:0 iota:0 kf:0 blk:jo blk:48 blk:k32 ki:16 blk:lf blk:e16 blk:sl blk:r16 base:0",
+    "blt:i jl:0 vo:0 v32:0 v32:16 ku:32 s:0 s:256 blt:448 s:272 ez:3 jo:0 vc:0 j1:384 vv:272 blt:jo pk:0 vv:0' xq0:0 uq:0 "
+    "xq0:128 ku:2 tt:0 tt:256 up:0 jo:16 up:64 vv:272' eq:0 vv:0'' mx:1 blt:la tt:0' tt:256' mx:137 jo:32 em:0 vv:272'' "
+    "em:128 base:0' vv:0''' ct:0 ct:128 wa:1296 offs:0 offs:1 tt:0'' tt:256'' gi:0 s:544 s:576 gi:32 ku:14",
+    "vv:0 j1:256 jj:16 kf:1 blk:lc jj:288 vc:256 blk:130 cm1:0 ups:0 ups:64 jj:16' cm:0 jj:288' vc:512 vc:768 kf:4 cm1:0' dm:0 "
+    "ups:128 ups:192 s:960 ub:0 ups:256 ups:320",
+    "wa:1296 eq:128 eq:256 eq:384", "wa:1296 blt:xm", "so:0 s:368", "so:0 up:128", "so:0 up:192", "so:0 up:256", "so:0 up:320", "so:0 vq:0",
+]
+PARTS = [("A", 0, 0, 16), ("A", 2, 0, 16), ("A", 3, 12, 16), ("V", 1, 0, 16), ("V", 3, 0, 8), ("V", 3, 8, 12)]
+_ORDER = []
 
 
 def _overlap(a, b):
@@ -59,67 +87,151 @@ def _overlap(a, b):
     return True
 
 
+def _order(ops):
+    if _ORDER:
+        return _ORDER
+    n = len(ops)
+    wake = [0.0 if o["e"] == "R" else WAKE for o in ops]
+    full = [o["len"] + o["lat"] for o in ops]
+    tail, urge = [0.0] * n, [0.0] * n
+    left, seen = [], set()
+
+    def visit(i):
+        if i not in seen:
+            seen.add(i)
+            for p in ops[i]["deps"] + ops[i]["behind"]:
+                visit(p)
+            left.append(i)
+    for i in range(n):
+        visit(i)
+    for i in reversed(left):
+        tail[i] += full[i]
+        urge[i] += full[i] + ops[i]["urge"]
+        for p in ops[i]["deps"]:
+            tail[p] = max(tail[p], tail[i] + wake[i])
+            urge[p] = max(urge[p], urge[i] + wake[i])
+        for p in ops[i]["behind"]:
+            tail[p] = max(tail[p], tail[i] - ops[p]["lat"])
+            urge[p] = max(urge[p], urge[i] - ops[p]["lat"])
+    done, free = {}, {}
+    while left:
+        est, near, best = {}, {}, None
+        for i in left:
+            est[i] = max([free.get(ops[i]["e"], 0.0)] + [(done[p] if p in done else est[p] + full[p]) + wake[i] for p in ops[i]["deps"]] +
+                         [est[p] + ops[p]["len"] for p in ops[i]["behind"] if p not in done])
+        bound = max(est[i] + tail[i] for i in left)
+        soon = min(est.values()) + 3000.0
+        for i in left:
+            if est[i] < soon:
+                near.setdefault(ops[i]["e"], []).append(i)
+        for i in left:
+            if est[i] < soon and all(p in done for p in ops[i]["deps"] + ops[i]["behind"]):
+                end = est[i] + ops[i]["len"]
+                hurt = any(est[j] < end and tail[j] > tail[i] and end + tail[j] > max(bound - SLACK, est[j] + ops[j]["len"] + tail[i])
+                           for j in near[ops[i]["e"]])
+                key = (hurt, est[i], -urge[i])
+                if best is None or key < best[0]:
+                    best = (key, i)
+        i = best[1]
+        done[i] = est[i] + full[i]
+        if ops[i]["e"] != "R":
+            free[ops[i]["e"]] = est[i] + ops[i]["len"]
+        left.remove(i)
+        _ORDER.append(i)
+    return _ORDER
+
+
 def rank_program(g, core, T, topo):
     rank = T.rank_of(core)
     if rank is None:
         return
     eng = {"V": g.vector, "A": g.scalar, "P": g.tensor, "G": g, "S": g.sync}
-    known = {e: {} for e in eng}
+    ops = []
     hist = []
-    total = {}
 
     def v(name, lo=0, hi=None, step=1):
         if hi is None:
             hi = SCRATCH[name][1][1]
         ap = T[name][:, lo:hi] if step == 1 else T[name][:, lo:hi:step]
+        n, wide = (hi - lo + step - 1) // step, SCRATCH[name][2] not in (BF, U16)
         if SCRATCH[name][0] == "psum":
-            return (ap, [(name, lo // 512 * 512, (hi + 511) // 512 * 512, 1)])
-        return (ap, [(name, lo, hi, step)])
+            return (ap, [(name, lo // 512 * 512, (hi + 511) // 512 * 512, 1)], n, wide, False)
+        return (ap, [(name, lo, hi, step)], n, wide, False)
 
     def col(name, c):
         return v(name, c, c + 1)
 
     def ind(w, o):
-        return (w[0].indirect(o[0]), w[1] + o[1])
+        return (w[0].indirect(o[0]), w[1] + o[1], 16 * o[2], w[3], True)
 
-    def wait(e, tok):
-        sem, val, clock = tok
-        if known[e].get(sem, 0) >= val:
-            return
-        eng[e].wait_ge(T.sem[sem], val)
-        for k, x in list(clock.items()) + [(sem, val)]:
-            if known[e].get(k, 0) < x:
-                known[e][k] = x
-
-    def issue(e, fn, reads, writes, after=(), sem=None, inc=1):
+    def issue(e, fn, reads, writes, length, lat=0.0, after=(), sem=None, inc=1, urge=0.0):
         rr = [r for x in reads for r in x[1]]
         ww = [r for x in writes for r in x[1]]
-        need = {}
-        for reg, isw, tok, q in hist:
-            ps = SCRATCH[reg[0]][0] == "psum" and q != e
+        deps = set(after)
+        for reg, isw, k in hist:
+            ps = SCRATCH[reg[0]][0] == "psum" and ops[k]["e"] != e
             if any(_overlap(reg, r) for r in ww) or ((isw or ps) and any(_overlap(reg, r) for r in rr)):
-                if tok[0] not in need or need[tok[0]][1] < tok[1]:
-                    need[tok[0]] = tok
-        for tok in sorted(list(need.values()) + list(after), key=lambda x: -len(x[2])):
-            wait(e, tok)
-        if sem is None:
-            sem = "s" + e
-        total[sem] = total.get(sem, 0) + inc
-        tok = (sem, total[sem], dict(known[e]))
-        ins = fn()
-        if ins is not None:
-            ins.then_inc(T.sem[sem], inc)
+                deps.add(k)
+        me = len(ops)
+        ops.append({"e": e, "fn": fn, "deps": sorted(deps), "len": length, "lat": lat, "sem": sem or "s" + e, "inc": inc, "urge": urge,
+                    "behind": [], "name": "%s:%d" % ww[0][:2] if ww else ""})
         keep = [h for h in hist if not any(h[0][0] == w[0] and w[3] == 1 and w[1] <= h[0][1] and h[0][2] <= w[2] for w in ww)]
-        hist[:] = keep + [(r, False, tok, e) for r in rr] + [(r, True, tok, e) for r in ww]
-        return tok
+        hist[:] = keep + [(r, False, me) for r in rr] + [(r, True, me) for r in ww]
+        return me
 
-    def arrived(sem, val, *views):
-        tok = (sem, val, {})
-        total[sem] = val
-        for x in views:
-            for r in x[1]:
-                hist.append((r, True, tok, "R"))
-        return tok
+    def arrived(sem, val, sent, *views):
+        return issue("R", None, [], views, 0.0, 0.0, sent, sem, val)
+
+    def emit():
+        known = {e: {} for e in eng}
+        total, tok = {}, {}
+
+        def wait(e, t):
+            sem, val, clock = t
+            if known[e].get(sem, 0) >= val:
+                return
+            eng[e].wait_ge(T.sem[sem], val)
+            for k, x in list(clock.items()) + [(sem, val)]:
+                if known[e].get(k, 0) < x:
+                    known[e][k] = x
+        named = {}
+        for i, o in enumerate(ops):
+            name = o["name"]
+            while name in named:
+                name += "'"
+            named[name] = i
+        for k in BL:
+            for b in ("blk", "blt"):
+                named["%s:%s" % (b, k)] = named.get("%s:%d" % (b, 32 * BL[k]))
+        for line in FIRST:
+            calls = [named[x] for x in line.split()]
+            for a, b in zip(calls, calls[1:]):
+                ops[b]["behind"].append(a)
+        for i in _order(ops):
+            o = ops[i]
+            e, sem = o["e"], o["sem"]
+            total[sem] = total.get(sem, 0) + o["inc"]
+            if e == "R":
+                tok[i] = (sem, total[sem], {})
+                continue
+            need = {}
+            for p in o["deps"]:
+                if tok[p][0] not in need or need[tok[p][0]][1] < tok[p][1]:
+                    need[tok[p][0]] = tok[p]
+            for t in sorted(need.values(), key=lambda x: -len(x[2])):
+                wait(e, t)
+            tok[i] = (sem, total[sem], dict(known[e]))
+            ins = o["fn"]()
+            if ins is not None:
+                ins.then_inc(T.sem[sem], o["inc"])
+        for sem in sorted(total, key=lambda x: x == "dout"):
+            wait("S", (sem, total[sem], {}))
+
+    def span(out, *ins, twice=False):
+        if any(x[4] for x in ins):
+            return 55.0 + GATHER * out[2]
+        wide = any(x[3] for x in (out,) + ins)
+        return CYC * max(64.0, out[2] * (2.0 if twice else 1.0) * (1.0 if wide else 0.5))
 
     def sc(x):
         return x[0] if isinstance(x, tuple) else x
@@ -129,29 +241,30 @@ def rank_program(g, core, T, topo):
 
     def ts(out, a, s1, op0, s2=None, op1=None):
         if op1 is None:
-            return issue("V", lambda: g.vector.tensor_scalar(out[0], a[0], sc(s1), None, op0), tup(a, s1), [out])
-        return issue("V", lambda: g.vector.tensor_scalar(out[0], a[0], sc(s1), sc(s2), op0, op1), tup(a, s1, s2), [out])
+            return issue("V", lambda: g.vector.tensor_scalar(out[0], a[0], sc(s1), None, op0), tup(a, s1), [out], span(out, a))
+        return issue("V", lambda: g.vector.tensor_scalar(out[0], a[0], sc(s1), sc(s2), op0, op1), tup(a, s1, s2), [out], span(out, a))
 
     def tt(out, a, b, op):
-        return issue("V", lambda: g.vector.tensor_tensor(out[0], a[0], b[0], op), [a, b], [out])
+        return issue("V", lambda: g.vector.tensor_tensor(out[0], a[0], b[0], op), [a, b], [out],
+                     span(out, a, b, twice=SCRATCH[a[1][0][0]][0] == "sbuf"))
 
     def cp(out, a):
-        return issue("V", lambda: g.vector.tensor_copy(out[0], a[0]), [a], [out])
+        return issue("V", lambda: g.vector.tensor_copy(out[0], a[0]), [a], [out], span(out, a))
 
     def scat(w, o, a):
-        return issue("V", lambda: g.vector.tensor_copy(w[0].indirect(o[0]), a[0]), [a, o], [w])
+        return issue("V", lambda: g.vector.tensor_copy(w[0].indirect(o[0]), a[0]), [a, o], [w], 50.0 + SCATTER * a[2])
 
     def ms(out, c):
-        return issue("V", lambda: g.vector.memset(out[0], c), [], [out])
+        return issue("V", lambda: g.vector.memset(out[0], c), [], [out], span(out))
 
     def scan(out, a, b, init, op0, op1):
-        return issue("V", lambda: g.vector.tensor_tensor_scan(out[0], a[0], b[0], sc(init), op0, op1), tup(a, b, init), [out])
+        return issue("V", lambda: g.vector.tensor_tensor_scan(out[0], a[0], b[0], sc(init), op0, op1), tup(a, b, init), [out], span(out, a, b))
 
     def tr(out, a):
-        return issue("V", lambda: g.vector.transpose(out[0], a[0]), [a], [out])
+        return issue("V", lambda: g.vector.transpose(out[0], a[0]), [a], [out], span(out, a))
 
-    def qz(q, s, a):
-        return issue("V", lambda: g.vector.quantize_mx(q[0], s[0], a[0]), [a], [q, s])
+    def qz(q, s, a, urge=0.0):
+        return issue("V", lambda: g.vector.quantize_mx(q[0], s[0], a[0]), [a], [q, s], 12.0 + 0.22 * a[2], urge=urge)
 
     def act(out, a, f, bias=None, scale=None):
         kw = {}
@@ -159,36 +272,36 @@ def rank_program(g, core, T, topo):
             kw["bias"] = sc(bias)
         if scale is not None:
             kw["scale"] = sc(scale)
-        return issue("A", lambda: g.scalar.activation(out[0], a[0], f, **kw), tup(a, bias, scale), [out])
+        return issue("A", lambda: g.scalar.activation(out[0], a[0], f, **kw), tup(a, bias, scale), [out],
+                     65.0 + GATHER * out[2] if a[4] else CYC * max(64.0, out[2]))
 
     def lin(out, a, scale, bias):
         return act(out, a, F.Identity, bias, scale)
 
     def fill(out, c):
-        r = out[1][0]
-        return lin(out, v("iota", 0, (r[2] - r[1] + r[3] - 1) // r[3]), 0.0, c)
+        return lin(out, v("iota", 0, out[2]), 0.0, c)
 
     def mm(out, lq, ls, rq, rs):
-        return issue("P", lambda: g.tensor.matmul_mx(out[0], lq[0], ls[0], rq[0], rs[0], True, True), [lq, ls, rq, rs], [out])
+        return issue("P", lambda: g.tensor.matmul_mx(out[0], lq[0], ls[0], rq[0], rs[0], True, True), [lq, ls, rq, rs], [out],
+                     PE * (out[2] + 16), 50.0)
 
-    def iota(out, pat, base, cm, small=False):
-        if small:
-            return issue("G", lambda: g.iota(out[0], pat, base, cm, allow_small_or_imprecise_dtypes=True), [], [out])
-        return issue("G", lambda: g.iota(out[0], pat, base, cm), [], [out])
+    def iota(out, pat, base=0, cm=0, urge=0.0):
+        kw = {} if SCRATCH[out[1][0][0]][2] == I32 else {"allow_small_or_imprecise_dtypes": True}
+        return issue("G", lambda: g.iota(out[0], pat, base, cm, **kw), [], [out], CYC * (160.0 + 2 * out[2]), urge=urge)
 
-    def dma(e, out, in_, sem, reads=(), writes=(), after=()):
-        return issue(e, lambda: eng[e].dma_start(out, in_), list(reads), list(writes), after, sem, 16)
+    def dma(e, out, in_, sem, lat, reads=(), writes=(), after=(), urge=0.0):
+        return issue(e, lambda: eng[e].dma_start(out, in_), list(reads), list(writes), 50.0, LOAD + lat, after, sem, 16, urge)
 
     def u8(x):
         return x[0].bitcast(dt.uint8)
 
-    def send(to, dst, src, raw, sem):
+    def send(to, dst, src, raw, sem, lat, first=0.0):
         rid, pid = topo.addr(to)[:2]
         m = topo.mask(core, to)
 
         def fn():
             g.remote_dma(u8(dst) if raw else dst[0], u8(src) if raw else src[0], T.sem[sem], T.sem.loc, pid, rid, m)
-        issue("G", fn, [src], [], (), "loc", len(topo.engines(core, to)))
+        return issue("G", fn, [src], [], 200.0 + first, HOP + lat, (), "loc", len(topo.engines(core, to)))
 
     def send2(to, dq, sq, ds, ss, sem):
         rid, pid = topo.addr(to)[:2]
@@ -201,391 +314,336 @@ def rank_program(g, core, T, topo):
                 RemoteDMATransfer(dst_ids=[DstId(rid=rid, pnc=pid)], dma_engine_mask=masks[0], remote_sem=T.sem[sem], src=u8(sq), dst=u8(dq)),
                 RemoteDMATransfer(dst_ids=[DstId(rid=rid, pnc=pid)], dma_engine_mask=masks[1], remote_sem=T.sem[sem], src=ss[0], dst=ds[0]),
             ], local_sem=T.sem.loc)
-        issue("G", fn, [sq, ss], [], (), "loc", len(en))
+        return issue("G", fn, [sq, ss], [], 200.0, HOP + 400.0, (), "loc", len(en))
 
     partner = [T.cores[rank ^ STEP[t]] for t in range(R)]
     ne = [len(topo.engines(partner[t], core)) for t in range(R)]
-
-    dma("S", T.pari[:], T.par[:], "dpar", writes=[v("pari")])
-    tx = dma("S", T.xb0[:, 0:1024], T.x[:], "dx", writes=[v("xb0", 0, 1024)])
-    dma("S", T.ut[:], T.u[:], "du", writes=[v("ut")])
-    dma("S", T.wq[:].bitcast(dt.uint8), T.wc[:], "dw", writes=[v("wq")], after=[tx])
-    dma("S", T.wss[:], T.ws[:], "dws", writes=[v("wss")])
-    dma("S", T.vt[:], T.v[:], "dv", writes=[v("vt")])
-
-    P_, I_, E_, H_, K_, B1, Q_, S1, C1 = range(9)
-    iota(col("ki", P_), [[0, 1]], 0, 1)
-    iota(v("iota"), [[1, 288]], 0, 0, True)
-    iota(v("ki", 10, 28), [[0, 9], [16, 2]], 0, 0)
-    iota(v("ki", 32, 56), [[1, 3], [16, 8]], 0, 0)
-    iota(v("c64"), [[64, 4], [0, 16]], 0, 0, True)
-    iota(v("kc"), [[1, 4], [0, 4]], 0, 0, True)
-    iota(v("kbi", 0, 32), [[1, 2], [2, 8], [0, 2]], 0, 0)
-    iota(v("kbi", 32, 48), [[1, 16]], 0, 0)
-    iota(v("io4"), [[4, 256]], 0, 0, True)
-    for c, m in ((I_, 15), (E_, 16), (H_, 1), (K_, 14), (B1, 2)):
-        ts(col("ki", c), col("ki", P_), m, A.bitwise_and)
-    ms(v("ez", 0, 256), 0.0)
-    cp(v("kf", 0, 6), v("ki", 0, 6))
-    ms(v("ez", 256, 520), 0.0)
-    kf = lambda c: col("kf", c)
-    ts(col("ki", Q_), kf(I_), 16.0, A.mult, kf(E_), A.subtract)
-    ts(col("ku", 1), kf(E_), 31.0, A.mult)
-    ts(v("vo"), v("ki", 10, 28), kf(I_), A.add)
-    ts(v("v32", 0, 16), v("iota", 0, 16), kf(I_), A.is_equal, 64.0, A.mult)
-    ts(v("v32", 16, 32), v("iota", 0, 16), kf(I_), A.is_equal, 128.0, A.mult)
-    ts(col("ki", S1), col("ki", Q_), 16, A.bitwise_and)
-    ts(col("ki", C1), col("ki", Q_), 224, A.bitwise_and)
-    ts(v("ez", 3, 515, 4), v("iota", 0, 128), kf(P_), A.is_equal)
-    cp(v("ku", 8, 32), v("ki", 32, 56))
-    cp(v("kf", S1, C1 + 1), v("ki", S1, C1 + 1))
-    lin(v("jl"), v("iota", 0, 256, 16), 1.0, kf(I_))
-    fill(v("win", 272, 288), float(SENT))
-    lin(kf(21), kf(K_), -16.0 / 30.5, 192.0 - 15.5 / 30.5)
-    fill(v("jb", 272, 288), float(SENT))
-    fill(col("mx", 0), 0.0)
-    fill(v("va", 272, 288), 0.0)
-    fill(v("vb", 272, 288), 0.0)
-    fill(v("ja", 272, 288), float(SENT))
-    lin(kf(22), kf(K_), -16.0, -15.5)
-    lin(v("va", 0, 272), ind(v("v32"), v("vo", 0, 17)), 1.0, 1.0)
-    lin(v("cm1"), v("iota", 0, 256), 1.0 / 30.5, kf(21))
-    ts(v("ku", 4, 8), v("iota", 0, 4), 0.0, A.mult, kf(I_), A.add)
-
-    def quant_e(b):
-        qz(v("eq", 128 * b, 128 * b + 128), v("es", 128 * b, 128 * b + 128), v("ez", 3 - b, 515 - b))
 
     def s(k, n=1):
         return v("s", 16 * k, 16 * (k + n))
 
     def sh(k, h):
         return v("s", 16 * k + h, 16 * k + 16, 2)
-    jo = lambda m: v("jo", 32 * m, 32 * m + 17)
 
-    def quant_x(t):
-        for h in range(2):
-            qz(v("xq%d" % t, 128 * h, 128 * h + 128), v("xs%d" % t, 128 * h, 128 * h + 128), v("xb%d" % t, 512 * h, 512 * h + 512))
+    kf = lambda c: col("kf", c)
+    jo = lambda m: v("jo", 16 * m, 16 * m + 16)
+    pp = lambda name: col("blt", 32 * BL[name])
+    ku = lambda name, n=1: v("ku", 2 * BL[name], 2 * BL[name] + n)
+    c32 = col("blt", 32 * len(BLOCKS))
+    P_, CMB, CAP, C1, DMB = range(5)
+    NR, DJ, Y, OFF, S2, S3, S26, LM, HA, HB, W = 0, 1, 2, 3, 4, 5, 6, 7, 8, 12, 16
+    EM, DD, SC, GA, GC, GF, BB, YY, B2, KK, CA, CC, CD, D1, D5, S1, S0, _, PW = range(28, 66, 2)
+    ends, starts = v("en", 7, 39, 4), v("en", 3, 35, 4)
 
-    def send_x(t):
-        send(partner[t], v("ls%d" % t, 0, 256), v("xs%d" % t), False, "qx%d" % t)
-        send(partner[t], v("lq%d" % t, 0, 256), v("xq%d" % t), True, "qx%d" % t)
+    def w32(k, lo=0, hi=32, step=1):
+        return v("s", 16 * k + lo, 16 * k + hi, step)
+    anc = w32(PW, 0, 31)
+    LA, LC, LF, LB = [v("offs", 2 * k, 2 * k + 2) for k in range(4)]
 
-    def scores(t):
-        for h in range(2):
-            mm(v("pc", 512 * h, 512 * h + 128), v("up", 128 * t, 128 * t + 128), v("ups", 128 * t, 128 * t + 128),
-               v("xq%d" % t, 128 * h, 128 * h + 128), v("xs%d" % t, 128 * h, 128 * h + 128))
+    dma("S", T.pari[:], T.par[:], "dpar", 300.0, writes=[v("pari")], urge=3e6)
+    tx = dma("S", T.xb0[:, 0:1024], T.x[:], "dx", 2000.0, writes=[v("xb0", 0, 1024)], urge=2e6)
+    dma("S", T.ut[:], T.u[:], "du", 2500.0, writes=[v("ut")], urge=1e6)
+    dma("S", T.wq[:].bitcast(dt.uint8), T.wc[:], "dw", 2000.0, writes=[v("wq")], after=[tx])
+    dma("S", T.wss[:], T.ws[:], "dws", 2000.0, writes=[v("wss")], after=[tx])
+    dma("S", T.vt[:], T.v[:], "dv", 3000.0, writes=[v("vt")], after=[tx])
 
-    def pick_q(t):
-        o = v("ku", 8 + 8 * t, 16 + 8 * t)
-        out, w = v("up", 128 * t, 128 * t + 128), v("uq")
-        issue("V", lambda: g.vector.tensor_copy(out[0].bitcast(dt.uint32), w[0].bitcast(dt.uint32).indirect(o[0])), [w, o], [out])
+    for k, (name, base, pat) in enumerate(BLOCKS):
+        if pat is not None:
+            iota(v("blk", 32 * k, 32 * k + 32), pat, base)
+    blk = lambda name, lo=0, hi=32, step=1: v("blk", 32 * BL[name] + lo, 32 * BL[name] + hi, step)
+    iota(blk("jo", 0, 16), [[32, 8], [288, 2]])
+    iota(blk("jo", 16, 32), [[32, 8], [-256, 2]], 272)
+    for lo in (0, 16):
+        iota(blk("pc", lo, lo + 16), [[4, 4], [0, 2], [1, 2]])
+    lin(blk("la"), blk("i"), 0.0, float(LS))
+    lin(blk("la", 0, 32, 4), blk("i", 0, 8), 0.0, float(DP))
+    lin(blk("lc"), blk("lf"), 1.0, float(T0))
+    lin(blk("lc", 2, 32, 4), blk("i", 0, 8), 0.0, float(LS))
+    for a, b in (("i", "i"), ("jo", "k32"), ("la", "r16"), ("xm", "pc")):
+        tr(v("blt", 32 * BL[a], 32 * BL[b] + 32), v("blk", 32 * BL[a], 32 * BL[b] + 32))
+    for a, b in (("jo", "jo"), ("sl", "r16"), ("xm", "pc")):
+        cp(v("ku", 2 * BL[a], 2 * BL[b] + 2), v("blt", 32 * BL[a], 32 * BL[b] + 32, 16))
+    ts(col("ku", 2 * BL["pc"] + 1), pp("pc"), 16.0, A.add)
+    cp(v("ku", 32, 36), v("blt", 0, 4))
+    iota(v("c16"), [[16, 16]])
+    iota(v("iota"), [[1, 272]])
+    tr(v("blt", 32 * len(BLOCKS), 32 * len(BLOCKS) + 32), v("iota", 0, 32))
+    ts(v("jl"), v("c16"), pp("i"), A.add)
+    lin(v("dmp"), v("jl"), 1.0, float(DUMP))
+    for b in range(4):
+        lin(v("j4", 16 * b, 16 * b + 16), v("jl"), 4.0, float(b))
+    iota(v("ki", 0, 16), [[0, 8], [16, 2]], urge=1000.0)
+    ts(v("vo"), v("ki", 0, 16), pp("i"), A.add)
+    iota(v("ki", 16, 40), [[1, 3], [16, 8]])
+    cp(v("pk"), v("ki", 16, 40))
+    iota(v("ki", 48, 80), [[1, 2], [4, 8], [0, 2]], 1)
+    iota(v("ki", 80, 96), [[1, 16]])
+    cp(v("kb"), v("ki", 48, 96))
+    iota(v("cn"), [[16, 4], [0, 8]])
+    lin(v("cn"), v("cn"), 1.0, c32)
+    fill(v("cd"), 0.0)
+    lin(v("cd", 7, 32, 8), v("jl", 0, 4), -1.0, 0.0)
+    iota(v("kc"), [[1, 4], [0, 4]])
+    iota(v("c64"), [[64, 4], [0, 16]], 1024)
+    iota(v("rs"), [[0, 16], [64, 16]])
+    iota(v("wa", ZZ, ZZ + 256), [[0, 256]])
+    iota(v("dp", DX + 256, DX + 1088, 272), [[0, 4]])
+    fill(v("wa", VV - 16, VV), 0.0)
+    fill(v("wa", VV + 256, VV + 272), 0.0)
+    for name in ("en", "sg", "ds"):
+        fill(v(name), 0.0)
+    lin(col("en", 3), pp("e16"), 1.0, 0.0)
+    lin(kf(CAP), pp("e16"), 1.0, 64.0)
+    lin(kf(C1), pp("e16"), 1.0, 1.0)
+    iota(v("base"), [[0, 4], [128, 2]], 128)
+    tt(v("base", 0, 6), v("blt", 32 * BL["la"], 32 * BL["lf"] + 32, 16), v("base", 0, 6), A.add)
+    iota(v("kk"), [[256, 8]], 256 * 32768)
+    fill(w32(PW, -2, -1), 0.0)
+    fill(w32(D1), 0.0)
+    fill(w32(S0), -32768.0)
+    for h in range(2):
+        lin(w32(S1, h, 32, 4), v("dmp", h, 16, 2), 256.0, -2048.0 * 256)
+        lin(w32(S0, h, 32, 4), v("dmp", h, 16, 2), 1.0, -2048.0)
+    lin(kf(CMB), pp("k32"), -1.0 / 30.5, 192.0 - 15.5 / 30.5)
+    lin(v("cm1"), v("iota", 0, 128), 1.0 / 30.5, kf(CMB))
+    lin(v("cm"), v("cm1"), BIG, -192.0 * BIG)
+    lin(kf(DMB), pp("k32"), -1.0, 0.5)
+    act(v("cm1"), v("iota", 0, 128), F.Sign, bias=kf(DMB))
+    lin(v("dm"), v("cm1"), 0.5, 0.5)
+    ms(v("mx", 0, 272, 136), 0.0)
+    ms(v("ez", 0, 256), 0.0)
+    ms(v("ez", 256, 520), 0.0)
+    iota(kf(P_), [[0, 1]], 0, 1, urge=5000.0)
+    ts(v("ez", 3, 515, 4), v("iota", 0, 128), kf(P_), A.is_equal)
+    for b in range(4):
+        qz(v("eq", 128 * b, 128 * b + 128), v("es", 128 * b, 128 * b + 128), v("ez", 3 - b, 515 - b), 6000.0)
+    qz(v("uq"), v("us"), v("ut"))
+    qz(v("vq"), v("vs"), v("vt"))
+    for t in range(R):
+        for c in range(8 * t, 8 * t + 8, 4):
+            o, out, w = v("pk", c, c + 4), v("up", 16 * c, 16 * c + 64), v("uq")
+            issue("V", lambda o=o, out=out, w=w: g.vector.tensor_copy(out[0].bitcast(dt.uint32), w[0].bitcast(dt.uint32).indirect(o[0])),
+                  [w, o], [out], 55.0 + GATHER * 64)
+            act(v("ups", 16 * c, 16 * c + 64), ind(v("us"), o), F.Copy)
 
-    def pick_s(t):
-        act(v("ups", 128 * t, 128 * t + 128), ind(v("us"), v("ku", 8 + 8 * t, 16 + 8 * t)), F.Copy)
+    def two_turns(name, lo):
+        tr(v("tt", 0, 256), v(name, lo, lo + 256))
+        tr(v("tt", 256, 544), v(name, lo - 16, lo + 272))
 
-    def best(stage, hs=(0, 1)):
-        if stage == 2:
-            scan(v("ct"), v("em"), v("dm"), 0.0, A.mult, A.add)
-            return
-        for h in hs:
-            a, b = 128 * h, 128 * h + 128
-            if stage == 0:
-                scan(v("mx", a + 1, b + 1), v("cm", a, b), v("pc", 512 * h, 512 * h + 128), 0.0, A.add, A.max)
-            if stage == 1:
-                tt(v("em", a, b), v("pc", 512 * h, 512 * h + 128), v("mx", a, b), A.is_le)
+    ms(v("vv", 256, 544, 272), 0.0)
+    ms(col("j1", J1 + SENT), float(SENT))
+    for lo in (0, 272, 544):
+        ms(v("jj", lo, lo + 16), float(SENT))
+    ts(v("v32", 0, 16), v("blk", 0, 16), pp("i"), A.is_equal, 64.0, A.mult)
+    ts(v("v32", 16, 32), v("blk", 0, 16), pp("i"), A.is_equal, 128.0, A.mult)
+    lin(v("vv", 0, 256), ind(v("v32"), v("vo")), 1.0, 1.0)
+    cp(v("vc", 0, 256), v("vv", 0, 256))
+    tt(s(NR), v("pari"), v("jl"), A.not_equal)
+    ts(s(W), v("pari"), -1.0, A.mult, float(SENT), A.add)
+    tt(s(W + 1), s(NR), s(W), A.mult)
+    ts(jo(0), s(W + 1), -1.0, A.mult, float(SENT), A.add)
+    act(v("j1", J1, J1 + 128), ind(v("iota", 0, 257), v("jo", 0, 8)), F.Copy)
+    cp(v("j1", J1 + 128, J1 + 256), ind(v("iota", 0, 257), v("jo", 8, 16)))
+    jw, ja, va = v("j1", J1, J1 + 257), JA, 0
+    for m, radix in enumerate(RADIX):
+        last = m == len(RADIX) - 1
+        if m:
+            two_turns("jj", JA + JB - ja)
+            cp(jo(m), ind(v("tt"), ku("jo")))
+            lin(v("vc", 256 * m, 256 * m + 256), v("vv", va, va + 256), 1.0, 0.0)
+        if last:
+            lin(v("vc", 768, 1024), v("vv", va, va + 256), 1.0, -96.5)
+        for k in range(1, radix):
+            if not last:
+                act(v("jj", ja, ja + 256), ind(jw, jo(m)), F.Copy)
+                jw, ja = v("jj", ja, ja + 257), JA + JB - ja
+            end = last and k == radix - 1
+            c = 768 if end else 256 * m
+            tt(v("wa", VV, VV + 256) if end else v("vv", 272 - va, 528 - va), ind(v("vv", va, va + 257), jo(m)), v("vc", c, c + 256), A.add)
+            va = 272 - va
 
-    def unpack_x(t):
-        arrived("qx%d" % t, 2 * ne[t], v("lq%d" % t, 0, 256), v("ls%d" % t, 0, 256))
+    def quant_x(t, h):
+        qz(v("xq%d" % t, 128 * h, 128 * h + 128), v("xs%d" % t, 128 * h, 128 * h + 128), v("xb%d" % t, 512 * h, 512 * h + 512))
+
+    def share_x(t):
+        sent = [send(partner[t], v("ls%d" % t, 0, 256), v("xs%d" % t), False, "qx%d" % t, 300.0, 0.0 if t else 1500.0),
+                send(partner[t], v("lq%d" % t, 0, 256), v("xq%d" % t), True, "qx%d" % t, 1800.0)]
+        arrived("qx%d" % t, 2 * ne[t], sent, v("lq%d" % t, 0, 256), v("ls%d" % t, 0, 256))
         for b in range(4):
             mm(v("pa", 512 * b, 512 * b + 256), v("eq", 128 * b, 128 * b + 128), v("es", 128 * b, 128 * b + 128),
                v("lq%d" % t, 0, 256), v("ls%d" % t, 0, 256))
-        for b in range(4):
-            act(v("dp", 272 * b, 272 * b + 256), v("pa", 512 * b, 512 * b + 256), F.Copy)
+            act(v("dp", DX + 272 * b, DX + 272 * b + 256), v("pa", 512 * b, 512 * b + 256), F.Copy)
 
-    DJ, OFF, Y, BD, ZE = 10, 11, 12, 13, 25
-    en_s, en_e = v("en", 0, 16), v("en", 2, 18)
+    def best(t):
+        for h in range(2):
+            a, b, ps = 128 * h, 128 * h + 128, v("pc", 512 * h, 512 * h + 128)
+            mm(ps, v("up", 128 * t, 128 * t + 128), v("ups", 128 * t, 128 * t + 128), v("xq%d" % t, a, b), v("xs%d" % t, a, b))
+            scan(v("mx", 136 * h + 1, 136 * h + 129), v("cm"), ps, 0.0, A.add, A.max)
+            tt(v("em", a, b), ps, v("mx", 136 * h, 136 * h + 128), A.is_le)
+            scan(v("ct", a, b), v("em", a, b), v("dm"), 0.0, A.mult, A.add)
+            ts(v("offs", h, 8, 2), v("base", h, 8, 2), col("ct", b - 1), A.subtract)
 
-    tt(s(0), v("pari"), v("jl"), A.not_equal)
-    ts(s(1), v("pari"), -1.0, A.mult, float(SENT), A.add)
-    ts(kf(12), kf(S1), 16.0, A.mult, kf(C1), A.add)
-    quant_e(0)
-    tt(s(2), s(0), s(1), A.mult)
-    quant_e(1)
-    ts(v("jo", 0, 16), s(2), -1.0, A.mult, float(SENT), A.add)
-    ts(col("jo", 16), col("s", 32), -1.0, A.mult, float(SENT), A.add)
-    cp(v("vc"), v("va", 0, 272))
-    ts(col("ku", 0), kf(12), kf(E_), A.add)
-    quant_e(2)
-    act(v("win", 0, 272), ind(v("iota"), jo(0)), F.Copy)
-    act(v("jb", 0, 272), ind(v("win", 0, 288), jo(0)), F.Copy)
-    tt(v("vb", 0, 272), ind(v("va"), jo(0)), v("vc"), A.add)
-    act(v("vc"), v("vb", 0, 272), F.Copy)
-    lin(v("cm"), v("cm1"), BIG, -192.0 * BIG)
-    act(v("dm1"), v("iota", 0, 256), F.Abs, bias=kf(22))
-    quant_e(3)
-    quant_x(0)
-    send_x(0)
-    js, vs = ["jb", "ja"], ["va", "vb"]
-    for m in range(1, 5):
-        tr(v("tt", 0, 256), v(js[(m - 1) % 2], 0, 256))
-        tr(v("tt", 256, 512), v(js[(m - 1) % 2], 16, 272))
-        if m == 1:
-            qz(v("uq"), v("us"), v("ut"))
-        if m == 2:
-            pick_q(1)
-        if m == 3:
-            best(1, (0,))
-        if m == 4:
-            best(2)
-            cp(v("kb"), v("kbi"))
-        cp(v("jo", 32 * m, 32 * m + 32), ind(v("tt"), v("ku", 0, 2)))
-        if m == 1:
-            pick_q(0)
-        if m == 2:
-            best(0, (0,))
-        if m == 3:
-            best(1, (1,))
-        if m == 4:
-            ts(v("offs", 6, 8), v("base", 6, 8), col("ct", 255), A.subtract)
-            cp(col("ku", 2), kf(16))
-        if m < 4:
-            act(v(js[m % 2], 0, 272), ind(v(js[(m - 1) % 2]), jo(m)), F.Copy)
-            tt(v(vs[(m + 1) % 2], 0, 272), ind(v(vs[m % 2]), jo(m)), v("vc"), A.add)
-            if m == 1:
-                pick_s(0)
-            act(v("vc"), v(vs[(m + 1) % 2], 0, 272), F.Copy)
-        else:
-            tt(v("wa", VV, VV + 272), ind(v(vs[m % 2]), jo(m)), v("vc"), A.add)
-        if m == 1:
-            scores(0)
-        if m == 2:
-            lin(kf(14), kf(K_), 16.0, 32.0)
-            lin(kf(15), kf(H_), -1.0, 1.0)
-            lin(kf(13), kf(B1), 16.0, kf(E_))
-            best(0, (1,))
-        if m == 3:
-            lin(col("base", 6), kf(14), 1.0, float(VV - ZZ))
-            lin(col("base", 7), kf(14), kf(15), float(VV - ZZ))
-            lin(kf(16), kf(H_), 64.0, kf(13))
-            fill(v("wa", ZZ, VV), 0.0)
-            lin(v("dmp"), v("jl"), 1.0, float(SENT))
-            fill(s(ZE), 0.0)
-            fill(v("en", 0, 2), kf(E_))
-            fill(v("win", 256, 352), 256.0)
-            fill(v("win", 352, 568), 0.0)
-            fill(v("win", 568, 784), 0.0)
-            for b in range(4):
-                fill(v("dp", 272 * b + 256, 272 * b + 272), 0.0)
-            ts(v("dm"), v("dm1"), 16.0, A.is_lt)
-            lin(kf(17), kf(E_), 1.0, 64.0)
-            lin(kf(18), kf(E_), -1.0, 1024.0)
-            fill(v("wim", 0, 96), 0.0)
-            fill(sh(37, 1), 0.0)
-            fill(v("pt", 256, 512), 0.0)
-            fill(v("ht", 256, 512), 0.0)
-    unpack_x(0)
-
-    def places(t):
-        if t == 0:
-            cp(v("gi", 0, 32), ind(v("wa", ZZ, VV + 272), v("offs", 6, 8)))
-            tr(v("tt", 0, 256), v("wa", VV, VV + 256))
-            tr(v("tt", 256, 512), v("wa", VV + 16, VV + 272))
-            ts(v("mi", 16, 32), v("gi", 16, 32), 63, A.bitwise_and)
-            ts(v("mi", 0, 16, 2), v("gi", 0, 16, 2), 64, A.bitwise_and)
-            ts(v("mi", 1, 16, 2), v("gi", 1, 16, 2), 128, A.bitwise_and)
-            cp(v("gi", 32, 48), ind(v("tt"), col("ku", 0)))
-            cp(s(9), v("mi", 16, 32))
-            ts(s(OFF), v("mi", 0, 16), 0.0, A.is_equal)
-            ts(s(30), v("mi", 0, 16), 0.0, A.not_equal)
-            ts(v("mi", 32, 48), v("gi", 32, 48), 63, A.bitwise_and)
-            scan(en_e, s(9), s(ZE), kf(E_), A.add, A.add)
-            tt(s(1), s(OFF), v("dmp"), A.mult)
-            ts(v("mi", 48, 64), v("gi", 0, 16), 63, A.bitwise_and)
-            tt(s(2), en_e, v("mi", 32, 48), A.subtract)
-            cp(s(DJ), v("mi", 32, 48))
-            cp(v("lo"), v("mi", 32, 48))
-        else:
-            ts(v("offs", 0, 6), v("base", 0, 6), col("ct", 255), A.subtract)
-            tt(s(6, 2), ind(v("wa", 0, VV), v("offs", 2, 4)), v("cin", 32, 64), A.add)
-            tt(s(4, 2), ind(v("wa", 0, VV), v("offs", 0, 2)), v("cin", 0, 32), A.mult)
-            if t < R - 1:
-                cp(s(28, 2), ind(v("wa", 0, NL), v("offs", 4, 6)))
-            scan(s(8), s(6), s(7), kf(E_), A.add, A.add)
-            tt(s(OFF), s(6), s(4), A.is_lt)
-            if t < R - 1:
-                ts(s(30), s(28), 0.0, A.is_gt)
-            tt(s(2), s(8), s(5), A.add)
-            tt(s(1), s(OFF), v("dmp"), A.mult)
-            for h in range(2):
-                tt(v("en", 2 + h, 18, 2), sh(8, 1), v("k0", 9, 24, 2), A.add)
-        tt(s(Y), s(2), s(1), A.max)
-        if t < R - 1:
-            tt(v("cin", 32, 48), s(30), s(DJ), A.mult)
-        ts(s(40), en_e, kf(17), A.min, -1.0, A.add)
+    def places_first():
+        vw = v("wa", VV, VV + 256)
+        two_turns("wa", VV)
+        ts(v("gi", 32, 48), ind(v("tt"), ku("jo")), 96.5, A.add)
+        ts(v("mi", 16, 32), v("gi", 32, 48), 63, A.bitwise_and)
+        ts(w32(GA), ind(vw, LB), 32.5, A.add)
+        ts(w32(GC), ind(vw, LB), M64, A.add, M64, A.subtract)
+        scan(ends, w32(GA, 0, 32, 4), w32(GC, 0, 32, 4), pp("e16"), A.add, A.subtract)
+        ts(v("gi", 0, 32), ind(vw, LB), 96.5, A.add, 16.0, A.mult)
+        for h in range(2):
+            ts(v("mi", h, 16, 2), v("gi", h, 32, 4), 1024 << h, A.bitwise_and)
+        tt(s(S2), ind(v("en"), ku("r16")), v("mi", 16, 32), A.subtract)
+        tt(s(OFF), v("dmp"), v("mi", 0, 16), A.subtract)
+        tt(s(Y), s(S2), s(OFF), A.max)
         cp(v("so"), s(Y))
-        ts(s(41), s(Y), kf(17), A.is_ge)
-        tt(s(42), en_s, s(Y), A.subtract)
-        scat(v("win", 256, 784), v("so"), v("iota", 0, 256))
-        tt(s(3), s(40), s(42), A.add)
-        tt(s(43), s(41), v("dmp"), A.mult)
-        tr(v("ts", 0, 64), v("win", 256, 320))
-        tr(v("ts", 64, 128), v("win", 272, 336))
-        tt(s(45), s(3), s(43), A.max)
-        ts(s(33), s(Y), -1.0, A.add)
-        cp(v("sl%d" % t), ind(v("ts"), col("ku", 2)))
-        send(partner[t], v("ll%d" % t), v("sl%d" % t, 0, 4), False, "li%d" % t)
+        cp(s(DJ), v("mi", 16, 32))
+        for h in range(2):
+            w8 = v("s", 16 * (W + 11) + 8 * h, 16 * (W + 11) + 8 * h + 8)
+            lin(w32(D1, 1 + h, 32, 4), sh(DJ, h), 1.0, 0.0)
+            lin(w8, sh(DJ, h), -512.0 * 256, 0.0)
+            tt(w32(S1, 2 + h, 32, 4), w8, v("kk"), A.add)
+        lin(w32(D5), w32(D1), 512.0, 0.0)
+        act(v("ub", 0, 256), vw, F.Abs, bias=-32.0)
+        act(v("ub", 256, 512), v("ub", 0, 256), F.Abs, bias=-64.0)
+        act(v("wa", DP, DP + 256), v("ub", 256, 512), F.Abs, bias=-32.0)
+        ts(v("wa", T0, T0 + 256), v("ub", 256, 512), 32.0, A.is_gt, 2048.0, A.mult)
+        ts(v("wa", T1, T1 + 256), vw, 0.0, A.is_lt, 2048.0, A.mult)
 
-    def tables_a():
-        act(v("un", 0, 256), v("wa", VV, VV + 256), F.Abs, bias=-128.5)
-        act(v("wa", A1, A1 + 256), v("wa", VV, VV + 256), F.Sign, bias=-128.5)
-        act(v("un", 256, 512), v("un", 0, 256), F.Abs, bias=-64.0)
-        fill(v("rs", 0, 256), 1.0)
-        act(v("wa", A0, A0 + 256), v("un", 256, 512), F.Sign, bias=32.0, scale=-1.0)
-        fill(v("rs", 256, 512), 1.0)
-        act(v("wa", DP, DP + 256), ind(v("iota"), v("lo")), F.Copy)
-        fill(v("rs", 0, 512, 16), 0.0)
-        for b in range(4):
-            lin(v("j4", 16 * b, 16 * b + 16), v("jl"), 4.0, float(b))
-        fill(col("k0", 7), 0.0)
+    def places_later():
+        tt(w32(GA), ind(v("wa", 0, LS + 256), LA), w32(CA), A.mult)
+        tt(w32(GC), ind(v("wa", 0, LS + 256), LC), w32(CC), A.add)
+        scan(v("en", 4, 36), w32(GA), w32(CD), pp("e16"), A.add, A.add)
+        tt(w32(BB, 0, 30), w32(GC, 0, 30), w32(GC, 2, 32), A.max)
+        tt(w32(YY, 0, 30), v("en", 5, 35), w32(BB, 0, 30), A.max)
+        cp(v("so"), ind(w32(YY, 0, 30), ku("y16")))
+        cp(s(Y), ind(w32(YY, 0, 30), ku("y16")))
 
-    def tables_c():
-        lin(kf(19), kf(14), 1.0, float(DP - VV))
-        lin(col("base", 0), kf(H_), 256.0, kf(14))
-        lin(col("base", 1), kf(14), 1.0, float(NL))
-        lin(col("base", 2), kf(14), 1.0, float(NL))
-        lin(col("base", 4), kf(H_), 256.0, kf(14))
-        lin(col("base", 5), kf(14), 1.0, float(DP))
-        lin(col("base", 3), kf(19), kf(15), float(VV))
+    def slots(t):
+        iota(v("win", 0, 96), [[0, 96]], SENT)
+        scat(v("win"), v("so"), v("iota", 0, 256))
+        tr(v("ts", 0, 64), v("win", 0, 64))
+        tr(v("ts", 64, 128), v("win", 16, 80))
+        cp(v("sl%d" % t), ind(v("ts"), ku("sl")))
+        return send(partner[t], v("ll%d" % t), v("sl%d" % t, 0, 4), False, "li%d" % t, 0.0)
 
-    def mirror_a(t):
-        cp(v("mo"), s(45))
-        ts(s(44), s(41), -4096.0, A.mult, kf(18), A.add)
-        tt(s(35), s(33), en_s, A.max)
-        ts(s(34), s(OFF), (-527.0, 257.0)[t % 2], A.mult, (256.0, 0.0)[t % 2], A.add)
-        scat(v("wim"), v("mo"), v("io4"))
-        tt(s(26), s(3), s(44), A.add)
-        tt(s(36), s(35), s(34), A.add)
-
-    def mirror_b(t):
-        tr(v("tm", 0, 64), v("wim", 0, 64))
-        tr(v("tm", 64, 128), v("wim", 16, 80))
-        tt(s(16, 4), ind(s(26), v("ku", 4, 8)), v("c64"), A.add)
-        tt(s(0), ind(v("tm"), col("ku", 2)), v("kc"), A.add)
-
-    def mirror_c(t):
-        cp(v("xo"), s(0))
-        cp(v("po"), s(36))
+    def homes(t):
+        w8 = v("s", 16 * (W + 2), 16 * (W + 2) + 8)
+        ts(w8, ends, kf(CAP), A.min, kf(C1), A.subtract)
+        tt(v("sg", 7, 39, 4), starts, w8, A.add)
+        tt(v("ds", 3, 35, 4), v("sg", 7, 39, 4), v("sg", 11, 40, 4), A.subtract)
+        tt(s(EM, 2), ind(v("en"), ku("r32", 2)), v("cn"), A.is_gt)
+        tt(s(DD, 2), ind(v("ds"), ku("r32", 2)), v("cd"), A.add)
+        scan(s(SC, 2), s(EM, 2), s(DD, 2), 0.0, A.mult, A.add)
+        ts(v("mo"), ind(s(SC, 2), ku("mo")), pp("e16"), A.max)
+        act(v("wm"), ind(v("win", 0, 96), v("mo", 0, 8)), F.Identity, scale=4.0)
+        tr(v("tm"), v("wm"))
+        tt(s(W + 3), ind(v("tm"), ku("xm")), v("kc"), A.add)
+        cp(v("xo"), s(W + 3))
         for b in range(4):
             act(v("xg", 64 * b, 64 * b + 64), ind(v("xb%d" % t, 0, 1024), v("xo", 4 * b, 4 * b + 4)), F.Copy)
+        ts(s(W + 4), s(Y), kf(CAP), A.is_ge, -4096.0, A.mult)
+        tt(s(S3), ind(v("sg"), ku("r16")), s(Y), A.subtract)
+        tt(s(S26), s(S3), s(W + 4), A.add)
+        tt(s(HA, 4), ind(s(S26), v("ku", 32, 36)), v("c64"), A.add)
+        tt(s(HB, 4), s(HA, 4), v("j4"), A.max)
+        cp(v("ho"), s(HB, 4))
 
-    def parents_b(t):
-        if t % 2 == 0:
-            act(v("win", 784, 1040) if t == 0 else v("opf"), ind(v("win", 0, 784), v("po")), F.Copy)
-        else:
-            act(v("win", 0, 256), ind(v("win", 256, 1040), v("po")), F.Copy)
+    def flags(unit):
+        cp(w32(GF), ind(v("wa", 0, LS), LF))
+        ts(w32(PW, -1, 31), w32(GF), 0.0, A.is_equal, unit, A.mult)
 
-    def prep_a(t):
-        bd = v("cin", 32, 48)
-        for h in range(2):
-            tt(v("un", 256 * h, 256 * h + 256), ind(bd, v("kb", 16 * h, 16 * h + 16)), v("wa", 256 * h, 256 * h + 256), A.mult)
-        tt(s(20, 4), s(16, 4), v("j4"), A.max)
-        ts(s(32), bd, -2.0, A.mult, 1.0, A.add)
-        tt(s(31), s(29) if t else v("mi", 48, 64), s(DJ), A.add)
-        tr(v("tt"), v("un"))
-        ts(sh(37, 0), sh(29, 0) if t else v("mi", 48, 64, 2), 1.0, A.add)
-        tt(v("k0", 8, 24), s(31), s(32), A.add)
-        cp(v("ho"), s(20, 4))
-        scan(v("un"), v("rs"), v("tt"), 0.0, A.mult, A.max)
-        tt(s(BD), s(37), bd, A.subtract)
-        tt(s(38), v("k0", 7, 23), v("k0", 8, 24), A.subtract)
-        tt(s(39), v("un", 15, 256, 16), v("un", 271, 512, 16), A.max)
-        tt(v("cin", 48, 64), s(38), s(BD), A.add)
+    def far_end():
+        flags(1.0 / 256)
+        tt(w32(B2), w32(PW, -1, 31), w32(D5), A.mult)
+        for k, lo in enumerate((T0, T1)):
+            tt(v("un", 256 * k, 256 * k + 256), ind(w32(B2), v("kb", 16 * k, 16 * k + 16)), v("wa", lo, lo + 256), A.subtract)
+            tr(v("tu", 256 * k, 256 * k + 256), v("un", 256 * k, 256 * k + 256))
+            scan(v("un", 256 * k, 256 * k + 256), v("rs"), v("tu", 256 * k, 256 * k + 256), 0.0, A.min, A.max)
+        tt(s(LM), v("un", 15, 256, 16), v("un", 271, 512, 16), A.max)
+        act(v("lw"), ind(s(LM), v("kb", 32, 48)), F.Identity, scale=256.0)
+        tr(v("wa", LS, LS + 256), v("lw"))
+        tt(w32(CA), w32(PW, -2, 30), w32(PW, -1, 31), A.subtract)
+        fill(w32(CA, 0, 32, 4), -1.0)
+        tt(w32(KK), w32(B2), w32(D1), A.subtract)
+        lin(w32(KK, 3, 32, 4), w32(GF, 0, 32, 4), -1.0, 33.5)
+        tt(w32(CD), w32(KK), w32(KK, -1, 31), A.subtract)
+        fill(w32(CD, 0, 32, 4), 32.5)
+        tt(w32(BB), ind(anc, ku("pc", 2)), w32(S1), A.mult)
+        tt(w32(CC), w32(BB), w32(S0), A.add)
 
-    def prep_b():
-        act(v("tt", 0, 256), ind(s(39), v("kb", 32, 48)), F.Identity, scale=-1.0)
-        lin(v("cin", 0, 16), s(30), 64.0, -64.0)
-        lin(v("cin", 16, 32, 2), sh(30, 0), 2.0, -1.0)
-        lin(v("cin", 17, 32, 2), sh(30, 1), 2.0, -2.0)
+    def parents():
+        flags(1.0)
+        tt(s(W + 6), ind(anc, ku("y16")), s(NR), A.mult)
+        tt(s(W + 7), v("dmp"), v("pari"), A.subtract)
+        tt(s(W + 8), s(W + 6), s(W + 7), A.mult)
+        tt(s(W + 9), v("dmp"), s(W + 8), A.subtract)
+        cp(v("po"), s(W + 9))
+        scat(v("j1", J1, J1 + 800), v("po"), v("iota", 0, 256))
+        cp(w32(KK), ind(v("iota", 0, 256), LB))
+        scat(v("j1", 0, 1024), LF, w32(KK))
+        dma("S", T.op[:], T.j1[0:128:16, J1:J1 + 256], "dout", 0.0, reads=[v("j1", J1, J1 + 256)])
 
-    def layer(t):
-        arrived("li%d" % t, ne[t], v("ll%d" % t))
-        o = v("ll%d" % t)
+    def layer(t, sent):
+        arrived("li%d" % t, ne[t], [sent], v("ll%d" % t))
         for b in range(4):
-            w = ind(v("dp", 272 * b, 272 * b + 272), o)
+            w = ind(v("dp", DX + 272 * b, DX + 272 * b + 257), v("ll%d" % t))
             if b % 2:
-                act(v("pt", b, 256, 4), w, F.Copy)
+                act(v("dp", PT + b, PT + 256, 4), w, F.Copy)
             else:
-                cp(v("pt", b, 256, 4), w)
+                cp(v("dp", PT + b, PT + 256, 4), w)
         pq, ps = v("hq%d" % t, 128, 256), v("hs%d" % t, 128, 256)
-        qz(pq, ps, v("pt"))
+        qz(pq, ps, v("dp", PT, PT + 512))
         for b in range(4):
             mm(v("pc", 512 * b, 512 * b + 128), v("wq", 128 * b, 128 * b + 128), v("wss", 128 * b, 128 * b + 128), pq, ps)
-        mirror_b(t)
-        for b in range(4):
             if b % 2:
-                ts(v("ht", b, 256, 4), v("pc", 512 * b, 512 * b + 64), 0.0, A.max, 0.03125, A.mult)
+                ts(v("dp", HT + b, HT + 256, 4), v("pc", 512 * b, 512 * b + 64), 0.0, A.max, 0.03125, A.mult)
             else:
-                act(v("ht", b, 256, 4), v("pc", 512 * b, 512 * b + 64), F.Relu, scale=0.03125)
-        qz(v("hq%d" % t, 0, 128), v("hs%d" % t, 0, 128), v("ht"))
-        send2(partner[t], v("lq%d" % t, 256, 320), v("hq%d" % t, 0, 64), v("ls%d" % t, 256, 512), v("hs%d" % t), "hh%d" % t)
+                act(v("dp", HT + b, HT + 256, 4), v("pc", 512 * b, 512 * b + 64), F.Relu, scale=0.03125)
+        qz(v("hq%d" % t, 0, 128), v("hs%d" % t, 0, 128), v("dp", HT, HT + 512))
+        return send2(partner[t], v("lq%d" % t, 256, 320), v("hq%d" % t, 0, 64), v("ls%d" % t, 256, 512), v("hs%d" % t), "hh%d" % t)
 
-    def update(t):
-        arrived("hh%d" % t, ne[t], v("lq%d" % t, 256, 320), v("ls%d" % t, 256, 512))
+    def update(t, sent):
+        arrived("hh%d" % t, ne[t], [sent], v("lq%d" % t, 256, 320), v("ls%d" % t, 256, 512))
         xb, xn = "xb%d" % t, "xb%d" % (t + 1)
         for b in range(4):
             mm(v("pa", 512 * b, 512 * b + 128), v("eq", 128 * b, 128 * b + 128), v("es", 128 * b, 128 * b + 128),
                v("lq%d" % t, 192, 320), v("ls%d" % t, 192, 320))
-        for b in range(4):
             tt(v(xb, 1024 + 64 * b, 1088 + 64 * b), v("pa", 512 * b + 64, 512 * b + 128), v("xg", 64 * b, 64 * b + 64), A.add)
-        for b in range(4):
-            w = ind(v(xb, 0, 1088 + 64 * b), v("ho", 16 * b, 16 * b + 16))
-            if b < 2:
-                act(v(xn, b, 1024, 4), w, F.Copy)
+        for e, b, lo, hi in PARTS:
+            w = ind(v(xb, 0, 1088 + 64 * b), v("ho", 16 * b + lo, 16 * b + hi))
+            out = v(xn, 64 * lo + b, 64 * hi, 4)
+            if e == "A":
+                act(out, w, F.Copy)
             else:
-                cp(v(xn, b, 1024, 4), w)
-        quant_x(t + 1)
+                cp(out, w)
+        for h in range(2):
+            quant_x(t + 1, h)
 
+    quant_x(0, 0)
+    quant_x(0, 1)
     for t in range(R):
-        if t:
-            send_x(t)
-            scores(t)
-            unpack_x(t)
-            if t == 1:
-                pick_q(2)
-            best(0)
-            tr(v("wa", NL, NL + 256), v("tt", 0, 256))
-            best(1)
-            best(2)
-        places(t)
+        share_x(t)
+        best(t)
         if t == 0:
-            tables_a()
-        mirror_a(t)
-        layer(t)
-        mirror_c(t)
-        if t < R - 1:
-            pick_s(t + 1)
-            prep_a(t)
+            places_first()
         else:
-            tt(s(20, 4), s(16, 4), v("j4"), A.max)
-            qz(v("vq"), v("vs"), v("vt"))
-            cp(v("ho"), s(20, 4))
-            parents_b(t)
-            dma("S", T.op[:], T.opf[0:128:16, :], "dout", reads=[v("opf")])
-        update(t)
+            places_later()
+        sent = slots(t)
+        homes(t)
         if t < R - 1:
-            prep_b()
-            if t == 0:
-                tables_c()
-            parents_b(t)
-            fill(v("win", 256, 352), 256.0)
+            far_end()
+        else:
+            parents()
+        update(t, layer(t, sent))
 
     for h in range(2):
-        mm(v("pc", 512 * h, 512 * h + 128), v("vq"), v("vs"), v("xq3", 128 * h, 128 * h + 128), v("xs3", 128 * h, 128 * h + 128))
-    dma("S", T.oc[:], T.xq3[:].bitcast(dt.uint8), "dout", reads=[v("xq3")])
+        a, b = 128 * h, 128 * h + 128
+        mm(v("pc", 512 * h, 512 * h + 128), v("vq"), v("vs"), v("xq3", a, b), v("xs3", a, b))
+        dma("S", T.oc[:, 4 * a:4 * b], T.xq3[:, a:b].bitcast(dt.uint8), "dout", 300.0, reads=[v("xq3", a, b)])
+        cp(v("yf", a, b), v("pc", 512 * h, 512 * h + 128))
+    dma("S", T.y[:], T.yf[:], "dout", 500.0, reads=[v("yf")])
     for k in range(4):
-        dma("A", T.osc[4 * k:4 * k + 4, :], T.xs3[32 * k:32 * k + 4, :], "dout", reads=[v("xs3")])
-    for h in range(2):
-        cp(v("yf", 128 * h, 128 * h + 128), v("pc", 512 * h, 512 * h + 128))
-    dma("S", T.y[:], T.yf[:], "dout", reads=[v("yf")])
-    for sem in sorted(total, key=lambda x: x == "dout"):
-        wait("S", (sem, total[sem], {}))
+        dma("A", T.osc[4 * k:4 * k + 4, :], T.xs3[32 * k:32 * k + 4, :], "dout", 0.0, reads=[v("xs3")])
+    emit()

@@ -6,16 +6,16 @@ F = ActivationFunctionType
 R = 3
 STEP = [1, 2, 3]
 BF, F32, I32, U16, U8, X4 = "bfloat16", "float32", "int32", "uint16", "uint8", "float8_e4m3fn_x4"
-SENT = 256
+SENT = 257
 DUMP = 544
 BIG = 2.0 ** 90
-M64 = 1.5 * 2.0 ** 29
-DP, T0, T1, ZZ, LS, VV = 0, 256, 512, 768, 1024, 1296
+M64 = 12288.0
+DP, T0, T1, ZZ, LS, VV = 0, 256, 512, 768, 1024, 1280
 HT, PT, DX = 0, 256, 512
-JA, JB, J1 = 16, 288, 256
-BLOCKS = [("i", 0, [[0, 2], [1, 16]]), ("jo", None, None), ("k32", 0, [[0, 2], [32, 4], [0, 4]]),
-          ("la", None, None), ("lc", None, None), ("lf", 0, [[0, 8], [256, 4]]),
-          ("e16", 0, [[16, 2], [0, 16]]), ("sl", 0, [[4, 8], [32, 2], [64, 2]]), ("r16", 7, [[0, 2], [4, 8], [0, 2]]),
+JA, JB, J1 = 0, 272, 256
+BLOCKS = [("i", 0, [[0, 2], [1, 16]]), ("k32", 0, [[0, 2], [32, 4], [0, 4]]),
+          ("la", None, None), ("lc", None, None), ("lf", 0, [[0, 8], [256, 4]]), ("r16", 7, [[0, 2], [4, 8], [0, 2]]),
+          ("q2", 0, [[0, 2], [1, 8], [0, 2]]), ("odd", 0, [[0, 16], [544, 2]]),
           ("xm", 0, [[4, 8], [32, 4]]), ("r32", 3, [[0, 4], [4, 8]]), ("mo", 7, [[0, 4], [8, 4], [0, 2]]),
           ("y16", 0, [[0, 2], [4, 8], [1, 2]]), ("pc", None, None)]
 BL = {_b[0]: _k for _k, _b in enumerate(BLOCKS)}
@@ -34,23 +34,23 @@ for _t in range(R + 1):
 for _t in range(R):
     _sb("lq%d" % _t, 320, X4)
     _sb("ls%d" % _t, 512, U8)
-    _sb("ll%d" % _t, 4, U16)
-    _sb("sl%d" % _t, 16, U16)
+    _sb("ll%d" % _t, 8, U16)
+    _sb("sl%d" % _t, 8, U16)
     _sb("hq%d" % _t, 256, X4)
     _sb("hs%d" % _t, 256, U8)
 for _n, _c, _d in [
     ("ut", 512, BF), ("vt", 512, BF), ("uq", 128, X4), ("us", 128, U8), ("vq", 128, X4), ("vs", 128, U8),
     ("up", 384, X4), ("ups", 384, U8), ("wq", 512, X4), ("wss", 512, U8), ("eq", 512, X4), ("es", 512, U8),
-    ("ez", 520, BF), ("pari", 16, I32), ("iota", 272, BF), ("ki", 96, I32), ("kf", 8, F32), ("c16", 16, F32),
-    ("blk", 32 * len(BLOCKS), BF), ("blt", 32 * len(BLOCKS) + 32, BF), ("ku", 40, U16), ("pk", 24, U16), ("kb", 48, U16),
+    ("ez", 520, BF), ("pari", 16, I32), ("iota", 264, F32), ("ki", 96, I32), ("kf", 8, F32), ("c16", 16, F32),
+    ("blk", 32 * len(BLOCKS), BF), ("blt", 32 * len(BLOCKS), BF), ("ku", 40, U16), ("pk", 24, U16), ("kb", 48, U16),
     ("jl", 16, F32), ("dmp", 16, F32), ("j4", 64, F32), ("c64", 64, F32), ("base", 8, F32), ("kc", 16, F32), ("kk", 8, F32),
     ("cn", 32, F32), ("cd", 32, F32), ("cm", 128, BF), ("cm1", 128, BF), ("dm", 128, BF),
     ("mx", 272, F32), ("em", 256, BF), ("ct", 256, BF),
-    ("jj", 560, BF), ("j1", 1056, F32), ("jo", 80, U16), ("tt", 544, BF),
-    ("vv", 544, BF), ("vc", 1024, BF), ("v32", 32, BF), ("vo", 16, U16), ("wa", VV + 272, BF),
+    ("jj", 544, BF), ("j1", 1056, F32), ("jo", 48, U16), ("m32", 96, BF), ("dg", 256, BF), ("dgo", 256, BF), ("gq", 32, BF), ("m8", 256, BF),
+    ("vv", 544, BF), ("vc", 768, BF), ("v32", 32, BF), ("vo", 16, U16), ("wa", VV + 256, BF),
     ("un", 512, BF), ("rs", 256, BF), ("tu", 512, BF), ("ub", 512, BF), ("lw", 256, BF),
     ("offs", 8, U16), ("gi", 48, I32), ("mi", 32, I32), ("s", 1088, F32), ("en", 40, F32), ("sg", 40, F32), ("ds", 40, F32),
-    ("so", 16, U16), ("win", 512 * 31 + 16, BF), ("ts", 128, BF), ("wm", 128, BF), ("tm", 128, BF), ("mo", 16, U16), ("xo", 16, U16),
+    ("so", 16, U16), ("win", 512 * 31 + 16, BF), ("wm", 128, BF), ("tm", 128, BF), ("mo", 16, U16), ("xo", 16, U16),
     ("ho", 64, U16), ("po", 16, U16),
     ("dp", DX + 1088, BF), ("xg", 256, BF), ("yf", 256, F32),
 ]:
@@ -61,21 +61,22 @@ SCRATCH["pc"] = ("psum", [128, 2048], F32)
 SEMAPHORES = ["sV", "sA", "sP", "sG", "dpar", "dx", "du", "dv", "dw", "dws", "dout", "loc"] + \
              ["%s%d" % (_k, _t) for _k in ("qx", "li", "hh") for _t in range(R)]
 
-CYC, WAKE, HOP, LOAD = 1.0, 150.0, 700.0, 900.0
+CYC, WAKE, HOP, LOAD = 1.0, 150.0, 500.0, 900.0
 GATHER, SCATTER, PE = 1.3, 3.2, 0.8
 SLACK = 150.0
 RADIX = (3, 3, 4)
 FIRST = [
-    "pari:0 xb0:0 ut:0",
-    "blk:i c16:0 ki:0 iota:0 kf:0 blk:jo blk:48 blk:k32 ki:16 blk:lf blk:e16 blk:sl blk:r16 base:0",
-    "blt:i jl:0 vo:0 v32:0 v32:16 ku:32 s:0 s:256 blt:448 s:272 ez:3 jo:0 vc:0 j1:384 vv:272 blt:jo pk:0 vv:0' xq0:0 uq:0 "
-    "xq0:128 ku:2 tt:0 tt:256 up:0 jo:16 up:64 vv:272' eq:0 vv:0'' mx:1 blt:la tt:0' tt:256' mx:137 jo:32 em:0 vv:272'' "
-    "em:128 base:0' vv:0''' ct:0 ct:128 wa:1296 offs:0 offs:1 tt:0'' tt:256'' gi:0 s:544 s:576 gi:32 ku:14",
-    "vv:0 j1:256 jj:16 kf:1 blk:lc jj:288 vc:256 blk:130 cm1:0 ups:0 ups:64 jj:16' cm:0 jj:288' vc:512 vc:768 kf:4 cm1:0' dm:0 "
-    "ups:128 ups:192 s:960 ub:0 ups:256 ups:320",
-    "wa:1296 eq:128 eq:256 eq:384", "wa:1296 blt:xm", "so:0 s:368", "so:0 up:128", "so:0 up:192", "so:0 up:256", "so:0 up:320", "so:0 vq:0",
+    "pari:0 ut:0 xb0:0",
+    "blk:i c16:0 ki:0 iota:0 blk:k32 ki:16 blk:lf blk:r16 kf:0 ez:0 blk:q2 blk:odd base:0 m8:0 win:0",
+    "blt:i v32:0 v32:16 vo:0 m32:1 m32:32 jl:0 kf:2 m32:64 s:0 s:256 ku:32 s:272 blt:k32 jo:0 vc:0 j1:384 vv:272 pk:0 uq:0 vv:0' "
+    "up:0 up:64 dgo:0 xq0:0 jo:16 xq0:128 vv:272' ez:3 vv:0'' mx:1 blt:la dgo:0' mx:137 m8:65 jo:32 em:0 m8:128 "
+    "vv:272'' em:128 base:0' vv:0''' ct:0 ct:128 kf:4 wa:1280 offs:0 offs:1 dgo:0'' gi:0 s:544 gq:0 gi:32",
+    "vv:0 dg:0 j1:256 jj:0 kf:1 blk:lc jj:272 vc:256 blk:98 cm1:0 ups:0 ups:64 jj:0' cm:0 jj:272' vc:512 kf:3 cm1:0' dm:0 "
+    "m8:64 en:0 dmp:0 sg:0 ds:0 cd:0 cn:0' s:864 s:960 s:1022 j4:0 j4:16 j4:32 j4:48 ups:128 ups:192 ub:0 ups:256 ups:320",
+    "wa:1280 m8:192 eq:0 eq:128 eq:256 eq:384", "wa:1280 blt:xm", "so:0 s:368", "so:0 up:128", "so:0 up:192", "so:0 up:256", "so:0 up:320", "so:0 vq:0",
 ]
 PARTS = [("A", 0, 0, 16), ("A", 2, 0, 16), ("A", 3, 12, 16), ("V", 1, 0, 16), ("V", 3, 0, 8), ("V", 3, 8, 12)]
+LAST = [("A", 0, 0, 8), ("A", 2, 0, 8), ("A", 0, 8, 16), ("A", 2, 8, 16), ("A", 3, 8, 16), ("V", 1, 0, 8), ("V", 3, 0, 8), ("V", 1, 8, 16)]
 _ORDER = []
 
 
@@ -329,8 +330,7 @@ def rank_program(g, core, T, topo):
     jo = lambda m: v("jo", 16 * m, 16 * m + 16)
     pp = lambda name: col("blt", 32 * BL[name])
     ku = lambda name, n=1: v("ku", 2 * BL[name], 2 * BL[name] + n)
-    c32 = col("blt", 32 * len(BLOCKS))
-    P_, CMB, CAP, C1, DMB = range(5)
+    P_, CMB, INV, DMB, IN8, ODD = range(6)
     NR, DJ, Y, OFF, S2, S3, S26, LM, HA, HB, W = 0, 1, 2, 3, 4, 5, 6, 7, 8, 12, 16
     EM, DD, SC, GA, GC, GF, BB, YY, B2, KK, CA, CC, CD, D1, D5, S1, S0, _, PW = range(28, 66, 2)
     ends, starts = v("en", 7, 39, 4), v("en", 3, 35, 4)
@@ -340,34 +340,31 @@ def rank_program(g, core, T, topo):
     anc = w32(PW, 0, 31)
     LA, LC, LF, LB = [v("offs", 2 * k, 2 * k + 2) for k in range(4)]
 
-    dma("S", T.pari[:], T.par[:], "dpar", 300.0, writes=[v("pari")], urge=3e6)
-    tx = dma("S", T.xb0[:, 0:1024], T.x[:], "dx", 2000.0, writes=[v("xb0", 0, 1024)], urge=2e6)
-    dma("S", T.ut[:], T.u[:], "du", 2500.0, writes=[v("ut")], urge=1e6)
-    dma("S", T.wq[:].bitcast(dt.uint8), T.wc[:], "dw", 2000.0, writes=[v("wq")], after=[tx])
+    dma("S", T.pari[:], T.par[:], "dpar", 300.0, writes=[v("pari")])
+    dma("S", T.ut[:], T.u[:], "du", 1200.0, writes=[v("ut")])
+    tx = dma("S", T.xb0[:, 0:1024], T.x[:], "dx", 2500.0, writes=[v("xb0", 0, 1024)])
+    tw = dma("S", T.wq[:].bitcast(dt.uint8), T.wc[:], "dw", 2000.0, writes=[v("wq")], after=[tx])
     dma("S", T.wss[:], T.ws[:], "dws", 2000.0, writes=[v("wss")], after=[tx])
-    dma("S", T.vt[:], T.v[:], "dv", 3000.0, writes=[v("vt")], after=[tx])
+    dma("S", T.vt[:], T.v[:], "dv", 3000.0, writes=[v("vt")], after=[tw])
 
     for k, (name, base, pat) in enumerate(BLOCKS):
         if pat is not None:
             iota(v("blk", 32 * k, 32 * k + 32), pat, base)
     blk = lambda name, lo=0, hi=32, step=1: v("blk", 32 * BL[name] + lo, 32 * BL[name] + hi, step)
-    iota(blk("jo", 0, 16), [[32, 8], [288, 2]])
-    iota(blk("jo", 16, 32), [[32, 8], [-256, 2]], 272)
     for lo in (0, 16):
         iota(blk("pc", lo, lo + 16), [[4, 4], [0, 2], [1, 2]])
     lin(blk("la"), blk("i"), 0.0, float(LS))
     lin(blk("la", 0, 32, 4), blk("i", 0, 8), 0.0, float(DP))
     lin(blk("lc"), blk("lf"), 1.0, float(T0))
     lin(blk("lc", 2, 32, 4), blk("i", 0, 8), 0.0, float(LS))
-    for a, b in (("i", "i"), ("jo", "k32"), ("la", "r16"), ("xm", "pc")):
+    for a, b in (("i", "i"), ("k32", "k32"), ("la", "odd"), ("xm", "pc")):
         tr(v("blt", 32 * BL[a], 32 * BL[b] + 32), v("blk", 32 * BL[a], 32 * BL[b] + 32))
-    for a, b in (("jo", "jo"), ("sl", "r16"), ("xm", "pc")):
+    for a, b in (("r16", "r16"), ("xm", "pc")):
         cp(v("ku", 2 * BL[a], 2 * BL[b] + 2), v("blt", 32 * BL[a], 32 * BL[b] + 32, 16))
     ts(col("ku", 2 * BL["pc"] + 1), pp("pc"), 16.0, A.add)
     cp(v("ku", 32, 36), v("blt", 0, 4))
     iota(v("c16"), [[16, 16]])
-    iota(v("iota"), [[1, 272]])
-    tr(v("blt", 32 * len(BLOCKS), 32 * len(BLOCKS) + 32), v("iota", 0, 32))
+    iota(v("iota"), [[1, 264]])
     ts(v("jl"), v("c16"), pp("i"), A.add)
     lin(v("dmp"), v("jl"), 1.0, float(DUMP))
     for b in range(4):
@@ -380,21 +377,17 @@ def rank_program(g, core, T, topo):
     iota(v("ki", 80, 96), [[1, 16]])
     cp(v("kb"), v("ki", 48, 96))
     iota(v("cn"), [[16, 4], [0, 8]])
-    lin(v("cn"), v("cn"), 1.0, c32)
+    lin(v("cn"), v("cn"), 1.0, pp("i"))
     fill(v("cd"), 0.0)
     lin(v("cd", 7, 32, 8), v("jl", 0, 4), -1.0, 0.0)
     iota(v("kc"), [[1, 4], [0, 4]])
     iota(v("c64"), [[64, 4], [0, 16]], 1024)
     iota(v("rs"), [[0, 16], [64, 16]])
     iota(v("wa", ZZ, ZZ + 256), [[0, 256]])
-    iota(v("dp", DX + 256, DX + 1088, 272), [[0, 4]])
-    fill(v("wa", VV - 16, VV), 0.0)
-    fill(v("wa", VV + 256, VV + 272), 0.0)
+    for b in range(4):
+        iota(v("dp", DX + 272 * b + 256, DX + 272 * b + 272), [[0, 16]])
     for name in ("en", "sg", "ds"):
         fill(v(name), 0.0)
-    lin(col("en", 3), pp("e16"), 1.0, 0.0)
-    lin(kf(CAP), pp("e16"), 1.0, 64.0)
-    lin(kf(C1), pp("e16"), 1.0, 1.0)
     iota(v("base"), [[0, 4], [128, 2]], 128)
     tt(v("base", 0, 6), v("blt", 32 * BL["la"], 32 * BL["lf"] + 32, 16), v("base", 0, 6), A.add)
     iota(v("kk"), [[256, 8]], 256 * 32768)
@@ -411,8 +404,7 @@ def rank_program(g, core, T, topo):
     act(v("cm1"), v("iota", 0, 128), F.Sign, bias=kf(DMB))
     lin(v("dm"), v("cm1"), 0.5, 0.5)
     ms(v("mx", 0, 272, 136), 0.0)
-    ms(v("ez", 0, 256), 0.0)
-    ms(v("ez", 256, 520), 0.0)
+    iota(v("ez"), [[0, 520]])
     iota(kf(P_), [[0, 1]], 0, 1, urge=5000.0)
     ts(v("ez", 3, 515, 4), v("iota", 0, 128), kf(P_), A.is_equal)
     for b in range(4):
@@ -426,40 +418,54 @@ def rank_program(g, core, T, topo):
                   [w, o], [out], 55.0 + GATHER * 64)
             act(v("ups", 16 * c, 16 * c + 64), ind(v("us"), o), F.Copy)
 
-    def two_turns(name, lo):
-        tr(v("tt", 0, 256), v(name, lo, lo + 256))
-        tr(v("tt", 256, 544), v(name, lo - 16, lo + 272))
+    ms(col("m32", 0), 0.0)
+    ts(v("m32", 1, 32), blk("i", 0, 31), pp("i"), A.is_equal, 511.0, A.mult)
+    ts(v("m32", 32, 64), blk("i"), pp("i"), A.not_equal)
+    tt(v("m32", 64, 96), v("m32", 0, 32), v("m32", 32, 64), A.add)
+    ts(kf(INV), pp("i"), 15.0, A.is_equal, 511.0 / 512, A.mult)
+    lin(kf(INV), kf(INV), 1.0, 1.0 / 512)
 
-    ms(v("vv", 256, 544, 272), 0.0)
-    ms(col("j1", J1 + SENT), float(SENT))
-    for lo in (0, 272, 544):
-        ms(v("jj", lo, lo + 16), float(SENT))
+    iota(v("m8", 0, 64), [[0, 8], [1, 8]])
+    fill(col("m8", 64), 0.0)
+    ts(v("m8", 65, 128), v("m8", 0, 63), pp("q2"), A.is_equal, 511.0, A.mult)
+    ts(v("m8", 128, 192), v("m8", 0, 64), pp("q2"), A.not_equal)
+    tt(v("m8", 192, 256), v("m8", 64, 128), v("m8", 128, 192), A.add)
+    ts(kf(IN8), pp("q2"), 7.0, A.is_equal, 511.0 / 512, A.mult)
+    lin(kf(IN8), kf(IN8), 1.0, 1.0 / 512)
+    lin(kf(ODD), pp("odd"), 1.0, -1.0)
+
+    def as_list(out, name, lo, less):
+        n = 16 * out[2]
+        scan(v("dgo", 0, n), v("dg", 0, n), v(name, lo, lo + n), 0.0, A.mult, A.max)
+        ts(out, v("dgo", 15, n, 16), kf(INV), A.mult, less, A.subtract)
+
+    ms(v("j1", J1 + 256, J1 + 258), float(SENT))
+    for lo in (256, 528):
+        ms(v("vv", lo, lo + 2), 0.0)
+        ms(v("jj", lo, lo + 2), SENT + 1.0)
     ts(v("v32", 0, 16), v("blk", 0, 16), pp("i"), A.is_equal, 64.0, A.mult)
     ts(v("v32", 16, 32), v("blk", 0, 16), pp("i"), A.is_equal, 128.0, A.mult)
     lin(v("vv", 0, 256), ind(v("v32"), v("vo")), 1.0, 1.0)
+    act(v("dg"), ind(v("m32", 64, 96), v("vo")), F.Copy)
     cp(v("vc", 0, 256), v("vv", 0, 256))
     tt(s(NR), v("pari"), v("jl"), A.not_equal)
     ts(s(W), v("pari"), -1.0, A.mult, float(SENT), A.add)
     tt(s(W + 1), s(NR), s(W), A.mult)
     ts(jo(0), s(W + 1), -1.0, A.mult, float(SENT), A.add)
-    act(v("j1", J1, J1 + 128), ind(v("iota", 0, 257), v("jo", 0, 8)), F.Copy)
-    cp(v("j1", J1 + 128, J1 + 256), ind(v("iota", 0, 257), v("jo", 8, 16)))
-    jw, ja, va = v("j1", J1, J1 + 257), JA, 0
+    act(v("j1", J1, J1 + 128), ind(v("iota", 0, 258), v("jo", 0, 8)), F.Copy)
+    cp(v("j1", J1 + 128, J1 + 256), ind(v("iota", 0, 258), v("jo", 8, 16)))
+    jw, ja, va = v("j1", J1, J1 + 258), JA, 0
     for m, radix in enumerate(RADIX):
-        last = m == len(RADIX) - 1
+        last, own = m == len(RADIX) - 1, v("vc", 256 * m, 256 * m + 256)
         if m:
-            two_turns("jj", JA + JB - ja)
-            cp(jo(m), ind(v("tt"), ku("jo")))
-            lin(v("vc", 256 * m, 256 * m + 256), v("vv", va, va + 256), 1.0, 0.0)
-        if last:
-            lin(v("vc", 768, 1024), v("vv", va, va + 256), 1.0, -96.5)
+            as_list(jo(m), "jj", JA + JB - ja, 1.0)
+            act(own, v("vv", va, va + 256), F.Copy)
         for k in range(1, radix):
             if not last:
-                act(v("jj", ja, ja + 256), ind(jw, jo(m)), F.Copy)
-                jw, ja = v("jj", ja, ja + 257), JA + JB - ja
-            end = last and k == radix - 1
-            c = 768 if end else 256 * m
-            tt(v("wa", VV, VV + 256) if end else v("vv", 272 - va, 528 - va), ind(v("vv", va, va + 257), jo(m)), v("vc", c, c + 256), A.add)
+                lin(v("jj", ja, ja + 256), ind(jw, jo(m)), 1.0, 0.0 if m + k > 1 else 1.0)
+                jw, ja = v("jj", ja, ja + 258), JA + JB - ja
+            out = v("wa", VV, VV + 256) if last and k == radix - 1 else v("vv", 272 - va, 528 - va)
+            tt(out, ind(v("vv", va, va + 258), jo(m)), own, A.add)
             va = 272 - va
 
     def quant_x(t, h):
@@ -485,13 +491,12 @@ def rank_program(g, core, T, topo):
 
     def places_first():
         vw = v("wa", VV, VV + 256)
-        two_turns("wa", VV)
-        ts(v("gi", 32, 48), ind(v("tt"), ku("jo")), 96.5, A.add)
+        as_list(v("gi", 32, 48), "wa", VV, 0.0)
         ts(v("mi", 16, 32), v("gi", 32, 48), 63, A.bitwise_and)
-        ts(w32(GA), ind(vw, LB), 32.5, A.add)
-        ts(w32(GC), ind(vw, LB), M64, A.add, M64, A.subtract)
-        scan(ends, w32(GA, 0, 32, 4), w32(GC, 0, 32, 4), pp("e16"), A.add, A.subtract)
-        ts(v("gi", 0, 32), ind(vw, LB), 96.5, A.add, 16.0, A.mult)
+        ts(w32(GA), ind(vw, LB), M64, A.add)
+        ts(v("gq"), ind(vw, LB), M64 - 32.5, A.add)
+        scan(ends, w32(GA, 0, 32, 4), v("gq", 0, 32, 4), 0.0, A.add, A.subtract)
+        ts(v("gi", 0, 32), ind(vw, LB), 16.0, A.mult)
         for h in range(2):
             ts(v("mi", h, 16, 2), v("gi", h, 32, 4), 1024 << h, A.bitwise_and)
         tt(s(S2), ind(v("en"), ku("r16")), v("mi", 16, 32), A.subtract)
@@ -505,45 +510,44 @@ def rank_program(g, core, T, topo):
             lin(w8, sh(DJ, h), -512.0 * 256, 0.0)
             tt(w32(S1, 2 + h, 32, 4), w8, v("kk"), A.add)
         lin(w32(D5), w32(D1), 512.0, 0.0)
-        act(v("ub", 0, 256), vw, F.Abs, bias=-32.0)
+        act(v("ub", 0, 256), vw, F.Abs, bias=-128.5)
         act(v("ub", 256, 512), v("ub", 0, 256), F.Abs, bias=-64.0)
         act(v("wa", DP, DP + 256), v("ub", 256, 512), F.Abs, bias=-32.0)
         ts(v("wa", T0, T0 + 256), v("ub", 256, 512), 32.0, A.is_gt, 2048.0, A.mult)
-        ts(v("wa", T1, T1 + 256), vw, 0.0, A.is_lt, 2048.0, A.mult)
+        ts(v("wa", T1, T1 + 256), vw, 128.0, A.is_lt, 2048.0, A.mult)
 
     def places_later():
         tt(w32(GA), ind(v("wa", 0, LS + 256), LA), w32(CA), A.mult)
         tt(w32(GC), ind(v("wa", 0, LS + 256), LC), w32(CC), A.add)
-        scan(v("en", 4, 36), w32(GA), w32(CD), pp("e16"), A.add, A.add)
+        scan(v("en", 4, 36), w32(GA), w32(CD), 0.0, A.add, A.add)
         tt(w32(BB, 0, 30), w32(GC, 0, 30), w32(GC, 2, 32), A.max)
         tt(w32(YY, 0, 30), v("en", 5, 35), w32(BB, 0, 30), A.max)
         cp(v("so"), ind(w32(YY, 0, 30), ku("y16")))
         cp(s(Y), ind(w32(YY, 0, 30), ku("y16")))
 
     def slots(t):
-        iota(v("win", 0, 96), [[0, 96]], SENT)
-        scat(v("win"), v("so"), v("iota", 0, 256))
-        tr(v("ts", 0, 64), v("win", 0, 64))
-        tr(v("ts", 64, 128), v("win", 16, 80))
-        cp(v("sl%d" % t), ind(v("ts"), ku("sl")))
-        return send(partner[t], v("ll%d" % t), v("sl%d" % t, 0, 4), False, "li%d" % t, 0.0)
+        iota(v("win", 0, 64), [[0, 64]], SENT + 1)
+        scat(v("win"), v("so"), v("iota", 1, 257))
+        scan(v("dgo", 0, 64), v("m8", 192, 256), v("win", 0, 64), 0.0, A.mult, A.max)
+        ts(v("sl%d" % t), v("dgo", 7, 64, 8), kf(IN8), A.mult, kf(ODD), A.add)
+        return send(partner[t], v("ll%d" % t), v("sl%d" % t), False, "li%d" % t, 0.0)
 
     def homes(t):
         w8 = v("s", 16 * (W + 2), 16 * (W + 2) + 8)
-        ts(w8, ends, kf(CAP), A.min, kf(C1), A.subtract)
+        ts(w8, ends, 64.0, A.min, 1.0, A.subtract)
         tt(v("sg", 7, 39, 4), starts, w8, A.add)
         tt(v("ds", 3, 35, 4), v("sg", 7, 39, 4), v("sg", 11, 40, 4), A.subtract)
         tt(s(EM, 2), ind(v("en"), ku("r32", 2)), v("cn"), A.is_gt)
         tt(s(DD, 2), ind(v("ds"), ku("r32", 2)), v("cd"), A.add)
         scan(s(SC, 2), s(EM, 2), s(DD, 2), 0.0, A.mult, A.add)
-        ts(v("mo"), ind(s(SC, 2), ku("mo")), pp("e16"), A.max)
-        act(v("wm"), ind(v("win", 0, 96), v("mo", 0, 8)), F.Identity, scale=4.0)
+        ts(v("mo"), ind(s(SC, 2), ku("mo")), 0.0, A.max)
+        lin(v("wm"), ind(v("win", 0, 64), v("mo", 0, 8)), 4.0, -4.0)
         tr(v("tm"), v("wm"))
         tt(s(W + 3), ind(v("tm"), ku("xm")), v("kc"), A.add)
         cp(v("xo"), s(W + 3))
         for b in range(4):
             act(v("xg", 64 * b, 64 * b + 64), ind(v("xb%d" % t, 0, 1024), v("xo", 4 * b, 4 * b + 4)), F.Copy)
-        ts(s(W + 4), s(Y), kf(CAP), A.is_ge, -4096.0, A.mult)
+        ts(s(W + 4), s(Y), 64.0, A.is_ge, -4096.0, A.mult)
         tt(s(S3), ind(v("sg"), ku("r16")), s(Y), A.subtract)
         tt(s(S26), s(S3), s(W + 4), A.add)
         tt(s(HA, 4), ind(s(S26), v("ku", 32, 36)), v("c64"), A.add)
@@ -587,12 +591,8 @@ def rank_program(g, core, T, topo):
 
     def layer(t, sent):
         arrived("li%d" % t, ne[t], [sent], v("ll%d" % t))
-        for b in range(4):
-            w = ind(v("dp", DX + 272 * b, DX + 272 * b + 257), v("ll%d" % t))
-            if b % 2:
-                act(v("dp", PT + b, PT + 256, 4), w, F.Copy)
-            else:
-                cp(v("dp", PT + b, PT + 256, 4), w)
+        cp(v("dp", PT, PT + 256, 2), ind(v("dp", DX, DX + 802), v("ll%d" % t)))
+        act(v("dp", PT + 1, PT + 256, 2), ind(v("dp", DX + 272, DX + 1074), v("ll%d" % t)), F.Copy)
         pq, ps = v("hq%d" % t, 128, 256), v("hs%d" % t, 128, 256)
         qz(pq, ps, v("dp", PT, PT + 512))
         for b in range(4):
@@ -602,16 +602,17 @@ def rank_program(g, core, T, topo):
             else:
                 act(v("dp", HT + b, HT + 256, 4), v("pc", 512 * b, 512 * b + 64), F.Relu, scale=0.03125)
         qz(v("hq%d" % t, 0, 128), v("hs%d" % t, 0, 128), v("dp", HT, HT + 512))
-        return send2(partner[t], v("lq%d" % t, 256, 320), v("hq%d" % t, 0, 64), v("ls%d" % t, 256, 512), v("hs%d" % t), "hh%d" % t)
+        return [send(partner[t], v("lq%d" % t, 256, 320), v("hq%d" % t, 0, 64), True, "hh%d" % t, 300.0),
+                send(partner[t], v("ls%d" % t, 256, 320), v("hs%d" % t, 0, 64), False, "hh%d" % t, 100.0)]
 
     def update(t, sent):
-        arrived("hh%d" % t, ne[t], [sent], v("lq%d" % t, 256, 320), v("ls%d" % t, 256, 512))
+        arrived("hh%d" % t, 2 * ne[t], sent, v("lq%d" % t, 256, 320), v("ls%d" % t, 256, 320))
         xb, xn = "xb%d" % t, "xb%d" % (t + 1)
         for b in range(4):
             mm(v("pa", 512 * b, 512 * b + 128), v("eq", 128 * b, 128 * b + 128), v("es", 128 * b, 128 * b + 128),
                v("lq%d" % t, 192, 320), v("ls%d" % t, 192, 320))
             tt(v(xb, 1024 + 64 * b, 1088 + 64 * b), v("pa", 512 * b + 64, 512 * b + 128), v("xg", 64 * b, 64 * b + 64), A.add)
-        for e, b, lo, hi in PARTS:
+        for e, b, lo, hi in (PARTS if t < R - 1 else LAST):
             w = ind(v(xb, 0, 1088 + 64 * b), v("ho", 16 * b + lo, 16 * b + hi))
             out = v(xn, 64 * lo + b, 64 * hi, 4)
             if e == "A":

from concourse.bass import DstId, RemoteDMATransfer
from concourse.mybir import dt, AluOpType, ActivationFunctionType

A = AluOpType
F = ActivationFunctionType
R = 3
STEP = [1, 2, 3]
BF, F32, I32, U16, U8, X4 = "bfloat16", "float32", "int32", "uint16", "uint8", "float8_e4m3fn_x4"
SENT = 257
DUMP = 544
BIG = 2.0 ** 90
M64 = 12288.0
DP, T0, T1, ZZ, LS, VV = 0, 256, 512, 768, 1024, 1280
HT, PT, DX = 0, 256, 512
JA, JB, J1 = 0, 272, 256
BLOCKS = [("i", 0, [[0, 2], [1, 16]]), ("k32", 0, [[0, 2], [32, 4], [0, 4]]),
          ("la", None, None), ("lc", None, None), ("lf", 0, [[0, 8], [256, 4]]), ("r16", 7, [[0, 2], [4, 8], [0, 2]]),
          ("q2", 0, [[0, 2], [1, 8], [0, 2]]), ("odd", 0, [[0, 16], [544, 2]]),
          ("xm", 0, [[4, 8], [32, 4]]), ("r32", 3, [[0, 4], [4, 8]]), ("mo", 7, [[0, 4], [8, 4], [0, 2]]),
          ("y16", 0, [[0, 2], [4, 8], [1, 2]]), ("pc", None, None)]
BL = {_b[0]: _k for _k, _b in enumerate(BLOCKS)}

SCRATCH = {}


def _sb(name, cols, dtype):
    SCRATCH[name] = ("sbuf", [128, cols], dtype)


for _t in range(R + 1):
    _sb("xb%d" % _t, 1280, BF)
    _sb("xq%d" % _t, 256, X4)
    _sb("xs%d" % _t, 256, U8)
for _t in range(R):
    _sb("lq%d" % _t, 320, X4)
    _sb("ls%d" % _t, 512, U8)
    _sb("ll%d" % _t, 8, U16)
    _sb("sl%d" % _t, 8, U16)
    _sb("hq%d" % _t, 256, X4)
    _sb("hs%d" % _t, 256, U8)
for _n, _c, _d in [
    ("ut", 512, BF), ("vt", 512, BF), ("uq", 128, X4), ("us", 128, U8), ("vq", 128, X4), ("vs", 128, U8),
    ("up", 384, X4), ("ups", 384, U8), ("wq", 512, X4), ("wss", 512, U8), ("eq", 512, X4), ("es", 512, U8),
    ("ez", 520, BF), ("pari", 16, I32), ("iota", 264, F32), ("ki", 96, I32), ("kf", 8, F32), ("c16", 16, F32),
    ("blk", 32 * len(BLOCKS), BF), ("blt", 32 * len(BLOCKS), BF), ("ku", 40, U16), ("pk", 24, U16), ("kb", 48, U16),
    ("jl", 16, F32), ("dmp", 16, F32), ("j4", 64, F32), ("c64", 64, F32), ("base", 8, F32), ("kc", 16, F32), ("kk", 8, F32),
    ("cn", 32, F32), ("cd", 32, F32), ("cm", 128, BF), ("cm1", 128, BF), ("dm", 128, BF),
    ("mx", 272, F32), ("em", 256, BF), ("ct", 256, BF),
    ("jj", 544, BF), ("j1", 1056, F32), ("jo", 48, U16), ("m32", 96, BF), ("dg", 256, BF), ("dgo", 256, BF), ("gq", 32, BF), ("m8", 256, BF),
    ("vv", 544, BF), ("vc", 768, BF), ("v32", 32, BF), ("vo", 16, U16), ("wa", VV + 256, BF),
    ("un", 512, BF), ("rs", 256, BF), ("tu", 512, BF), ("ub", 512, BF), ("lw", 256, BF),
    ("offs", 8, U16), ("gi", 48, I32), ("mi", 32, I32), ("s", 1088, F32), ("en", 40, F32), ("sg", 40, F32), ("ds", 40, F32),
    ("so", 16, U16), ("win", 512 * 31 + 16, BF), ("wm", 128, BF), ("tm", 128, BF), ("mo", 16, U16), ("xo", 16, U16),
    ("ho", 64, U16), ("po", 16, U16),
    ("dp", DX + 1088, BF), ("xg", 256, BF), ("yf", 256, F32),
]:
    _sb(_n, _c, _d)
SCRATCH["pa"] = ("psum", [128, 2048], F32)
SCRATCH["pc"] = ("psum", [128, 2048], F32)

SEMAPHORES = ["sV", "sA", "sP", "sG", "dpar", "dx", "du", "dv", "dw", "dws", "dout", "loc"] + \
             ["%s%d" % (_k, _t) for _k in ("qx", "li", "hh") for _t in range(R)]

CYC, WAKE, HOP, LOAD = 1.0, 150.0, 500.0, 900.0
GATHER, SCATTER, PE = 1.3, 3.2, 0.8
SLACK = 150.0
RADIX = (3, 3, 4)
FIRST = [
    "pari:0 ut:0 xb0:0",
    "blk:i c16:0 ki:0 iota:0 blk:k32 ki:16 blk:lf blk:r16 kf:0 ez:0 blk:q2 blk:odd base:0 m8:0 win:0",
    "blt:i v32:0 v32:16 vo:0 m32:1 m32:32 jl:0 kf:2 m32:64 s:0 s:256 ku:32 s:272 blt:k32 jo:0 vc:0 j1:384 vv:272 pk:0 uq:0 vv:0' "
    "up:0 up:64 dgo:0 xq0:0 jo:16 xq0:128 vv:272' ez:3 vv:0'' mx:1 blt:la dgo:0' mx:137 m8:65 jo:32 em:0 m8:128 "
    "vv:272'' em:128 base:0' vv:0''' ct:0 ct:128 kf:4 wa:1280 offs:0 offs:1 dgo:0'' gi:0 s:544 gq:0 gi:32",
    "vv:0 dg:0 j1:256 jj:0 kf:1 blk:lc jj:272 vc:256 blk:98 cm1:0 ups:0 ups:64 jj:0' cm:0 jj:272' vc:512 kf:3 cm1:0' dm:0 "
    "m8:64 en:0 dmp:0 sg:0 ds:0 cd:0 cn:0' s:864 s:960 s:1022 j4:0 j4:16 j4:32 j4:48 ups:128 ups:192 ub:0 ups:256 ups:320",
    "wa:1280 m8:192 eq:0 eq:128 eq:256 eq:384", "wa:1280 blt:xm", "so:0 s:368", "so:0 up:128", "so:0 up:192", "so:0 up:256", "so:0 up:320", "so:0 vq:0",
]
PARTS = [("A", 0, 0, 16), ("A", 2, 0, 16), ("A", 3, 12, 16), ("V", 1, 0, 16), ("V", 3, 0, 8), ("V", 3, 8, 12)]
LAST = [("A", 0, 0, 8), ("A", 2, 0, 8), ("A", 0, 8, 16), ("A", 2, 8, 16), ("A", 3, 8, 16), ("V", 1, 0, 8), ("V", 3, 0, 8), ("V", 1, 8, 16)]
_ORDER = []


def _overlap(a, b):
    if a[0] != b[0] or a[2] <= b[1] or b[2] <= a[1]:
        return False
    if a[3] == b[3] and a[3] > 1:
        return (a[1] - b[1]) % a[3] == 0
    return True


def _order(ops):
    if _ORDER:
        return _ORDER
    n = len(ops)
    wake = [0.0 if o["e"] == "R" else WAKE for o in ops]
    full = [o["len"] + o["lat"] for o in ops]
    tail, urge = [0.0] * n, [0.0] * n
    left, seen = [], set()

    def visit(i):
        if i not in seen:
            seen.add(i)
            for p in ops[i]["deps"] + ops[i]["behind"]:
                visit(p)
            left.append(i)
    for i in range(n):
        visit(i)
    for i in reversed(left):
        tail[i] += full[i]
        urge[i] += full[i] + ops[i]["urge"]
        for p in ops[i]["deps"]:
            tail[p] = max(tail[p], tail[i] + wake[i])
            urge[p] = max(urge[p], urge[i] + wake[i])
        for p in ops[i]["behind"]:
            tail[p] = max(tail[p], tail[i] - ops[p]["lat"])
            urge[p] = max(urge[p], urge[i] - ops[p]["lat"])
    done, free = {}, {}
    while left:
        est, near, best = {}, {}, None
        for i in left:
            est[i] = max([free.get(ops[i]["e"], 0.0)] + [(done[p] if p in done else est[p] + full[p]) + wake[i] for p in ops[i]["deps"]] +
                         [est[p] + ops[p]["len"] for p in ops[i]["behind"] if p not in done])
        bound = max(est[i] + tail[i] for i in left)
        soon = min(est.values()) + 3000.0
        for i in left:
            if est[i] < soon:
                near.setdefault(ops[i]["e"], []).append(i)
        for i in left:
            if est[i] < soon and all(p in done for p in ops[i]["deps"] + ops[i]["behind"]):
                end = est[i] + ops[i]["len"]
                hurt = any(est[j] < end and tail[j] > tail[i] and end + tail[j] > max(bound - SLACK, est[j] + ops[j]["len"] + tail[i])
                           for j in near[ops[i]["e"]])
                key = (hurt, est[i], -urge[i])
                if best is None or key < best[0]:
                    best = (key, i)
        i = best[1]
        done[i] = est[i] + full[i]
        if ops[i]["e"] != "R":
            free[ops[i]["e"]] = est[i] + ops[i]["len"]
        left.remove(i)
        _ORDER.append(i)
    return _ORDER


def rank_program(g, core, T, topo):
    rank = T.rank_of(core)
    if rank is None:
        return
    eng = {"V": g.vector, "A": g.scalar, "P": g.tensor, "G": g, "S": g.sync}
    ops = []
    hist = []

    def v(name, lo=0, hi=None, step=1):
        if hi is None:
            hi = SCRATCH[name][1][1]
        ap = T[name][:, lo:hi] if step == 1 else T[name][:, lo:hi:step]
        n, wide = (hi - lo + step - 1) // step, SCRATCH[name][2] not in (BF, U16)
        if SCRATCH[name][0] == "psum":
            return (ap, [(name, lo // 512 * 512, (hi + 511) // 512 * 512, 1)], n, wide, False)
        return (ap, [(name, lo, hi, step)], n, wide, False)

    def col(name, c):
        return v(name, c, c + 1)

    def ind(w, o):
        return (w[0].indirect(o[0]), w[1] + o[1], 16 * o[2], w[3], True)

    def issue(e, fn, reads, writes, length, lat=0.0, after=(), sem=None, inc=1, urge=0.0):
        rr = [r for x in reads for r in x[1]]
        ww = [r for x in writes for r in x[1]]
        deps = set(after)
        for reg, isw, k in hist:
            ps = SCRATCH[reg[0]][0] == "psum" and ops[k]["e"] != e
            if any(_overlap(reg, r) for r in ww) or ((isw or ps) and any(_overlap(reg, r) for r in rr)):
                deps.add(k)
        me = len(ops)
        ops.append({"e": e, "fn": fn, "deps": sorted(deps), "len": length, "lat": lat, "sem": sem or "s" + e, "inc": inc, "urge": urge,
                    "behind": [], "name": "%s:%d" % ww[0][:2] if ww else ""})
        keep = [h for h in hist if not any(h[0][0] == w[0] and w[3] == 1 and w[1] <= h[0][1] and h[0][2] <= w[2] for w in ww)]
        hist[:] = keep + [(r, False, me) for r in rr] + [(r, True, me) for r in ww]
        return me

    def arrived(sem, val, sent, *views):
        return issue("R", None, [], views, 0.0, 0.0, sent, sem, val)

    def emit():
        known = {e: {} for e in eng}
        total, tok = {}, {}

        def wait(e, t):
            sem, val, clock = t
            if known[e].get(sem, 0) >= val:
                return
            eng[e].wait_ge(T.sem[sem], val)
            for k, x in list(clock.items()) + [(sem, val)]:
                if known[e].get(k, 0) < x:
                    known[e][k] = x
        named = {}
        for i, o in enumerate(ops):
            name = o["name"]
            while name in named:
                name += "'"
            named[name] = i
        for k in BL:
            for b in ("blk", "blt"):
                named["%s:%s" % (b, k)] = named.get("%s:%d" % (b, 32 * BL[k]))
        for line in FIRST:
            calls = [named[x] for x in line.split()]
            for a, b in zip(calls, calls[1:]):
                ops[b]["behind"].append(a)
        for i in _order(ops):
            o = ops[i]
            e, sem = o["e"], o["sem"]
            total[sem] = total.get(sem, 0) + o["inc"]
            if e == "R":
                tok[i] = (sem, total[sem], {})
                continue
            need = {}
            for p in o["deps"]:
                if tok[p][0] not in need or need[tok[p][0]][1] < tok[p][1]:
                    need[tok[p][0]] = tok[p]
            for t in sorted(need.values(), key=lambda x: -len(x[2])):
                wait(e, t)
            tok[i] = (sem, total[sem], dict(known[e]))
            ins = o["fn"]()
            if ins is not None:
                ins.then_inc(T.sem[sem], o["inc"])
        for sem in sorted(total, key=lambda x: x == "dout"):
            wait("S", (sem, total[sem], {}))

    def span(out, *ins, twice=False):
        if any(x[4] for x in ins):
            return 55.0 + GATHER * out[2]
        wide = any(x[3] for x in (out,) + ins)
        return CYC * max(64.0, out[2] * (2.0 if twice else 1.0) * (1.0 if wide else 0.5))

    def sc(x):
        return x[0] if isinstance(x, tuple) else x

    def tup(*xs):
        return [x for x in xs if isinstance(x, tuple)]

    def ts(out, a, s1, op0, s2=None, op1=None):
        if op1 is None:
            return issue("V", lambda: g.vector.tensor_scalar(out[0], a[0], sc(s1), None, op0), tup(a, s1), [out], span(out, a))
        return issue("V", lambda: g.vector.tensor_scalar(out[0], a[0], sc(s1), sc(s2), op0, op1), tup(a, s1, s2), [out], span(out, a))

    def tt(out, a, b, op):
        return issue("V", lambda: g.vector.tensor_tensor(out[0], a[0], b[0], op), [a, b], [out],
                     span(out, a, b, twice=SCRATCH[a[1][0][0]][0] == "sbuf"))

    def cp(out, a):
        return issue("V", lambda: g.vector.tensor_copy(out[0], a[0]), [a], [out], span(out, a))

    def scat(w, o, a):
        return issue("V", lambda: g.vector.tensor_copy(w[0].indirect(o[0]), a[0]), [a, o], [w], 50.0 + SCATTER * a[2])

    def ms(out, c):
        return issue("V", lambda: g.vector.memset(out[0], c), [], [out], span(out))

    def scan(out, a, b, init, op0, op1):
        return issue("V", lambda: g.vector.tensor_tensor_scan(out[0], a[0], b[0], sc(init), op0, op1), tup(a, b, init), [out], span(out, a, b))

    def tr(out, a):
        return issue("V", lambda: g.vector.transpose(out[0], a[0]), [a], [out], span(out, a))

    def qz(q, s, a, urge=0.0):
        return issue("V", lambda: g.vector.quantize_mx(q[0], s[0], a[0]), [a], [q, s], 12.0 + 0.22 * a[2], urge=urge)

    def act(out, a, f, bias=None, scale=None):
        kw = {}
        if bias is not None:
            kw["bias"] = sc(bias)
        if scale is not None:
            kw["scale"] = sc(scale)
        return issue("A", lambda: g.scalar.activation(out[0], a[0], f, **kw), tup(a, bias, scale), [out],
                     65.0 + GATHER * out[2] if a[4] else CYC * max(64.0, out[2]))

    def lin(out, a, scale, bias):
        return act(out, a, F.Identity, bias, scale)

    def fill(out, c):
        return lin(out, v("iota", 0, out[2]), 0.0, c)

    def mm(out, lq, ls, rq, rs):
        return issue("P", lambda: g.tensor.matmul_mx(out[0], lq[0], ls[0], rq[0], rs[0], True, True), [lq, ls, rq, rs], [out],
                     PE * (out[2] + 16), 50.0)

    def iota(out, pat, base=0, cm=0, urge=0.0):
        kw = {} if SCRATCH[out[1][0][0]][2] == I32 else {"allow_small_or_imprecise_dtypes": True}
        return issue("G", lambda: g.iota(out[0], pat, base, cm, **kw), [], [out], CYC * (160.0 + 2 * out[2]), urge=urge)

    def dma(e, out, in_, sem, lat, reads=(), writes=(), after=(), urge=0.0):
        return issue(e, lambda: eng[e].dma_start(out, in_), list(reads), list(writes), 50.0, LOAD + lat, after, sem, 16, urge)

    def u8(x):
        return x[0].bitcast(dt.uint8)

    def send(to, dst, src, raw, sem, lat, first=0.0):
        rid, pid = topo.addr(to)[:2]
        m = topo.mask(core, to)

        def fn():
            g.remote_dma(u8(dst) if raw else dst[0], u8(src) if raw else src[0], T.sem[sem], T.sem.loc, pid, rid, m)
        return issue("G", fn, [src], [], 200.0 + first, HOP + lat, (), "loc", len(topo.engines(core, to)))

    def send2(to, dq, sq, ds, ss, sem):
        rid, pid = topo.addr(to)[:2]
        en = topo.engines(core, to)
        h = len(en) // 2
        masks = [sum(1 << e for e in en[:h]), sum(1 << e for e in en[h:])]

        def fn():
            g.remote_dma_fused([
                RemoteDMATransfer(dst_ids=[DstId(rid=rid, pnc=pid)], dma_engine_mask=masks[0], remote_sem=T.sem[sem], src=u8(sq), dst=u8(dq)),
                RemoteDMATransfer(dst_ids=[DstId(rid=rid, pnc=pid)], dma_engine_mask=masks[1], remote_sem=T.sem[sem], src=ss[0], dst=ds[0]),
            ], local_sem=T.sem.loc)
        return issue("G", fn, [sq, ss], [], 200.0, HOP + 400.0, (), "loc", len(en))

    partner = [T.cores[rank ^ STEP[t]] for t in range(R)]
    ne = [len(topo.engines(partner[t], core)) for t in range(R)]

    def s(k, n=1):
        return v("s", 16 * k, 16 * (k + n))

    def sh(k, h):
        return v("s", 16 * k + h, 16 * k + 16, 2)

    kf = lambda c: col("kf", c)
    jo = lambda m: v("jo", 16 * m, 16 * m + 16)
    pp = lambda name: col("blt", 32 * BL[name])
    ku = lambda name, n=1: v("ku", 2 * BL[name], 2 * BL[name] + n)
    P_, CMB, INV, DMB, IN8, ODD = range(6)
    NR, DJ, Y, OFF, S2, S3, S26, LM, HA, HB, W = 0, 1, 2, 3, 4, 5, 6, 7, 8, 12, 16
    EM, DD, SC, GA, GC, GF, BB, YY, B2, KK, CA, CC, CD, D1, D5, S1, S0, _, PW = range(28, 66, 2)
    ends, starts = v("en", 7, 39, 4), v("en", 3, 35, 4)

    def w32(k, lo=0, hi=32, step=1):
        return v("s", 16 * k + lo, 16 * k + hi, step)
    anc = w32(PW, 0, 31)
    LA, LC, LF, LB = [v("offs", 2 * k, 2 * k + 2) for k in range(4)]

    dma("S", T.pari[:], T.par[:], "dpar", 300.0, writes=[v("pari")])
    dma("S", T.ut[:], T.u[:], "du", 1200.0, writes=[v("ut")])
    tx = dma("S", T.xb0[:, 0:1024], T.x[:], "dx", 2500.0, writes=[v("xb0", 0, 1024)])
    tw = dma("S", T.wq[:].bitcast(dt.uint8), T.wc[:], "dw", 2000.0, writes=[v("wq")], after=[tx])
    dma("S", T.wss[:], T.ws[:], "dws", 2000.0, writes=[v("wss")], after=[tx])
    dma("S", T.vt[:], T.v[:], "dv", 3000.0, writes=[v("vt")], after=[tw])

    for k, (name, base, pat) in enumerate(BLOCKS):
        if pat is not None:
            iota(v("blk", 32 * k, 32 * k + 32), pat, base)
    blk = lambda name, lo=0, hi=32, step=1: v("blk", 32 * BL[name] + lo, 32 * BL[name] + hi, step)
    for lo in (0, 16):
        iota(blk("pc", lo, lo + 16), [[4, 4], [0, 2], [1, 2]])
    lin(blk("la"), blk("i"), 0.0, float(LS))
    lin(blk("la", 0, 32, 4), blk("i", 0, 8), 0.0, float(DP))
    lin(blk("lc"), blk("lf"), 1.0, float(T0))
    lin(blk("lc", 2, 32, 4), blk("i", 0, 8), 0.0, float(LS))
    for a, b in (("i", "i"), ("k32", "k32"), ("la", "odd"), ("xm", "pc")):
        tr(v("blt", 32 * BL[a], 32 * BL[b] + 32), v("blk", 32 * BL[a], 32 * BL[b] + 32))
    for a, b in (("r16", "r16"), ("xm", "pc")):
        cp(v("ku", 2 * BL[a], 2 * BL[b] + 2), v("blt", 32 * BL[a], 32 * BL[b] + 32, 16))
    ts(col("ku", 2 * BL["pc"] + 1), pp("pc"), 16.0, A.add)
    cp(v("ku", 32, 36), v("blt", 0, 4))
    iota(v("c16"), [[16, 16]])
    iota(v("iota"), [[1, 264]])
    ts(v("jl"), v("c16"), pp("i"), A.add)
    lin(v("dmp"), v("jl"), 1.0, float(DUMP))
    for b in range(4):
        lin(v("j4", 16 * b, 16 * b + 16), v("jl"), 4.0, float(b))
    iota(v("ki", 0, 16), [[0, 8], [16, 2]], urge=1000.0)
    ts(v("vo"), v("ki", 0, 16), pp("i"), A.add)
    iota(v("ki", 16, 40), [[1, 3], [16, 8]])
    cp(v("pk"), v("ki", 16, 40))
    iota(v("ki", 48, 80), [[1, 2], [4, 8], [0, 2]], 1)
    iota(v("ki", 80, 96), [[1, 16]])
    cp(v("kb"), v("ki", 48, 96))
    iota(v("cn"), [[16, 4], [0, 8]])
    lin(v("cn"), v("cn"), 1.0, pp("i"))
    fill(v("cd"), 0.0)
    lin(v("cd", 7, 32, 8), v("jl", 0, 4), -1.0, 0.0)
    iota(v("kc"), [[1, 4], [0, 4]])
    iota(v("c64"), [[64, 4], [0, 16]], 1024)
    iota(v("rs"), [[0, 16], [64, 16]])
    iota(v("wa", ZZ, ZZ + 256), [[0, 256]])
    for b in range(4):
        iota(v("dp", DX + 272 * b + 256, DX + 272 * b + 272), [[0, 16]])
    for name in ("en", "sg", "ds"):
        fill(v(name), 0.0)
    iota(v("base"), [[0, 4], [128, 2]], 128)
    tt(v("base", 0, 6), v("blt", 32 * BL["la"], 32 * BL["lf"] + 32, 16), v("base", 0, 6), A.add)
    iota(v("kk"), [[256, 8]], 256 * 32768)
    fill(w32(PW, -2, -1), 0.0)
    fill(w32(D1), 0.0)
    fill(w32(S0), -32768.0)
    for h in range(2):
        lin(w32(S1, h, 32, 4), v("dmp", h, 16, 2), 256.0, -2048.0 * 256)
        lin(w32(S0, h, 32, 4), v("dmp", h, 16, 2), 1.0, -2048.0)
    lin(kf(CMB), pp("k32"), -1.0 / 30.5, 192.0 - 15.5 / 30.5)
    lin(v("cm1"), v("iota", 0, 128), 1.0 / 30.5, kf(CMB))
    lin(v("cm"), v("cm1"), BIG, -192.0 * BIG)
    lin(kf(DMB), pp("k32"), -1.0, 0.5)
    act(v("cm1"), v("iota", 0, 128), F.Sign, bias=kf(DMB))
    lin(v("dm"), v("cm1"), 0.5, 0.5)
    ms(v("mx", 0, 272, 136), 0.0)
    iota(v("ez"), [[0, 520]])
    iota(kf(P_), [[0, 1]], 0, 1, urge=5000.0)
    ts(v("ez", 3, 515, 4), v("iota", 0, 128), kf(P_), A.is_equal)
    for b in range(4):
        qz(v("eq", 128 * b, 128 * b + 128), v("es", 128 * b, 128 * b + 128), v("ez", 3 - b, 515 - b), 6000.0)
    qz(v("uq"), v("us"), v("ut"))
    qz(v("vq"), v("vs"), v("vt"))
    for t in range(R):
        for c in range(8 * t, 8 * t + 8, 4):
            o, out, w = v("pk", c, c + 4), v("up", 16 * c, 16 * c + 64), v("uq")
            issue("V", lambda o=o, out=out, w=w: g.vector.tensor_copy(out[0].bitcast(dt.uint32), w[0].bitcast(dt.uint32).indirect(o[0])),
                  [w, o], [out], 55.0 + GATHER * 64)
            act(v("ups", 16 * c, 16 * c + 64), ind(v("us"), o), F.Copy)

    ms(col("m32", 0), 0.0)
    ts(v("m32", 1, 32), blk("i", 0, 31), pp("i"), A.is_equal, 511.0, A.mult)
    ts(v("m32", 32, 64), blk("i"), pp("i"), A.not_equal)
    tt(v("m32", 64, 96), v("m32", 0, 32), v("m32", 32, 64), A.add)
    ts(kf(INV), pp("i"), 15.0, A.is_equal, 511.0 / 512, A.mult)
    lin(kf(INV), kf(INV), 1.0, 1.0 / 512)

    iota(v("m8", 0, 64), [[0, 8], [1, 8]])
    fill(col("m8", 64), 0.0)
    ts(v("m8", 65, 128), v("m8", 0, 63), pp("q2"), A.is_equal, 511.0, A.mult)
    ts(v("m8", 128, 192), v("m8", 0, 64), pp("q2"), A.not_equal)
    tt(v("m8", 192, 256), v("m8", 64, 128), v("m8", 128, 192), A.add)
    ts(kf(IN8), pp("q2"), 7.0, A.is_equal, 511.0 / 512, A.mult)
    lin(kf(IN8), kf(IN8), 1.0, 1.0 / 512)
    lin(kf(ODD), pp("odd"), 1.0, -1.0)

    def as_list(out, name, lo, less):
        n = 16 * out[2]
        scan(v("dgo", 0, n), v("dg", 0, n), v(name, lo, lo + n), 0.0, A.mult, A.max)
        ts(out, v("dgo", 15, n, 16), kf(INV), A.mult, less, A.subtract)

    ms(v("j1", J1 + 256, J1 + 258), float(SENT))
    for lo in (256, 528):
        ms(v("vv", lo, lo + 2), 0.0)
        ms(v("jj", lo, lo + 2), SENT + 1.0)
    ts(v("v32", 0, 16), v("blk", 0, 16), pp("i"), A.is_equal, 64.0, A.mult)
    ts(v("v32", 16, 32), v("blk", 0, 16), pp("i"), A.is_equal, 128.0, A.mult)
    lin(v("vv", 0, 256), ind(v("v32"), v("vo")), 1.0, 1.0)
    act(v("dg"), ind(v("m32", 64, 96), v("vo")), F.Copy)
    cp(v("vc", 0, 256), v("vv", 0, 256))
    tt(s(NR), v("pari"), v("jl"), A.not_equal)
    ts(s(W), v("pari"), -1.0, A.mult, float(SENT), A.add)
    tt(s(W + 1), s(NR), s(W), A.mult)
    ts(jo(0), s(W + 1), -1.0, A.mult, float(SENT), A.add)
    act(v("j1", J1, J1 + 128), ind(v("iota", 0, 258), v("jo", 0, 8)), F.Copy)
    cp(v("j1", J1 + 128, J1 + 256), ind(v("iota", 0, 258), v("jo", 8, 16)))
    jw, ja, va = v("j1", J1, J1 + 258), JA, 0
    for m, radix in enumerate(RADIX):
        last, own = m == len(RADIX) - 1, v("vc", 256 * m, 256 * m + 256)
        if m:
            as_list(jo(m), "jj", JA + JB - ja, 1.0)
            act(own, v("vv", va, va + 256), F.Copy)
        for k in range(1, radix):
            if not last:
                lin(v("jj", ja, ja + 256), ind(jw, jo(m)), 1.0, 0.0 if m + k > 1 else 1.0)
                jw, ja = v("jj", ja, ja + 258), JA + JB - ja
            out = v("wa", VV, VV + 256) if last and k == radix - 1 else v("vv", 272 - va, 528 - va)
            tt(out, ind(v("vv", va, va + 258), jo(m)), own, A.add)
            va = 272 - va

    def quant_x(t, h):
        qz(v("xq%d" % t, 128 * h, 128 * h + 128), v("xs%d" % t, 128 * h, 128 * h + 128), v("xb%d" % t, 512 * h, 512 * h + 512))

    def share_x(t):
        sent = [send(partner[t], v("ls%d" % t, 0, 256), v("xs%d" % t), False, "qx%d" % t, 300.0, 0.0 if t else 1500.0),
                send(partner[t], v("lq%d" % t, 0, 256), v("xq%d" % t), True, "qx%d" % t, 1800.0)]
        arrived("qx%d" % t, 2 * ne[t], sent, v("lq%d" % t, 0, 256), v("ls%d" % t, 0, 256))
        for b in range(4):
            mm(v("pa", 512 * b, 512 * b + 256), v("eq", 128 * b, 128 * b + 128), v("es", 128 * b, 128 * b + 128),
               v("lq%d" % t, 0, 256), v("ls%d" % t, 0, 256))
            act(v("dp", DX + 272 * b, DX + 272 * b + 256), v("pa", 512 * b, 512 * b + 256), F.Copy)

    def best(t):
        for h in range(2):
            a, b, ps = 128 * h, 128 * h + 128, v("pc", 512 * h, 512 * h + 128)
            mm(ps, v("up", 128 * t, 128 * t + 128), v("ups", 128 * t, 128 * t + 128), v("xq%d" % t, a, b), v("xs%d" % t, a, b))
            scan(v("mx", 136 * h + 1, 136 * h + 129), v("cm"), ps, 0.0, A.add, A.max)
            tt(v("em", a, b), ps, v("mx", 136 * h, 136 * h + 128), A.is_le)
            scan(v("ct", a, b), v("em", a, b), v("dm"), 0.0, A.mult, A.add)
            ts(v("offs", h, 8, 2), v("base", h, 8, 2), col("ct", b - 1), A.subtract)

    def places_first():
        vw = v("wa", VV, VV + 256)
        as_list(v("gi", 32, 48), "wa", VV, 0.0)
        ts(v("mi", 16, 32), v("gi", 32, 48), 63, A.bitwise_and)
        ts(w32(GA), ind(vw, LB), M64, A.add)
        ts(v("gq"), ind(vw, LB), M64 - 32.5, A.add)
        scan(ends, w32(GA, 0, 32, 4), v("gq", 0, 32, 4), 0.0, A.add, A.subtract)
        ts(v("gi", 0, 32), ind(vw, LB), 16.0, A.mult)
        for h in range(2):
            ts(v("mi", h, 16, 2), v("gi", h, 32, 4), 1024 << h, A.bitwise_and)
        tt(s(S2), ind(v("en"), ku("r16")), v("mi", 16, 32), A.subtract)
        tt(s(OFF), v("dmp"), v("mi", 0, 16), A.subtract)
        tt(s(Y), s(S2), s(OFF), A.max)
        cp(v("so"), s(Y))
        cp(s(DJ), v("mi", 16, 32))
        for h in range(2):
            w8 = v("s", 16 * (W + 11) + 8 * h, 16 * (W + 11) + 8 * h + 8)
            lin(w32(D1, 1 + h, 32, 4), sh(DJ, h), 1.0, 0.0)
            lin(w8, sh(DJ, h), -512.0 * 256, 0.0)
            tt(w32(S1, 2 + h, 32, 4), w8, v("kk"), A.add)
        lin(w32(D5), w32(D1), 512.0, 0.0)
        act(v("ub", 0, 256), vw, F.Abs, bias=-128.5)
        act(v("ub", 256, 512), v("ub", 0, 256), F.Abs, bias=-64.0)
        act(v("wa", DP, DP + 256), v("ub", 256, 512), F.Abs, bias=-32.0)
        ts(v("wa", T0, T0 + 256), v("ub", 256, 512), 32.0, A.is_gt, 2048.0, A.mult)
        ts(v("wa", T1, T1 + 256), vw, 128.0, A.is_lt, 2048.0, A.mult)

    def places_later():
        tt(w32(GA), ind(v("wa", 0, LS + 256), LA), w32(CA), A.mult)
        tt(w32(GC), ind(v("wa", 0, LS + 256), LC), w32(CC), A.add)
        scan(v("en", 4, 36), w32(GA), w32(CD), 0.0, A.add, A.add)
        tt(w32(BB, 0, 30), w32(GC, 0, 30), w32(GC, 2, 32), A.max)
        tt(w32(YY, 0, 30), v("en", 5, 35), w32(BB, 0, 30), A.max)
        cp(v("so"), ind(w32(YY, 0, 30), ku("y16")))
        cp(s(Y), ind(w32(YY, 0, 30), ku("y16")))

    def slots(t):
        iota(v("win", 0, 64), [[0, 64]], SENT + 1)
        scat(v("win"), v("so"), v("iota", 1, 257))
        scan(v("dgo", 0, 64), v("m8", 192, 256), v("win", 0, 64), 0.0, A.mult, A.max)
        ts(v("sl%d" % t), v("dgo", 7, 64, 8), kf(IN8), A.mult, kf(ODD), A.add)
        return send(partner[t], v("ll%d" % t), v("sl%d" % t), False, "li%d" % t, 0.0)

    def homes(t):
        w8 = v("s", 16 * (W + 2), 16 * (W + 2) + 8)
        ts(w8, ends, 64.0, A.min, 1.0, A.subtract)
        tt(v("sg", 7, 39, 4), starts, w8, A.add)
        tt(v("ds", 3, 35, 4), v("sg", 7, 39, 4), v("sg", 11, 40, 4), A.subtract)
        tt(s(EM, 2), ind(v("en"), ku("r32", 2)), v("cn"), A.is_gt)
        tt(s(DD, 2), ind(v("ds"), ku("r32", 2)), v("cd"), A.add)
        scan(s(SC, 2), s(EM, 2), s(DD, 2), 0.0, A.mult, A.add)
        ts(v("mo"), ind(s(SC, 2), ku("mo")), 0.0, A.max)
        lin(v("wm"), ind(v("win", 0, 64), v("mo", 0, 8)), 4.0, -4.0)
        tr(v("tm"), v("wm"))
        tt(s(W + 3), ind(v("tm"), ku("xm")), v("kc"), A.add)
        cp(v("xo"), s(W + 3))
        for b in range(4):
            act(v("xg", 64 * b, 64 * b + 64), ind(v("xb%d" % t, 0, 1024), v("xo", 4 * b, 4 * b + 4)), F.Copy)
        ts(s(W + 4), s(Y), 64.0, A.is_ge, -4096.0, A.mult)
        tt(s(S3), ind(v("sg"), ku("r16")), s(Y), A.subtract)
        tt(s(S26), s(S3), s(W + 4), A.add)
        tt(s(HA, 4), ind(s(S26), v("ku", 32, 36)), v("c64"), A.add)
        tt(s(HB, 4), s(HA, 4), v("j4"), A.max)
        cp(v("ho"), s(HB, 4))

    def flags(unit):
        cp(w32(GF), ind(v("wa", 0, LS), LF))
        ts(w32(PW, -1, 31), w32(GF), 0.0, A.is_equal, unit, A.mult)

    def far_end():
        flags(1.0 / 256)
        tt(w32(B2), w32(PW, -1, 31), w32(D5), A.mult)
        for k, lo in enumerate((T0, T1)):
            tt(v("un", 256 * k, 256 * k + 256), ind(w32(B2), v("kb", 16 * k, 16 * k + 16)), v("wa", lo, lo + 256), A.subtract)
            tr(v("tu", 256 * k, 256 * k + 256), v("un", 256 * k, 256 * k + 256))
            scan(v("un", 256 * k, 256 * k + 256), v("rs"), v("tu", 256 * k, 256 * k + 256), 0.0, A.min, A.max)
        tt(s(LM), v("un", 15, 256, 16), v("un", 271, 512, 16), A.max)
        act(v("lw"), ind(s(LM), v("kb", 32, 48)), F.Identity, scale=256.0)
        tr(v("wa", LS, LS + 256), v("lw"))
        tt(w32(CA), w32(PW, -2, 30), w32(PW, -1, 31), A.subtract)
        fill(w32(CA, 0, 32, 4), -1.0)
        tt(w32(KK), w32(B2), w32(D1), A.subtract)
        lin(w32(KK, 3, 32, 4), w32(GF, 0, 32, 4), -1.0, 33.5)
        tt(w32(CD), w32(KK), w32(KK, -1, 31), A.subtract)
        fill(w32(CD, 0, 32, 4), 32.5)
        tt(w32(BB), ind(anc, ku("pc", 2)), w32(S1), A.mult)
        tt(w32(CC), w32(BB), w32(S0), A.add)

    def parents():
        flags(1.0)
        tt(s(W + 6), ind(anc, ku("y16")), s(NR), A.mult)
        tt(s(W + 7), v("dmp"), v("pari"), A.subtract)
        tt(s(W + 8), s(W + 6), s(W + 7), A.mult)
        tt(s(W + 9), v("dmp"), s(W + 8), A.subtract)
        cp(v("po"), s(W + 9))
        scat(v("j1", J1, J1 + 800), v("po"), v("iota", 0, 256))
        cp(w32(KK), ind(v("iota", 0, 256), LB))
        scat(v("j1", 0, 1024), LF, w32(KK))
        dma("S", T.op[:], T.j1[0:128:16, J1:J1 + 256], "dout", 0.0, reads=[v("j1", J1, J1 + 256)])

    def layer(t, sent):
        arrived("li%d" % t, ne[t], [sent], v("ll%d" % t))
        cp(v("dp", PT, PT + 256, 2), ind(v("dp", DX, DX + 802), v("ll%d" % t)))
        act(v("dp", PT + 1, PT + 256, 2), ind(v("dp", DX + 272, DX + 1074), v("ll%d" % t)), F.Copy)
        pq, ps = v("hq%d" % t, 128, 256), v("hs%d" % t, 128, 256)
        qz(pq, ps, v("dp", PT, PT + 512))
        for b in range(4):
            mm(v("pc", 512 * b, 512 * b + 128), v("wq", 128 * b, 128 * b + 128), v("wss", 128 * b, 128 * b + 128), pq, ps)
            if b % 2:
                ts(v("dp", HT + b, HT + 256, 4), v("pc", 512 * b, 512 * b + 64), 0.0, A.max, 0.03125, A.mult)
            else:
                act(v("dp", HT + b, HT + 256, 4), v("pc", 512 * b, 512 * b + 64), F.Relu, scale=0.03125)
        qz(v("hq%d" % t, 0, 128), v("hs%d" % t, 0, 128), v("dp", HT, HT + 512))
        return [send(partner[t], v("lq%d" % t, 256, 320), v("hq%d" % t, 0, 64), True, "hh%d" % t, 300.0),
                send(partner[t], v("ls%d" % t, 256, 320), v("hs%d" % t, 0, 64), False, "hh%d" % t, 100.0)]

    def update(t, sent):
        arrived("hh%d" % t, 2 * ne[t], sent, v("lq%d" % t, 256, 320), v("ls%d" % t, 256, 320))
        xb, xn = "xb%d" % t, "xb%d" % (t + 1)
        for b in range(4):
            mm(v("pa", 512 * b, 512 * b + 128), v("eq", 128 * b, 128 * b + 128), v("es", 128 * b, 128 * b + 128),
               v("lq%d" % t, 192, 320), v("ls%d" % t, 192, 320))
            tt(v(xb, 1024 + 64 * b, 1088 + 64 * b), v("pa", 512 * b + 64, 512 * b + 128), v("xg", 64 * b, 64 * b + 64), A.add)
        for e, b, lo, hi in (PARTS if t < R - 1 else LAST):
            w = ind(v(xb, 0, 1088 + 64 * b), v("ho", 16 * b + lo, 16 * b + hi))
            out = v(xn, 64 * lo + b, 64 * hi, 4)
            if e == "A":
                act(out, w, F.Copy)
            else:
                cp(out, w)
        for h in range(2):
            quant_x(t + 1, h)

    quant_x(0, 0)
    quant_x(0, 1)
    for t in range(R):
        share_x(t)
        best(t)
        if t == 0:
            places_first()
        else:
            places_later()
        sent = slots(t)
        homes(t)
        if t < R - 1:
            far_end()
        else:
            parents()
        update(t, layer(t, sent))

    for h in range(2):
        a, b = 128 * h, 128 * h + 128
        mm(v("pc", 512 * h, 512 * h + 128), v("vq"), v("vs"), v("xq3", a, b), v("xs3", a, b))
        dma("S", T.oc[:, 4 * a:4 * b], T.xq3[:, a:b].bitcast(dt.uint8), "dout", 300.0, reads=[v("xq3", a, b)])
        cp(v("yf", a, b), v("pc", 512 * h, 512 * h + 128))
    dma("S", T.y[:], T.yf[:], "dout", 500.0, reads=[v("yf")])
    for k in range(4):
        dma("A", T.osc[4 * k:4 * k + 4, :], T.xs3[32 * k:32 * k + 4, :], "dout", 0.0, reads=[v("xs3")])
    emit()
